import numpy as np, ml_dtypes
CORES = [16,18,20,22]
N = 4
BF = ml_dtypes.bfloat16
S, M = 4096, 256
def pack(x, slot, w):
    return {"x": np.clip(np.rint(x), -255, 255).astype(np.int32).astype(np.float32).astype(BF), "slot": slot.astype(np.int32), "w": np.rint(w).astype(np.int32).astype(np.float32)}
def setup_inputs(rng):
    x = rng.standard_normal((N, 128, S), dtype=np.float32) * rng.integers(20, 61, (1, 128, 1)) + rng.integers(-80, 81, (1, 128, 1)) + rng.integers(-15, 16, (N, 128, 1))
    slot = np.floor(M * rng.random((N, 8, S)) ** rng.integers(1, 4, (1, 8, 1))).astype(np.int64) ^ rng.integers(0, M, (1, 8, 1))
    return pack(x, slot, rng.integers(-255, 256, (N, 128, 1)))
def setup_inputs_one(rng):
    d = setup_inputs(rng); e = rng.integers(0, M, (1, 8, 1)); e[0, 0] = 0; e[0, 7] = M - 1
    d["slot"][:] = e; d["w"].reshape(N, 8, 16)[:, ::2] = 0; return d
def setup_inputs_gaps(rng):
    x = np.floor(255 * rng.random((N, 128, S)) ** 4) - 255
    slot = 2 * rng.integers(0, M // 2, (N, 8, S)) + ((np.arange(N)[:, None, None] + np.arange(8)[:, None]) & 1)
    z = rng.integers(0, M, (1, 8, 1)); slot = np.where(slot == z, slot ^ 2, slot)
    slot[0, :, S - 1] = z[0, :, 0]; slot[N - 1, :, 0] = z[0, :, 0]
    x[0, :, S - 1] = rng.integers(-60, 0, 128); x[N - 1, :, 0] = -255
    return pack(x, slot, rng.integers(-255, 256, (N, 128, 1)))
def setup_inputs_ends(rng):
    p = rng.choice(np.array([0, 2.0 ** -6, 2.0 ** -11]), 128); p[0] = 0; p[1] = 2.0 ** -6
    x = np.where(rng.random((N, 128, S)) < p[:, None], 255, -255)
    slot = rng.integers(0, M, (N, 8, S)); slot[:, 1::2] = rng.choice(np.array([0, 1, M - 2, M - 1]), (N, 4, S))
    w = rng.choice(np.array([-255, 255]), (N, 128, 1)); w[:, :16] = 255
    return pack(x, slot, w)
def setup_inputs_spread(rng):
    x = rng.integers(-255, 256, (N, 128, S)) * np.exp2(-rng.integers(0, 9, (N, 1, S)))
    slot = np.floor(M * rng.random((N, 8, S)) ** rng.integers(1, 13, (N, 8, 1))).astype(np.int64) ^ rng.integers(0, M, (1, 8, 1))
    return pack(x, slot, rng.integers(-255, 256, (N, 128, 1)) * np.exp2(-rng.integers(0, 8, (N, 128, 1))))
def check_inputs(d):
    bad = []
    for k in ("x", "w"):
        v = d[k].astype(np.float32)
        if not (np.all(np.abs(v) <= 255) and np.all(v == np.rint(v))): bad.append(k + " whole, -255 to 255")
    if not (np.all(d["slot"] >= 0) and np.all(d["slot"] < M)): bad.append("slot 0 to M - 1")
    return bad
def reference(x, slot, w):
    h = np.arange(8)
    v = np.ascontiguousarray(x.astype(np.float32).astype(np.int64).reshape(N, 8, 16, S).transpose(0, 3, 1, 2)).reshape(N * S, 8, 16)
    s = slot.transpose(0, 2, 1).reshape(N * S, 8)
    c = w.astype(np.int64).reshape(N, 1, 8, 16)
    for layer in range(2):
        if layer == 1: s = np.sum(v.reshape(N, S, 8, 16) * c, axis=3).reshape(N * S, 8) & (M - 1)
        m = np.full((8, M, 16), -256, np.int64); y = np.empty_like(v)
        for t in range(N * S):
            y[t] = np.maximum(m[h, s[t]], v[t]); m[h, s[t]] = y[t]
        v = y
    return {"y": np.ascontiguousarray(v.reshape(N, S, 8, 16).transpose(0, 2, 3, 1)).reshape(N, 128, S).astype(np.float32).astype(BF)}

@@ -1,0 +1,524 @@
+from concourse.bass import DstId, RemoteDMATransfer
+from concourse.mybir import AluOpType as A, AxisListType as AX, ActivationFunctionType as F
+
+H = 2048
+W = H + 256
+WC = H + 16
+PF = W // 3
+CEN = 1152.0
+NEUT = -2048.0
+SC = 2.0 ** -14
+MAG = 12582912.0
+
+ORDER = """
+vCO1.0 gp0.0 ySI0.0 sSI1.0 gDD.0 vpI2.0 vpI0.0 vpI3.0 gM8.0 vpI1.0 yX0.0 gJJ.0 vpF.0 yX1.0 ywc.0 ySJ.0 vCO0.0 vM8.0 vEB.0
+gIC.0 gmZ.0 ySV0.0 vdsq.0 vEB.1 vEE0.0 sEE5.0 sEE1.0 vb1.0 vEE4.0 gmB.0 sEE3.0 vzc.0 sEE7.0 vEE2.0 vDI00.0 vDB00.0 vDI10.0
+sDB00.0 gmC.0 vDB10.0 pPX0.0 vZ.0 sDB10.0 vd16.0 vb16.0 sTO00.0 vEE6.0 vTA.0 pPX1.0 vID.0 vc2.0 vTR.0 gmF.0 gHC.0 gI64.0
+vDI01.0 sTO01.0 pPX0.1 vDI11.0 vDB01.0 vSB.0 vTR.1 sDB01.0 vDB11.0 pQ01.0 sTO10.0 pPX1.1 yCP101.0 yDF1.0 vBS00.0 vZD.0
+vCU0.0 sTO11.0 pPX0.2 vBS01.0 vPR00.0 sDB11.0 pQ11.0 vPR01.0 pPX1.2 sTO02.0 vBS10.0 pQ00.0 vBL0.0 vBS11.0 vCU1.0 pQ01.1
+sTO03.0 vBL1.0 vL100.0 vPR10.0 sSW0.0 vPR11.0 pQ10.0 vL101.0 pQ01.2 pQ11.1 pPX0.3 pPX1.3 vSV0.0 vBS02.0 vL110.0 vL111.0
+pQ11.2 pQ01.3 sTO12.0 pQ00.1 sTO13.0 vCW0.0 vSV0.1 sSW1.0 vSL.0 vXF.0 vCW0.1 ySV0.1 pQ11.3 pQ10.1 sSW1.1 sXF.0 vBS12.0
+vHF0.0 pQ11.4 vCW1.0 vPR00.1 vPR01.1 pQ00.2 vL200.0 pQ01.4 vCW1.1 sDF0.0 vL201.0 vPR10.1 vPR11.1 pQ10.2 sDF0.1 vL210.0
+pQ11.5 vHE0.0 vDW0.0 sTM0.0 sTM1.0 vL211.0 vHF1.0 vDW0.1 sDA.0 sCP000.0 sDA1.0 sCP001.0 vCP001.0 sCP010.0 vHE1.0 vYS0.0
+sCP011.0 vYS0b.0 vYS1.0 vTB00.0 vYS1b.0 sYL3.0 vTB01.0 vzh.0 gTB01.0 vws.0 vZW.0 vZH1.0 vZH0.0 sYL1.0 xLD0.0 vCA0.0 vDA1.0
+vYS0b.1 vCA1.0 sY01.0 vY05.0 sY03.0 pQ00.3 pQ00.4 vY07.0 pQ10.3 gXF.0 pQ00.5 pQ00.6 pQ10.4 vSI0.0 pQ10.5 vDI00.1 pQ10.6
+vDB00.1 vDI01.1 sDB00.1 vDB01.1 pPX1.4 vSI1.0 sDB01.1 pPX0.4 vDI10.1 sTO01.1 vDB10.1 vDI11.1 sDB10.1 vDB11.1 sTO00.1 pPX1.5
+sTO11.1 pQ01.5 pPX0.5 vBS00.1 vBS01.1 vCU0.1 sTO10.1 pPX1.6 vBL0.1 vPR00.2 sTO03.1 pQ11.6 pPX0.6 vBS10.1 vPR01.2 vCU1.1
+pQ00.7 sTO02.1 pQ01.6 vL100.1 sDB11.1 vPR10.2 sSW0.1 vBS11.1 pQ10.7 vL101.1 vBL1.1 vPR11.2 vSV0.2 pQ01.7 pQ11.7 pPX0.7
+pPX1.7 vL110.1 vL111.1 vBS02.1 vCW0.2 sTO12.1 sTO13.1 sSW1.2 vSV0.3 pQ11.8 pQ00.8 vCW0.3 pQ01.8 sSW1.3 vSJ.0 vHF0.1 pQ11.9
+vPR00.3 vPR01.3 pQ00.9 pQ10.8 vBS12.1 pQ01.9 vHE0.1 vCW1.2 pQ11.10 vL200.1 vCP101.0 vCW1.3 sDF1.0 vL201.1 vPR10.3 vPR11.3
+pQ10.9 sDF1.1 vL210.1 pQ11.11 vHF1.1 vDW1.0 sTM0.1 sTM1.1 vL211.1 vDW1.1 sDA.1 sCP100.0 sDA1.1 sCP101.0 vYS0.1 sCP110.0
+vHE1.1 vYS0b.2 sCP111.0 vYS1.1 vTB10.0 vYS1b.1 vTB11.0 sYL1.1 vSJ.1 gTB11.0 vSL.1 sYL3.1 xLD1.0 vCA0.1 vDA1.1 vYS0b.3 vCA1.1
+sY10.0 vY15.0 sY11.0 yY10.0 sY12.0 vY16.0 yY15.0 sY13.0 yY12.0 vY17.0 yY16.0 yY13.0 yY11.0 yY17.0
+"""
+OPT = {"sig": 3.8, "gam": 1.56, "pe": 0.6, "E": 2800.0, "capA": "x", "capB": "s", "xf": "s",
+       "x1a": [[0, 768, 1408, 2048], [0, 896, 1472, 2048]], "x1e": "svv", "x1b": [0, 1024, 2048], "x2b": [0, 1024, 2048],
+       "ua": "ss", "ua1": "ssss", "lb": "ss", "kb": [0, 1024, 2048], "kb1": [0, 1024, 1536, 2048], "order": ORDER}
+
+SCRATCH = {
+    "X": ("sbuf", [128, 2 * H], "bfloat16"), "Y0": ("sbuf", [128, 2 * H], "bfloat16"), "Y1": ("sbuf", [128, 2 * H], "bfloat16"),
+    "wc": ("sbuf", [128, 4], "float32"), "ws": ("sbuf", [128, 4], "float32"),
+    "pI": ("sbuf", [128, 4], "int32"), "pF": ("sbuf", [128, 16], "float32"), "p0": ("sbuf", [128, 4], "int32"),
+    "IC": ("sbuf", [128, 144], "float32"), "JJ": ("sbuf", [128, 128], "float32"), "DD": ("sbuf", [128, 128], "float32"),
+    "I64": ("sbuf", [128, 192], "float32"), "HC": ("sbuf", [128, 32], "float32"),
+    "CO": ("sbuf", [128, 128], "float32"), "EB": ("sbuf", [128, 128], "float32"), "M8": ("sbuf", [128, 8], "float32"),
+    "EE": ("sbuf", [128, 1024], "bfloat16"),
+    "Z": ("sbuf", [128, 144], "float16"), "ZD": ("sbuf", [128, 144], "bfloat16"), "ZW": ("sbuf", [128, 144], "bfloat16"),
+    "TA": ("sbuf", [128, 128], "float32"), "TR": ("sbuf", [128, 128], "float32"), "ID": ("sbuf", [128, 128], "bfloat16"),
+    "mB": ("sbuf", [128, PF], "bfloat16"), "mF": ("sbuf", [128, PF], "float32"), "mC": ("sbuf", [128, PF], "bfloat16"),
+    "mZ": ("sbuf", [128, WC // 3], "float32"), "SV0": ("sbuf", [128, WC], "float32"), "NEG": ("sbuf", [128, W], "bfloat16"),
+    "SJ": ("sbuf", [128, 128], "int32"), "SB": ("sbuf", [128, 128], "bfloat16"), "SL": ("sbuf", [128, 128], "uint16"),
+    "YL": ("sbuf", [128, H], "bfloat16"),
+    "XF": ("sbuf", [128, H], "float32"), "TM": ("sbuf", [128, W], "float32"), "DA": ("sbuf", [128, W], "bfloat16"),
+    "PX0": ("psum", [128, 1024], "float32"), "PX1": ("psum", [128, 1024], "float32"),
+}
+for _h in range(2):
+    SCRATCH.update({
+        "ZH%d" % _h: ("sbuf", [128, 192], "bfloat16"),
+        "SI%d" % _h: ("sbuf", [128, 256], "int32"), "DI%d" % _h: ("sbuf", [128, 512], "int32"), "DB%d" % _h: ("sbuf", [128, 512], "bfloat16"),
+        "IH%d" % _h: ("sbuf", [128, H], "bfloat16"), "IL%d" % _h: ("sbuf", [128, H], "float32"),
+        "TO%d" % _h: ("sbuf", [128, 4], "float32"), "BS%d" % _h: ("sbuf", [128, 4], "float32"), "BL%d" % _h: ("sbuf", [128, 2], "uint16"),
+        "CU%d" % _h: ("sbuf", [128, H], "float16"), "PR%d" % _h: ("sbuf", [128, H], "float16"),
+        "L1%d" % _h: ("sbuf", [128, 128], "uint16"), "L2%d" % _h: ("sbuf", [128, 128], "uint16"),
+        "SW%d" % _h: ("sbuf", [128, WC], "float32"), "CW%d" % _h: ("sbuf", [128, WC], "float32"),
+        "HF%d" % _h: ("sbuf", [128, 32], "float32"), "HE%d" % _h: ("sbuf", [128, 32], "uint16"),
+        "CP0%d" % _h: ("sbuf", [128, W], "bfloat16"), "CP1%d" % _h: ("sbuf", [128, W], "bfloat16"),
+        "YS%d" % _h: ("sbuf", [128, W], "bfloat16"), "CA%d" % _h: ("sbuf", [128, 256], "bfloat16"),
+        "DF%d" % _h: ("sbuf", [128, W], "float32"), "DW%d" % _h: ("sbuf", [128, W], "bfloat16"),
+        "TB%d" % _h: ("sbuf", [128, 512], "bfloat16"), "LD%d" % _h: ("sbuf", [128, 3, 256], "bfloat16"),
+        "Q%d0" % _h: ("psum", [128, 512], "float32"), "Q%d1" % _h: ("psum", [128, 512], "float32"),
+    })
+SEMAPHORES = ["sv", "ss", "sp", "sg", "dsa", "dsb", "dw", "dxa", "dxb", "dxf", "dsj", "dfill", "dz0", "dz1", "dout",
+              "arr0", "arr1", "sent0", "sent1"]
+
+
+def rank_program(g, core, T, topo):
+    rank = T.rank_of(core)
+    if rank is None:
+        return
+    n = len(T.cores)
+    O = OPT
+    Q = {"v": g.vector, "s": g.scalar, "p": g.tensor, "g": g, "y": g.sync}
+    V, S, P = g.vector, g.scalar, g.tensor
+    calls, names = [], {}
+    wr, rd = {}, {}
+
+    def add(q, r, w, busy, lag, emit, soft=()):
+        deps = set()
+        for k in r:
+            if k in wr:
+                deps.add(wr[k])
+        for k in w:
+            if k in wr:
+                deps.add(wr[k])
+            deps.update(rd.get(k, []))
+        me = len(calls)
+        nm = q + (w or r)[-1]
+        names[nm] = names.get(nm, -1) + 1
+        calls.append({"name": "%s.%d" % (nm, names[nm]), "q": q, "deps": deps, "busy": busy, "lag": lag, "emit": emit,
+                      "soft": [(wr[k], d) for k, d in soft]})
+        for k in r:
+            rd.setdefault(k, []).append(me)
+        for k in w:
+            wr[k] = me
+            rd[k] = []
+
+    cnt = {}
+
+    def op(q, r, w, els, fn):
+        def emit():
+            s = "s" + q
+            fn().then_inc(T.sem[s], 1)
+            cnt[s] = cnt.get(s, 0) + 1
+            return (s, cnt[s])
+        add(q, r, w, els * O["pe"] if q == "p" else 55 + 0.83 * max(64, els), 0, emit)
+
+    def dmas(q, s, r, w, pairs, lag):
+        def emit():
+            for o, i in pairs:
+                Q[q].dma_start(o, i).then_inc(T.sem[s], 16)
+                cnt[s] = cnt.get(s, 0) + 16
+            return (s, cnt[s])
+        add(q, r, w, 60 * len(pairs), lag, emit)
+
+    sig, gam = O["sig"], O["gam"]
+
+    dmas("y", "dsa", [], ["SI0"], [(T.SI0[64 * f:64 * f + 64, :], T.slot[:, 0:H]) for f in range(2)], 2300)
+    dmas("s", "dsb", [], ["SI1"], [(T.SI1[64 * f:64 * f + 64, :], T.slot[:, H:2 * H]) for f in range(2)], 2300)
+    dmas("y", "dxa", [], ["X0"], [(T.X[:, 0:H], T.x[:, 0:H])], 4500)
+    dmas("y", "dxb", [], ["X1"], [(T.X[:, H:2 * H], T.x[:, H:2 * H])], 6000)
+    dmas("y", "dw", [], ["wc"], [(T.wc[:, 0:1], T.w[:])], 2500)
+    dmas("y", "dsj", [], ["SJ"], [(T.SJ[:, 16 * j:16 * j + 16], T.slot[j, H:2 * H]) for j in range(8)], 4000)
+
+    fl = {"allow_small_or_imprecise_dtypes": True}
+    op("g", [], ["p0"], 100, lambda: g.iota(T.p0[:, 0:1], [[0, 1]], 0, 1))
+    op("g", [], ["JJ"], 350, lambda: g.iota(T.JJ[:], [[8, 8], [0, 16]], 0, 0, **fl))
+    op("g", [], ["DD"], 350, lambda: g.iota(T.DD[:], [[0, 8], [1, 16]], 0, 0, **fl))
+    op("g", [], ["IC"], 380, lambda: g.iota(T.IC[:], [[1, 144]], 0, 0, **fl))
+    op("g", [], ["M8"], 110, lambda: g.iota(T.M8[:], [[1, 8]], 0, 0, **fl))
+    op("g", [], ["I64"], 480, lambda: g.iota(T.I64[:], [[0, 3], [1, 64]], 0, 0, **fl))
+    op("g", [], ["HC"], 160, lambda: g.iota(T.HC[:], [[0, 2], [1, 16]], int(CEN), 0, **fl))
+    op("v", [], ["CO1"], 128, lambda: V.memset(T.CO[64:128, :], -1.0))
+    op("g", [], ["mB"], 100 + 2 * PF, lambda: g.iota(T.mB[:], [[0, PF]], int(NEUT), 0, **fl))
+    op("g", [], ["mF"], 100 + 2 * PF, lambda: g.iota(T.mF[:], [[0, PF]], -1, 0, **fl))
+    op("g", [], ["mZ"], 100 + 2 * WC // 3, lambda: g.iota(T.mZ[:], [[0, WC // 3]], 0, 0, **fl))
+    fills, fk = [], ["fill", "DW0", "DW1", "DF0", "DF1"]
+    caps = [h for h in range(2) if O["capA" if h == 0 else "capB"] == "x"]
+    if caps:
+        op("g", [], ["mC"], 100 + 2 * PF, lambda: g.iota(T.mC[:], [[0, PF]], 512, 0, **fl))
+    for j in range(3):
+        c = slice(PF * j, PF * j + PF)
+        fills += [(T.NEG[:, c], T.mB[:]), (T.DW0[:, c], T.mB[:]), (T.DF0[:, c], T.mF[:]), (T.DW1[:, c], T.mB[:]), (T.DF1[:, c], T.mF[:])]
+        fills += [(T["CP%d%d" % (l, h)][:, c], T.mC[:]) for l in range(2) for h in caps]
+    fk += ["CP%d%d%d" % (l, h, q) for l in range(2) for h in caps for q in range(2)]
+    dmas("y", "dfill", ["mB", "mF", "mC"], fk, fills, 6000)
+
+    def low_bits(j, m):
+        op("v", ["p0"], ["pI%d" % j], 1, lambda: V.tensor_scalar(T.pI[:, j:j + 1], T.p0[:, 0:1], m, None, A.bitwise_and))
+    for j, m in enumerate((56, 7, 15, 127)):
+        low_bits(j, m)
+    op("v", ["pI0", "pI1", "pI2", "pI3"], ["pF"], 1, lambda: V.tensor_copy(T.pF[:, 0:4], T.pI[:, 0:4]))
+    p56, p7, pd, pp = (T.pF[:, j:j + 1] for j in range(4))
+    dsq, b1, b16, c2, d16, zc, zh = (T.pF[:, j:j + 1] for j in range(4, 11))
+    op("v", ["DD"], ["CO0"], 128, lambda: V.tensor_scalar(T.CO[0:64, :], T.DD[0:64, :], 2.0, None, A.mult))
+    op("v", ["JJ", "pF"], ["EB"], 128, lambda: V.tensor_scalar(T.EB[:], T.JJ[:], p56, None, A.is_equal))
+    op("v", ["M8", "pF"], ["M8"], 8, lambda: V.tensor_scalar(T.M8[:], T.M8[:], p7, None, A.is_equal))
+    op("v", ["EB", "CO0", "CO1"], ["EB"], 256, lambda: V.tensor_tensor(T.EB[:], T.EB[:], T.CO[:], A.mult))
+    op("v", ["pF"], ["dsq"], 1, lambda: V.tensor_scalar(dsq, pd, pd, None, A.mult))
+    op("v", ["dsq"], ["b1"], 1, lambda: V.tensor_scalar(b1, dsq, -1.0, 1.0, A.mult, A.add))
+    op("v", ["pF"], ["zc"], 1, lambda: V.tensor_scalar(zc, pp, pd, 15.0, A.subtract, A.add))
+    op("v", ["IC", "pF"], ["TA"], 128, lambda: V.tensor_scalar(T.TA[:], T.IC[:, 0:128], pp, None, A.is_gt))
+    op("v", ["IC", "zc"], ["TR"], 128, lambda: V.tensor_scalar(T.TR[:], T.IC[:, 0:128], zc, None, A.is_le))
+    op("v", ["TA", "TR"], ["TR"], 256, lambda: V.tensor_tensor(T.TR[:], T.TR[:], T.TA[:], A.mult))
+    op("v", ["dsq"], ["b16"], 1, lambda: V.tensor_scalar(b16, dsq, -16.0, 16.0, A.mult, A.add))
+    op("v", ["pF"], ["c2"], 1, lambda: V.tensor_scalar(c2, pd, 16.0, -CEN, A.mult, A.add))
+    op("v", ["pF"], ["d16"], 1, lambda: V.tensor_scalar(d16, pd, 16.0, None, A.mult))
+    op("v", ["zc"], ["zh"], 1, lambda: V.tensor_scalar(zh, zc, 0.5, -0.5, A.mult, A.add))
+    op("v", ["IC", "zc"], ["Z"], 144, lambda: V.tensor_scalar(T.Z[:], T.IC[:], zc, None, A.is_equal))
+    op("v", ["IC", "zc", "d16"], ["ZD"], 144, lambda: V.tensor_scalar(T.ZD[:], T.IC[:], zc, d16, A.is_equal, A.mult))
+    op("v", ["wc"], ["ws"], 1, lambda: V.tensor_scalar(T.ws[:, 0:1], T.wc[:, 0:1], 1.0 / SC, None, A.mult))
+    op("v", ["I64", "zh", "ws"], ["ZH0"], 192, lambda: V.tensor_scalar(T.ZH0[:], T.I64[:], zh, T.ws[:, 0:1], A.is_equal, A.mult))
+    op("v", ["I64", "zh", "wc"], ["ZH1"], 192, lambda: V.tensor_scalar(T.ZH1[:], T.I64[:], zh, T.wc[:, 0:1], A.is_equal, A.mult))
+    op("v", ["IC", "pF"], ["ID"], 128, lambda: V.tensor_scalar(T.ID[:], T.IC[:, 0:128], pp, None, A.is_equal))
+    op("v", ["IC", "zc", "wc"], ["ZW"], 144, lambda: V.tensor_scalar(T.ZW[:], T.IC[:], zc, T.wc[:, 0:1], A.is_equal, A.mult))
+
+    def slot_list(l):
+        if l == 0:
+            op("v", ["SJ"], ["SB"], 128, lambda: V.tensor_copy(T.SB[:], T.SJ[:]))
+            op("p", ["SB", "ID"], ["Q11"], 128, lambda: P.matmul(T.Q11[:, 0:128], T.SB[:], T.ID[:], True, True))
+            op("v", [], ["Q11", "SL"], 128, lambda: V.tensor_copy(T.SL[:], T.Q11[:, 0:128]))
+            return
+
+        def run():
+            for r in range(16):
+                m = P.matmul(T.Q11[:, 0:128], T.ZW[:, 15 - r:143 - r], T.Y0[:, H + r:2 * H:16], r == 0, r == 15)
+            return m
+        op("p", ["ZW"] + ["Y0%d" % j for j in range(4, 8)], ["Q11"], 2048, run)
+        op("v", [], ["Q11", "SJ"], 128, lambda: V.tensor_copy(T.SJ[:], T.Q11[:, 0:128]))
+        op("v", ["SJ"], ["SJ"], 128, lambda: V.tensor_scalar(T.SJ[:], T.SJ[:], 255, None, A.bitwise_and))
+        op("v", ["SJ"], ["SL"], 128, lambda: V.tensor_copy(T.SL[:], T.SJ[:]))
+
+    def spread(i):
+        o = T.EE[:, 128 * i:128 * i + 128]
+        if i % 2:
+            op("s", ["EB", "M8"], ["EE%d" % i], 128, lambda: S.activation(o, T.EB[:], F.Identity, scale=T.M8[:, i:i + 1]))
+        else:
+            op("v", ["EB", "M8"], ["EE%d" % i], 128, lambda: V.tensor_scalar(o, T.EB[:], T.M8[:, i:i + 1], None, A.mult))
+    for i in range(8):
+        spread(i)
+
+    def digit(h, d):
+        di, db = T["DI%d" % h][:, 256 * d:256 * d + 256], T["DB%d" % h]
+        k = "%d%d" % (h, d)
+        if d == 0:
+            op("v", ["SI%d" % h], ["DI" + k], 256, lambda: V.tensor_scalar(di, T["SI%d" % h][:], 4, 15, A.arith_shift_right, A.bitwise_and))
+        else:
+            op("v", ["SI%d" % h], ["DI" + k], 256, lambda: V.tensor_scalar(di, T["SI%d" % h][:], 15, None, A.bitwise_and))
+        op("v", ["DI" + k], ["DB" + k], 256, lambda: V.tensor_copy(db[:, 256 * d:256 * d + 256], di))
+        u = db[64:128, 256 * d:256 * d + 256]
+        op("s", ["DB" + k], ["DB" + k], 256, lambda: S.activation(u, u, F.Square))
+
+    def indicate(h, d, q):
+        px = T["PX%d" % q]
+
+        def run():
+            for j in range(4):
+                i = 4 * q + j
+                m = P.matmul(px[:, 256 * j:256 * j + 256], T.EE[:, 128 * i:128 * i + 128],
+                             T["DB%d" % h][:, 256 * d:256 * d + 256], True, True)
+            return m
+        op("p", ["DB%d%d" % (h, d)] + ["EE%d" % (4 * q + j) for j in range(4)], ["PX%d" % q], 1024, run)
+        o = T[("IH%d", "IL%d")[d] % h][:, 1024 * q:1024 * q + 1024]
+        c = 2 * d + q
+        op("s", [("b1", "b16")[d]], ["PX%d" % q, "I%d%d%d" % (d, h, q), "TO%d%d" % (h, c)], 1050,
+           lambda: S.activation(o, px[:], F.Relu, bias=(b1, b16)[d], scale=(1.0, 16.0)[d], accum_out=T["TO%d" % h][:, c:c + 1]))
+
+    def base(h, d):
+        op("p", ["TR", "TO%d%d" % (h, 2 * d), "TO%d%d" % (h, 2 * d + 1)], ["Q%d1" % h], 256,
+           lambda: P.matmul(T["Q%d1" % h][:, 0:2], T.TR[:], T["TO%d" % h][:, 2 * d:2 * d + 2], True, True))
+        op("v", [], ["Q%d1" % h, "BS%d%d" % (h, 2 * d)], 2,
+           lambda: V.tensor_reduce(T["BS%d" % h][:, 2 * d:2 * d + 1], T["Q%d1" % h][:, 0:2], AX.X, A.add))
+
+    def gather_mm(h, q, src, keys, z, zk, start, stop):
+        def run():
+            for r in range(16):
+                m = P.matmul(T["Q%d%d" % (h, q)][:, 0:64], z[:, 15 - r:143 - r], src[:, 1024 * q + r:1024 * q + 1024:16],
+                             start and r == 0, stop and r == 15)
+            return m
+        op("p", keys + [zk], ["Q%d%d" % (h, q)], 1024, run)
+
+    def to_list(h, q, name, mul, plus):
+        op("v", [], ["Q%d%d" % (h, q), "%s%d%d" % (name, h, q)], 64,
+           lambda: V.tensor_scalar(T["%s%d" % (name, h)][:, 64 * q:64 * q + 64], T["Q%d%d" % (h, q)][:, 0:64], mul, plus, A.mult, A.add))
+
+    def pass1(h):
+        bs, ih, cu, pr = T["BS%d" % h], T["IH%d" % h], T["CU%d" % h], T["PR%d" % h]
+        base(h, 0)
+        op("v", ["BS%d0" % h, "I0%d0" % h, "I0%d1" % h], ["CU%d" % h], 1024,
+           lambda: V.tensor_tensor_scan(cu[:], ih[:], ih[:], bs[:, 0:1], A.add, A.max))
+
+        def piece(q):
+            c = slice(1024 * q, 1024 * q + 1024)
+            op("v", ["CU%d" % h, "I0%d%d" % (h, q)], ["PR%d%d" % (h, q)], 512,
+               lambda: V.tensor_tensor_scan(pr[:, c], cu[:, c], ih[:, c], 0.0, A.max, A.mult))
+            gather_mm(h, q, pr, ["PR%d%d" % (h, q)], T.Z, "Z", True, True)
+            to_list(h, q, "L1", 1.0, 0.25)
+        piece(0); piece(1)
+
+    def span(name, h, a, b):
+        return ["%s%d%d" % (name, h, q) for q in range(a // 1024, (b + 1023) // 1024)]
+
+    def scatter1(e, h, a, b):
+        keys = span("I1", h, a, b) + span("L1", h, a, b)
+        sw = "SV0" if e == "v" else "SW%d" % h
+        o = T[sw][:, 0:H + 1].indirect(T["L1%d" % h][:, a // 16:b // 16])
+        i = T["IL%d" % h][:, a:b]
+        if e == "v":
+            op("v", keys, [sw], sig * (b - a), lambda: V.tensor_scalar(o, i, 0.0625, 0.0, A.mult, A.add))
+        else:
+            op("s", keys, [sw], sig * (b - a), lambda: S.activation(o, i, F.Tanh))
+
+    def pass2(h):
+        bs, cw, to = T["BS%d" % h], T["CW%d" % h], T["TO%d" % h]
+        base(h, 1)
+        op("v", ["BS%d2" % h, "c2"], ["CW%d" % h], 1, lambda: V.tensor_scalar(cw[:, 0:1], bs[:, 2:3], 0.0625, c2, A.mult, A.add))
+        op("v", ["BS%d0" % h, "TO%d0" % h, "TO%d1" % h], ["BS%d1" % h], 1,
+           lambda: V.tensor_scalar(bs[:, 1:2], bs[:, 0:1], to[:, 0:1], to[:, 1:2], A.add, A.add))
+        op("v", ["BS%d0" % h, "BS%d1" % h], ["BL%d" % h], 1, lambda: V.tensor_copy(T["BL%d" % h][:], bs[:, 0:2]))
+        for q in range(2):
+            gather_mm(h, q, T["IH%d" % h], ["I0%d%d" % (h, q)], T.ZD, "ZD", True, False)
+        if h == 0:
+            op("v", ["SW0", "SV0"], ["CW0"], H,
+               lambda: V.tensor_tensor_scan(cw[:, 1:H + 1], T.SV0[:, 1:H + 1], T.SW0[:, 1:H + 1], cw[:, 0:1], A.add, A.add))
+        else:
+            op("v", ["SW1", "fill"], ["CW1"], H,
+               lambda: V.tensor_tensor_scan(cw[:, 1:H + 1], T.NEG[:, 0:H], T.SW1[:, 1:H + 1], cw[:, 0:1], A.max, A.add))
+
+        def piece(q):
+            c = slice(1024 * q, 1024 * q + 1024)
+            op("v", ["CW%d" % h, "L1%d%d" % (h, q), "I1%d%d" % (h, q)], ["PR%d%d" % (h, q)], gam * 1024,
+               lambda: V.tensor_tensor(T["PR%d" % h][:, c], cw[:, 0:H + 1].indirect(T["L1%d" % h][:, 64 * q:64 * q + 64]),
+                                       T["IL%d" % h][:, c], A.mult))
+            gather_mm(h, q, T["PR%d" % h], ["PR%d%d" % (h, q)], T.Z, "Z", False, True)
+            to_list(h, q, "L2", 0.0625, CEN + 0.25)
+        piece(0); piece(1)
+        op("v", ["CW%d" % h, "BL%d" % h, "HC"], ["HF%d" % h], 50,
+           lambda: V.tensor_tensor(T["HF%d" % h][:], cw[:, 0:H + 1].indirect(T["BL%d" % h][:]), T.HC[:], A.add))
+        op("v", ["HF%d" % h], ["HE%d" % h], 32, lambda: V.tensor_scalar(T["HE%d" % h][:], T["HF%d" % h][:], 0.25, None, A.add))
+
+    def next_slots(h):
+        def part(j):
+            def run():
+                for i in (2 * j, 2 * j + 1):
+                    m = P.matmul(T["Q%d0" % h][:, 0:256], T["ZH%d" % h][:, 7 - i:135 - i],
+                                 T.Y0[:, H * h + 256 * i:H * h + 256 * i + 256], i == 0, i == 7)
+                return m
+            op("p", ["ZH%d" % h, "Y0%d" % (4 * h + j)], ["Q%d0" % h], 512, run)
+        for j in range(4):
+            part(j)
+        op("v", [], ["Q%d0" % h, "SI%d" % h], 256, lambda: V.tensor_copy(T["SI%d" % h][:], T["Q%d0" % h][:, 0:256]))
+
+    def receivers(l, r):
+        return [1] if (l, r) == (1, 0) else list(range(r + 1, n))
+
+    def engine_mask(l, r):
+        m = topo.mask(T.cores[r], T.cores[r + 1])
+        for t in receivers(l, r):
+            m &= topo.mask(T.cores[r], T.cores[t])
+        return m
+
+    def layer(l):
+        src = (T.X, T.Y0)[l]
+        bkeys = ["X1"] if l == 0 else ["Y0%d" % j for j in range(4, 8)]
+        dst = T["Y%d" % l]
+        df, dw = T["DF%d" % l], T["DW%d" % l]
+        win, wink = (T.DA, dw), ("DA", "DW%d" % l)
+        tb, ld = T["TB%d" % l], T["LD%d" % l]
+        cp = (T["CP%d0" % l], T["CP%d1" % l])
+        cpk = [["CP%d%d%d" % (l, h, q) for q in range(2)] for h in range(2)]
+
+        if l == 1:
+            next_slots(0); next_slots(1)
+            dmas("g", "dxf", ["Y0%d" % j for j in range(4)], ["XF"], [(T.XF[:], T.Y0[:, 0:H])], 6000)
+        elif O["xf"] == "s":
+            op("s", ["X0"], ["XF"], H, lambda: S.activation(T.XF[:], T.X[:, 0:H], F.Identity, scale=SC))
+        else:
+            op("v", ["X0"], ["XF"], H, lambda: V.tensor_scalar(T.XF[:], T.X[:, 0:H], SC, None, A.mult))
+        for h, d in ((0, 0), (1, 0), (0, 1), (1, 1)):
+            digit(h, d)
+            indicate(h, d, 0); indicate(h, d, 1)
+        pass1(0); pass1(1)
+        z = WC // 3
+        dmas("y", "dz%d" % l, ["mZ"], ["SW0", "SV0"], [(T[k][:, z * j:z * j + z], T.mZ[:]) for k in ("SW0", "SV0") for j in range(3)], 5000)
+        slot_list(l)
+        for who, h, cuts in ((O["x1e"], 0, O["x1a"][l]), ("ssss", 1, O["x1b"])):
+            for e, a, b in zip(who, cuts, cuts[1:]):
+                scatter1(e, h, a, b)
+        pass2(0); pass2(1)
+
+        def place_a(q):
+            op("s", ["XF", "L20%d" % q], ["DF%d" % l], sig * 1024,
+               lambda: S.activation(df[:].indirect(T.L20[:, 64 * q:64 * q + 64]), T.XF[:, 1024 * q:1024 * q + 1024], F.Tanh))
+
+        def place_b(a, b):
+            op("v", bkeys + span("L2", 1, a, b), ["DW%d" % l], sig * (b - a),
+               lambda: V.tensor_copy(dw[:].indirect(T.L21[:, a // 16:b // 16]), src[:, H + a:H + b]))
+        place_a(0); place_a(1)
+        for a, b in zip(O["x2b"], O["x2b"][1:]):
+            place_b(a, b)
+        HW = W // 2
+
+        def rounded(q):
+            c = slice(HW * q, HW * q + HW)
+            op("s", ["DF%d" % l], ["TM%d" % q], HW, lambda: S.activation(T.TM[:, c], df[:, c], F.Identity, bias=MAG, scale=1.0 / SC))
+            op("s", ["TM%d" % q], ["DA%d" % q] + (["DA"] if q == 0 else []), HW, lambda: S.activation(T.DA[:, c], T.TM[:, c], F.Identity, bias=-MAG))
+        rounded(0); rounded(1)
+        part = [["DA0", "DA1"], [wink[1], wink[1]]]
+
+        def cap(h, e):
+            if e == "x":
+                op("v", ["HE%d" % h, "fill"], cpk[h], sig * 256,
+                   lambda: V.tensor_copy(cp[h][:].indirect(T["HE%d" % h][:, 0:16]), T.NEG[:, 0:256]))
+                return
+
+            def piece(q):
+                c = slice(HW * q, HW * q + HW)
+                if e == "v":
+                    op("v", [part[h][q]], [cpk[h][q]], HW / 2, lambda: V.tensor_scalar(cp[h][:, c], win[h][:, c], 1024.0, 261632.0, A.mult, A.add))
+                else:
+                    op("s", [part[h][q]], [cpk[h][q]], HW, lambda: S.activation(cp[h][:, c], win[h][:, c], F.Identity, bias=261632.0, scale=1024.0))
+            piece(0); piece(1)
+        cap(0, O["capA"]); cap(1, O["capB"])
+
+        def running(h, split):
+            ys = T["YS%d" % h]
+            if not split:
+                op("v", cpk[h] + part[h] + [wink[h]], ["YS%d" % h, "YS%db" % h], HW,
+                   lambda: V.tensor_tensor_scan(ys[:], cp[h][:], win[h][:], NEUT, A.min, A.max))
+                return
+            op("v", [cpk[h][0], part[h][0], wink[h]], ["YS%d" % h], HW / 2,
+               lambda: V.tensor_tensor_scan(ys[:, 0:HW], cp[h][:, 0:HW], win[h][:, 0:HW], NEUT, A.min, A.max))
+            op("v", [cpk[h][1], part[h][1], wink[h], "YS%d" % h], ["YS%db" % h], HW / 2,
+               lambda: V.tensor_tensor_scan(ys[:, HW:W], cp[h][:, HW:W], win[h][:, HW:W], ys[:, HW - 1:HW], A.min, A.max))
+
+        def table(h):
+            op("v", ["YS%d" % h, "YS%db" % h, "HE%d" % h], ["TB%d%d" % (l, h)], gam * 256,
+               lambda: V.tensor_copy(tb[:, 256 * h:256 * h + 256], T["YS%d" % h][:].indirect(T["HE%d" % h][:, 16:32])))
+
+        def store(a, b, w):
+            if l == 1:
+                dmas("y", "dout", w, [], [(T.y[:, a:b], dst[:, a:b])], 2000 + (b - a))
+
+        def unsort_a(e, a, b):
+            i = T.YS0[:].indirect(T.L20[:, a // 16:b // 16])
+            r = ["YS0", "YS0b"] + span("L2", 0, a, b)
+            w = ["Y%d%d" % (l, j) for j in range(a // 512, b // 512)]
+            k = SC if l == 0 else 1.0
+            if e == "v":
+                op("v", r, w, gam * (b - a), lambda: V.tensor_scalar(dst[:, a:b], i, k, None, A.mult))
+            else:
+                op("s", r, w, gam * (b - a), lambda: S.activation(dst[:, a:b], i, F.Identity, scale=k))
+            store(a, b, w)
+
+        def local_b(e, a, b):
+            i = T.YS1[:].indirect(T.L21[:, a // 16:b // 16])
+            r, w = ["YS1", "YS1b"] + span("L2", 1, a, b), ["YL%d" % j for j in range(a // 512, b // 512)]
+            if e == "v":
+                op("v", r, w, gam * (b - a), lambda: V.tensor_copy(T.YL[:, a:b], i))
+            else:
+                op("s", r, w, gam * (b - a), lambda: S.activation(T.YL[:, a:b], i, F.Identity))
+
+        def merge(out, outk, a, ak, b, bk):
+            op("v", [ak, bk], [outk], 512, lambda: V.tensor_tensor(out, a, b, A.max))
+
+        running(0, True); table(0)
+        running(1, True)
+        if rank < n - 1:
+            table(1)
+        for j, e in enumerate(O["lb"]):
+            local_b(e, H // len(O["lb"]) * j, H // len(O["lb"]) * (j + 1))
+        senders = [r for r in range(rank) if rank in receivers(l, r)]
+        if senders:
+            def landed():
+                cnt["arr%d" % l] = sum(bin(engine_mask(l, r)).count("1") for r in senders)
+                return ("arr%d" % l, cnt["arr%d" % l])
+            soft = [("TB%d0" % l, O["E"]), ("TB%d1" % l, O["E"])] if rank < n - 1 else [("TB%d0" % l, O["E"] + 400), ("YS1b", O["E"] + 400)]
+            add("x", [], ["LD%d" % l], 0, 0, landed, soft)
+        if rank < n - 1:
+            peers = [T.cores[t] for t in receivers(l, rank)]
+            passed = (l, rank) == (1, 1)
+
+            def send():
+                ids = [DstId(rid=topo.addr(c)[0], pnc=topo.addr(c)[1]) for c in peers]
+                srcs = [tb[:, 0:256], tb[:, 256:512]] + ([ld[:, 0, :]] if passed else [])
+                g.remote_dma_fused([RemoteDMATransfer(dst_ids=ids, dma_engine_mask=engine_mask(l, rank), remote_sem=T.sem["arr%d" % l],
+                                                      srcs=srcs, dsts=[ld[:, rank, :] for c in peers], alu_op=2)],
+                                   local_sem=T.sem["sent%d" % l])
+                cnt["sent%d" % l] = bin(engine_mask(l, rank)).count("1")
+                return ("sent%d" % l, cnt["sent%d" % l])
+            add("g", (["LD%d" % l] if passed else []) + ["TB%d0" % l, "TB%d1" % l], [], 300, 2000, send)
+        if senders:
+            ca, cak = ld[:, senders[0], :], "LD%d" % l
+            for r in senders[1:]:
+                merge(T.CA0[:], "CA0", ca, cak, ld[:, r, :], "LD%d" % l)
+                ca, cak = T.CA0[:], "CA0"
+            op("v", [cak, "HE0"], ["DA", "DA0", "DA1"], sig * 256, lambda: V.tensor_copy(T.DA[:].indirect(T.HE0[:, 0:16]), ca))
+            running(0, False)
+            merge(T.CA1[:], "CA1", ca, cak, tb[:, 0:256], "TB%d0" % l)
+            cb, cbk = T.CA1[:], "CA1"
+        else:
+            cb, cbk = tb[:, 0:256], "TB%d0" % l
+
+        def carry_b(a, b):
+            w = ["Y%d%d" % (l, j) for j in range((H + a) // 512, (H + b) // 512)]
+            op("v", [cbk, "SL"] + ["YL%d" % j for j in range(a // 512, b // 512)], w, gam * (b - a),
+               lambda: V.tensor_tensor(dst[:, H + a:H + b], cb.indirect(T.SL[:, a // 16:b // 16]), T.YL[:, a:b], A.max))
+            store(H + a, H + b, w)
+        who = O["ua"] if l == 0 else O["ua1"]
+        for j, e in enumerate(who):
+            unsort_a(e, H // len(who) * j, H // len(who) * (j + 1))
+        cuts = O["kb"] if l == 0 else O["kb1"]
+        for a, b in zip(cuts, cuts[1:]):
+            carry_b(a, b)
+
+    layer(0); layer(1)
+
+    N = len(calls)
+    if O.get("hook"):
+        O["hook"](calls)
+    users = [[] for _ in range(N)]
+    left = [0] * N
+    for i, c in enumerate(calls):
+        for d in list(c["deps"]) + [d for d, x in c["soft"]]:
+            users[d].append(i); left[i] += 1
+    place = {nm: j for j, nm in enumerate(O["order"].split())}
+    prio = [0.0] * N
+    for i in range(N - 1, -1, -1):
+        prio[i] = place.get(calls[i]["name"], min([prio[u] for u in users[i]] + [1e9]) - 0.5)
+    ready, order = [i for i in range(N) if left[i] == 0], []
+    while ready:
+        i = min(ready, key=lambda j: (prio[j], j))
+        ready.remove(i); order.append(i)
+        for u in users[i]:
+            left[u] -= 1
+            if left[u] == 0:
+                ready.append(u)
+
+    seen, token = {}, {}
+
+    def wait(q, tok):
+        s, v = tok
+        if seen.get((q, s), 0) < v:
+            Q[q].wait_ge(T.sem[s], v)
+            seen[(q, s)] = v
+    for i in order:
+        c = calls[i]
+        need = {}
+        for d in c["deps"]:
+            s, v = token[d]
+            need[s] = max(need.get(s, 0), v)
+        for s in sorted(need):
+            wait(c["q"], (s, need[s]))
+        token[i] = c["emit"]()
+    for s in sorted(cnt):
+        wait("g", (s, cnt[s]))

@@ -1,109 +1,218 @@
+import math
 from concourse.bass import DstId, RemoteDMATransfer
 from concourse.mybir import AluOpType as A, AxisListType as AX, ActivationFunctionType as F
 
 H = 2048
 W = H + 256
-WC = H + 16
+HW = W // 2
 PF = W // 3
 CEN = 1152.0
-NEUT = -2048.0
-SC = 2.0 ** -14
-MAG = 12582912.0
+WC = H + 16
+SC = 2.0 ** -12
 
-ORDER = """
-vCO1.0 gp0.0 ySI0.0 sSI1.0 gDD.0 vpI2.0 vpI0.0 vpI3.0 gM8.0 vpI1.0 yX0.0 gJJ.0 vpF.0 yX1.0 ywc.0 ySJ.0 vCO0.0 vM8.0 vEB.0
-gIC.0 gmZ.0 ySV0.0 vdsq.0 vEB.1 vEE0.0 sEE5.0 sEE1.0 vb1.0 vEE4.0 gmB.0 sEE3.0 vzc.0 sEE7.0 vEE2.0 vDI00.0 vDB00.0 vDI10.0
-sDB00.0 gmC.0 vDB10.0 pPX0.0 vZ.0 sDB10.0 vd16.0 vb16.0 sTO00.0 vEE6.0 vTA.0 pPX1.0 vID.0 vc2.0 vTR.0 gmF.0 gHC.0 gI64.0
-vDI01.0 sTO01.0 pPX0.1 vDI11.0 vDB01.0 vSB.0 vTR.1 sDB01.0 vDB11.0 pQ01.0 sTO10.0 pPX1.1 yCP101.0 yDF1.0 vBS00.0 vZD.0
-vCU0.0 sTO11.0 pPX0.2 vBS01.0 vPR00.0 sDB11.0 pQ11.0 vPR01.0 pPX1.2 sTO02.0 vBS10.0 pQ00.0 vBL0.0 vBS11.0 vCU1.0 pQ01.1
-sTO03.0 vBL1.0 vL100.0 vPR10.0 sSW0.0 vPR11.0 pQ10.0 vL101.0 pQ01.2 pQ11.1 pPX0.3 pPX1.3 vSV0.0 vBS02.0 vL110.0 vL111.0
-pQ11.2 pQ01.3 sTO12.0 pQ00.1 sTO13.0 vCW0.0 vSV0.1 sSW1.0 vSL.0 vXF.0 vCW0.1 ySV0.1 pQ11.3 pQ10.1 sSW1.1 sXF.0 vBS12.0
-vHF0.0 pQ11.4 vCW1.0 vPR00.1 vPR01.1 pQ00.2 vL200.0 pQ01.4 vCW1.1 sDF0.0 vL201.0 vPR10.1 vPR11.1 pQ10.2 sDF0.1 vL210.0
-pQ11.5 vHE0.0 vDW0.0 sTM0.0 sTM1.0 vL211.0 vHF1.0 vDW0.1 sDA.0 sCP000.0 sDA1.0 sCP001.0 vCP001.0 sCP010.0 vHE1.0 vYS0.0
-sCP011.0 vYS0b.0 vYS1.0 vTB00.0 vYS1b.0 sYL3.0 vTB01.0 vzh.0 gTB01.0 vws.0 vZW.0 vZH1.0 vZH0.0 sYL1.0 xLD0.0 vCA0.0 vDA1.0
-vYS0b.1 vCA1.0 sY01.0 vY05.0 sY03.0 pQ00.3 pQ00.4 vY07.0 pQ10.3 gXF.0 pQ00.5 pQ00.6 pQ10.4 vSI0.0 pQ10.5 vDI00.1 pQ10.6
-vDB00.1 vDI01.1 sDB00.1 vDB01.1 pPX1.4 vSI1.0 sDB01.1 pPX0.4 vDI10.1 sTO01.1 vDB10.1 vDI11.1 sDB10.1 vDB11.1 sTO00.1 pPX1.5
-sTO11.1 pQ01.5 pPX0.5 vBS00.1 vBS01.1 vCU0.1 sTO10.1 pPX1.6 vBL0.1 vPR00.2 sTO03.1 pQ11.6 pPX0.6 vBS10.1 vPR01.2 vCU1.1
-pQ00.7 sTO02.1 pQ01.6 vL100.1 sDB11.1 vPR10.2 sSW0.1 vBS11.1 pQ10.7 vL101.1 vBL1.1 vPR11.2 vSV0.2 pQ01.7 pQ11.7 pPX0.7
-pPX1.7 vL110.1 vL111.1 vBS02.1 vCW0.2 sTO12.1 sTO13.1 sSW1.2 vSV0.3 pQ11.8 pQ00.8 vCW0.3 pQ01.8 sSW1.3 vSJ.0 vHF0.1 pQ11.9
-vPR00.3 vPR01.3 pQ00.9 pQ10.8 vBS12.1 pQ01.9 vHE0.1 vCW1.2 pQ11.10 vL200.1 vCP101.0 vCW1.3 sDF1.0 vL201.1 vPR10.3 vPR11.3
-pQ10.9 sDF1.1 vL210.1 pQ11.11 vHF1.1 vDW1.0 sTM0.1 sTM1.1 vL211.1 vDW1.1 sDA.1 sCP100.0 sDA1.1 sCP101.0 vYS0.1 sCP110.0
-vHE1.1 vYS0b.2 sCP111.0 vYS1.1 vTB10.0 vYS1b.1 vTB11.0 sYL1.1 vSJ.1 gTB11.0 vSL.1 sYL3.1 xLD1.0 vCA0.1 vDA1.1 vYS0b.3 vCA1.1
-sY10.0 vY15.0 sY11.0 yY10.0 sY12.0 vY16.0 yY15.0 sY13.0 yY12.0 vY17.0 yY16.0 yY13.0 yY11.0 yY17.0
-"""
-OPT = {"sig": 3.8, "gam": 1.56, "pe": 0.6, "E": 2800.0, "capA": "x", "capB": "s", "xf": "s",
-       "x1a": [[0, 768, 1408, 2048], [0, 896, 1472, 2048]], "x1e": "svv", "x1b": [0, 1024, 2048], "x2b": [0, 1024, 2048],
-       "ua": "ss", "ua1": "ssss", "lb": "ss", "kb": [0, 1024, 2048], "kb1": [0, 1024, 1536, 2048], "order": ORDER}
+OPT = {"sig": 2.6, "gam": 1.3, "pe": 0.46, "E": 2800.0, "hop": 220.0,
+       "near": [["ss", "ss"], ["ss", "ss"]],
+       "look": [["vvvv", "vvvv"], ["vvvv", "vvvv"]],
+       "back": [["s", "s"], ["s", "s"]],
+       "pos": "tt", "put": ["ss", "ss"], "cap": ["xx", "xx"], "tab": "vv", "size": [2, 1], "carry": ["ka", "ak"], "moves": 210000, "heat": 200.0,
+       "early": True, "zero": 0, "joint": [False, False], "mp": False, "late": [1, 0], "addv": [["123", "123"], ["123", "123"]], "slow": 2.2, "mix": 0.6, "seed": 9, "narrow": ["vv", "vv"], "free": [], "dl": 2.0,
+       "cuts": [[[("s", 0, 1024), ("v", 1024, 2048)], [("s", 0, 1024), ("s", 1024, 2048)]]] * 2,
+       "pieces": [[(0, 2), (2, 4)], [(0, 2), (2, 3), (3, 4)]], "rounds": 1,
+       "steps": [("carry", 0), ("front", 0), ("sums", 0), ("near", 0), ("count", 0), ("early", 0), ("carry", 1), ("front", 1),
+                 ("near", 1), ("late", 0), ("sums", 1), ("count", 1), ("early", 1), ("late", 1), ("put", 0), ("put", 1),
+                 ("heads", 1), ("cap", 1), ("first", 1), ("heads", 0), ("cap", 0), ("first", 0), ("lists", 0), ("lists", 1)],
+       "far": [50000.0, 12000.0]}
 
+SCRATCH = {}
+WIDE = all(x == "123" for y in OPT["addv"] for x in y)
+NZ = 512
+NST = 1024 if "v" in OPT["put"][0] else 256
 SCRATCH = {
-    "X": ("sbuf", [128, 2 * H], "bfloat16"), "Y0": ("sbuf", [128, 2 * H], "bfloat16"), "Y1": ("sbuf", [128, 2 * H], "bfloat16"),
+    "Y0": ("sbuf", [128, 8, 512] if OPT["pos"] == "tt" else [128, 2 * H], "bfloat16"), "Y1": ("sbuf", [128, 2 * H], "bfloat16"),
     "wc": ("sbuf", [128, 4], "float32"), "ws": ("sbuf", [128, 4], "float32"),
-    "pI": ("sbuf", [128, 4], "int32"), "pF": ("sbuf", [128, 16], "float32"), "p0": ("sbuf", [128, 4], "int32"),
-    "IC": ("sbuf", [128, 144], "float32"), "JJ": ("sbuf", [128, 128], "float32"), "DD": ("sbuf", [128, 128], "float32"),
-    "I64": ("sbuf", [128, 192], "float32"), "HC": ("sbuf", [128, 32], "float32"),
-    "CO": ("sbuf", [128, 128], "float32"), "EB": ("sbuf", [128, 128], "float32"), "M8": ("sbuf", [128, 8], "float32"),
-    "EE": ("sbuf", [128, 1024], "bfloat16"),
-    "Z": ("sbuf", [128, 144], "float16"), "ZD": ("sbuf", [128, 144], "bfloat16"), "ZW": ("sbuf", [128, 144], "bfloat16"),
-    "TA": ("sbuf", [128, 128], "float32"), "TR": ("sbuf", [128, 128], "float32"), "ID": ("sbuf", [128, 128], "bfloat16"),
-    "mB": ("sbuf", [128, PF], "bfloat16"), "mF": ("sbuf", [128, PF], "float32"), "mC": ("sbuf", [128, PF], "bfloat16"),
-    "mZ": ("sbuf", [128, WC // 3], "float32"), "SV0": ("sbuf", [128, WC], "float32"), "NEG": ("sbuf", [128, W], "bfloat16"),
-    "SJ": ("sbuf", [128, 128], "int32"), "SB": ("sbuf", [128, 128], "bfloat16"), "SL": ("sbuf", [128, 128], "uint16"),
-    "YL": ("sbuf", [128, H], "bfloat16"),
-    "XF": ("sbuf", [128, H], "float32"), "TM": ("sbuf", [128, W], "float32"), "DA": ("sbuf", [128, W], "bfloat16"),
-    "PX0": ("psum", [128, 1024], "float32"), "PX1": ("psum", [128, 1024], "float32"),
+    "pI": ("sbuf", [128, 8], "int32"), "pF": ("sbuf", [128, 32], "float32"), "p0": ("sbuf", [128, 4], "int32"),
+    "IC": ("sbuf", [128, 144], "float32"), "KEY": ("sbuf", [128, 128], "float32"), "JG": ("sbuf", [128, 128], "float32"),
+    "I2": ("sbuf", [128, 4, 64], "bfloat16"), "CS": ("sbuf", [128, H], "bfloat16"), "WS": ("sbuf", [128, H], "bfloat16"),
+    "ID": ("sbuf", [128, 4, 32], "bfloat16"), "NID": ("sbuf", [128, 128], "bfloat16"), "N16": ("sbuf", [128, 128], "bfloat16"),
+    "ZR": ("sbuf", [128, NZ], "bfloat16"), "TA": ("sbuf", [128, 128], "float32"), "TQ": ("sbuf", [128, 128], "bfloat16"), "TR": ("sbuf", [128, 128], "float32"),
+    "HD": ("sbuf", [128, 256], "float32"), "HC": ("sbuf", [128, 32], "float16"),
+    "ZW": ("sbuf", [128, 144], "bfloat16"), "GW": ("sbuf", [128, 128], "bfloat16"),
+    "U2": ("sbuf", [128, 8, 256], "bfloat16"),
+    "mB": ("sbuf", [128, 256], "bfloat16"), "mF": ("sbuf", [128, 384], "float32"), "mC": ("sbuf", [128, PF], "bfloat16"),
+    "ST": ("sbuf", [128, NST], "bfloat16"), "LA": ("sbuf", [128, 3, 256], "bfloat16"),
+    "JJ": ("sbuf", [128, 128], "float32"), "DD": ("sbuf", [128, 128], "float32"), "JH": ("sbuf", [128, 128], "float32"),
+    "I64": ("sbuf", [128, 192], "float32"), "HR": ("sbuf", [128, 32], "float32"), "M8": ("sbuf", [128, 8], "float32"),
+    "CO": ("sbuf", [128, 128], "float32"), "EB": ("sbuf", [128, 128], "float32"), "EE": ("sbuf", [128, 1024], "bfloat16"),
+    "Z": ("sbuf", [128, 144], "float16"), "ZD": ("sbuf", [128, 144], "bfloat16"), "ZH": ("sbuf", [128, 192], "bfloat16"),
+    "GH": ("sbuf", [128, 128], "bfloat16"), "TC": ("sbuf", [128, 128], "float32"), "TS": ("sbuf", [128, 128], "float32"),
+    "mZ": ("sbuf", [128, WC // 3], "float32"), "mN": ("sbuf", [128, 512], "bfloat16"), "NEG": ("sbuf", [128, H], "bfloat16"),
 }
 for _h in range(2):
     SCRATCH.update({
-        "ZH%d" % _h: ("sbuf", [128, 192], "bfloat16"),
-        "SI%d" % _h: ("sbuf", [128, 256], "int32"), "DI%d" % _h: ("sbuf", [128, 512], "int32"), "DB%d" % _h: ("sbuf", [128, 512], "bfloat16"),
-        "IH%d" % _h: ("sbuf", [128, H], "bfloat16"), "IL%d" % _h: ("sbuf", [128, H], "float32"),
-        "TO%d" % _h: ("sbuf", [128, 4], "float32"), "BS%d" % _h: ("sbuf", [128, 4], "float32"), "BL%d" % _h: ("sbuf", [128, 2], "uint16"),
-        "CU%d" % _h: ("sbuf", [128, H], "float16"), "PR%d" % _h: ("sbuf", [128, H], "float16"),
-        "L1%d" % _h: ("sbuf", [128, 128], "uint16"), "L2%d" % _h: ("sbuf", [128, 128], "uint16"),
-        "SW%d" % _h: ("sbuf", [128, WC], "float32"), "CW%d" % _h: ("sbuf", [128, WC], "float32"),
-        "HF%d" % _h: ("sbuf", [128, 32], "float32"), "HE%d" % _h: ("sbuf", [128, 32], "uint16"),
-        "CP0%d" % _h: ("sbuf", [128, W], "bfloat16"), "CP1%d" % _h: ("sbuf", [128, W], "bfloat16"),
-        "YS%d" % _h: ("sbuf", [128, W], "bfloat16"), "CA%d" % _h: ("sbuf", [128, 256], "bfloat16"),
-        "DF%d" % _h: ("sbuf", [128, W], "float32"), "DW%d" % _h: ("sbuf", [128, W], "bfloat16"),
+        "R%d" % _h: ("sbuf", [128, 144], "bfloat16"), "PM%d" % _h: ("sbuf", [128, 144], "bfloat16"),
+        "SI%d" % _h: ("sbuf", [128, 256], "int32"),
+        "LP%d" % _h: ("sbuf", [128, 128], "uint16"), "HE%d" % _h: ("sbuf", [128, 32], "uint16"),
+        "YS%d" % _h: ("sbuf", [128, W], "bfloat16"), "YR%d" % _h: ("sbuf", [128, W], "bfloat16"), "CY%d" % _h: ("sbuf", [128, 256], "bfloat16"),
+        "SX%d" % _h: ("sbuf", [128, 4, 32], "bfloat16"), "SL%d" % _h: ("sbuf", [128, 128], "uint16"),
+        "YL%d" % _h: ("sbuf", [128, H], "bfloat16"), "CK%d" % _h: ("sbuf", [128, 256], "bfloat16"),
+        "XF%d" % _h: ("sbuf", [128, H], "float32"),
         "TB%d" % _h: ("sbuf", [128, 512], "bfloat16"), "LD%d" % _h: ("sbuf", [128, 3, 256], "bfloat16"),
-        "Q%d0" % _h: ("psum", [128, 512], "float32"), "Q%d1" % _h: ("psum", [128, 512], "float32"),
+        "M%d" % _h: ("psum", [128, 16, 32], "float32"), "QB%d" % _h: ("psum", [128, 256, 2], "float32"),
     })
-SEMAPHORES = ["sv", "ss", "sp", "sg", "dsa", "dsb", "dw", "dxa", "dxb", "dxf", "dsj", "dfill", "dz0", "dz1", "dout",
-              "arr0", "arr1", "sent0", "sent1"]
+    if OPT["pos"][_h] == "t":
+        SCRATCH.update({
+            "X%d" % _h: ("sbuf", [128, 16, 128], "bfloat16"),
+            "DI%d" % _h: ("sbuf", [128, 128], "int32"), "DB%d" % _h: ("sbuf", [128, 8, 32], "bfloat16"),
+            "LK%d" % _h: ("sbuf", [128, 128], "uint16"),
+            "TL": ("sbuf", [128, 2, 384], "bfloat16"), "OH": ("sbuf", [128, 16, 16, 32], "bfloat16"),
+            "PH%d" % _h: ("sbuf", [128, 2, 256], "float16"), "TT%d" % _h: ("sbuf", [128, H], "float32"),
+            "G2%d" % _h: ("sbuf", [128, H], "float16"),
+            "EA%d" % _h: ("sbuf", [128, 64, 32], "bfloat16"), "EQ%d" % _h: ("sbuf", [128, 64, 32], "bfloat16"),
+            "XE%d" % _h: ("sbuf", [128, 128], "float16"), "XT%d" % _h: ("sbuf", [128, 4, 32], "float16"),
+            "TU%d" % _h: ("sbuf", [128, 512], "float32"), "PQ%d" % _h: ("sbuf", [128, 16, 32], "float32" if WIDE else "float16"),
+            "HQ%d" % _h: ("sbuf", [128, 24, 2], "float16"), "NR%d" % _h: ("sbuf", [128, 128], "bfloat16"), "LN%d" % _h: ("sbuf", [128, 128], "uint16"),
+            "D%d" % _h: ("psum", [128, 16, 32], "float32"), "QA%d" % _h: ("psum", [128, 16, 32], "float32"),
+        })
+    else:
+        SCRATCH.update({
+            "X%d" % _h: ("sbuf", [128, H], "bfloat16"), "DI%d" % _h: ("sbuf", [128, 512], "int32"), "DB%d" % _h: ("sbuf", [128, 512], "bfloat16"),
+            "IH%d" % _h: ("sbuf", [128, H], "bfloat16"), "IL%d" % _h: ("sbuf", [128, H], "float32"),
+            "TO%d" % _h: ("sbuf", [128, 4], "float32"), "BS%d" % _h: ("sbuf", [128, 4], "float32"), "BL%d" % _h: ("sbuf", [128, 2], "uint16"),
+            "CU%d" % _h: ("sbuf", [128, H], "float16"), "PR%d" % _h: ("sbuf", [128, H], "float16"), "L1%d" % _h: ("sbuf", [128, 128], "uint16"),
+            "SW%d" % _h: ("sbuf", [128, WC], "float32"), "SV%d" % _h: ("sbuf", [128, WC], "float32"), "CW%d" % _h: ("sbuf", [128, WC], "float32"),
+            "HF%d" % _h: ("sbuf", [128, 32], "float32"), "SK%d" % _h: ("sbuf", [128, 128], "int32"),
+            "PX%d" % _h: ("psum", [128, 1024], "float32"),
+        })
+    for _l in range(2):
+        SCRATCH["WN0%d" % _h] = ("sbuf", [128, W], "float32" if OPT["put"][0][_h] == "s" else "bfloat16")
+        SCRATCH["CP%d%d" % (_l, _h)] = ("sbuf", [128, W], "bfloat16")
+SEMAPHORES = ["sv", "ss", "sp", "sg", "dsa", "dsb", "dw", "dxa", "dxb", "dxf00", "dxf02", "dxf10", "dxf12", "dout", "arr0", "arr1", "sent0", "sent1",
+              "arrA", "sentA", "dneg", "dsj0", "dsj1", "dz00", "dz01", "dz10", "dz11"]
+SEMAPHORES += ["f%s%d%d" % (_k, _l, _h) for _k in ("WN", "CP") for _l in range(2) for _h in range(2)]
+BANKS = [_k for _k in SCRATCH if SCRATCH[_k][0] == "psum"]
 
 
-def rank_program(g, core, T, topo):
-    rank = T.rank_of(core)
-    if rank is None:
-        return
+def polish(order, fixed, queue, before, users, busy, tail, moves):
+    N, L = len(busy), len(order)
+    preds, succs = [set(d for d, x in b) for b in before], [set(u for u, x in b) for b in users]
+    seed = [OPT["seed"]]
+
+    def draw():
+        seed[0] = (seed[0] * 1103515245 + 12345) % 2147483648
+        return seed[0] / 2147483648.0
+
+    names = sorted(set(queue))
+    queue = [-1 if q == "x" else names.index(q) for q in queue]
+    cases = []
+    for slow in (1.0, OPT["slow"]):
+        b, rest = [x * slow if names[q] == "p" and q >= 0 else x for x, q in zip(busy, queue)], [0.0] * N
+        for i in range(N - 1, -1, -1):
+            rest[i] = max([tail[i]] + [x + b[u] + rest[u] for u, x in users[i]])
+        cases.append((b, rest))
+    ends = [i for i in order if not users[i] or tail[i] >= 0.0 > min(tail)]
+    mix = OPT["mix"]
+
+    def both(order, lo, old, limit):
+        a = length(order, lo, old[0][2], old[0][3], (limit - mix * 0.98 * old[1][0]) / (1 - mix), *cases[0])
+        b = a and (length(order, lo, old[1][2], old[1][3], (limit - (1 - mix) * a[0]) / mix, *cases[1]) if mix else a)
+        return b and (a, b)
+
+    def length(order, lo, fin, cause, limit, busy, rest):
+        fin, cause, last = fin[:], cause[:], [-1] * (len(names) + 1)
+        for i in order[:lo]:
+            last[queue[i]] = i
+        for i in order[lo:]:
+            t, c, q = 0.0, -1, queue[i]
+            for d, x in before[i]:
+                if fin[d] + x > t:
+                    t, c = fin[d] + x, d
+            if q >= 0:
+                j = last[q]
+                if j >= 0 and fin[j] > t:
+                    t, c = fin[j], -2 - j
+                last[q] = i
+            t += busy[i]
+            if t + rest[i] > limit:
+                return None
+            fin[i], cause[i] = t, c
+        e = max(ends, key=lambda i: fin[i] + tail[i])
+        end, pairs = fin[e] + tail[e], []
+        while e >= 0:
+            c = cause[e]
+            if c <= -2:
+                c = -2 - c
+                pairs.append((c, e))
+            e = c
+        return end, pairs, fin, cause
+
+    held = both(order, 0, [(0.0, [], [0.0] * N, [-1] * N)] * 2, 1e18)
+    now = (1 - mix) * held[0][0] + mix * held[1][0]
+    best, pos = (now, order), {v: j for j, v in enumerate(order)}
+    for k in range(moves):
+        pairs = held[k % 2][1]
+        if pairs and draw() < 0.7:
+            a, b = pairs[int(draw() * len(pairs))]
+            far = (0, 0, 0, 3, 10, 30)[int(draw() * 6)]
+            v, to = (b, pos[a] - far) if draw() < 0.5 else (a, pos[b] + far)
+        else:
+            v = order[fixed + int(draw() * (L - fixed))]
+            to = pos[v] + int((draw() + draw() - 1.0) * 60)
+        to, p = max(fixed, min(L - 1, to)), pos[v]
+        if p < fixed:
+            continue
+        lo, hi = min(to, p), max(to, p) + 1
+        part, need = order[lo:hi], {v}
+        for u in (reversed(part) if to < p else part):
+            if u in need:
+                need |= (preds if to < p else succs)[u]
+        go, stay = [u for u in part if u in need], [u for u in part if u not in need]
+        part = go + stay if to < p else stay + go
+        new = order[:lo] + part + order[hi:]
+        got = both(new, lo, held, now - math.log(draw() + 1e-9) * (OPT["heat"] * (1.0 - k / moves) ** 2 + 2.0))
+        if got:
+            order, held = new, got
+            now = (1 - mix) * held[0][0] + mix * held[1][0]
+            for j, u in enumerate(part):
+                pos[u] = lo + j
+            if now < best[0]:
+                best = (now, order)
+    return best[1]
+
+
+def collect(g, T, topo, rank):
     n = len(T.cores)
+    tag, names, step = [""], {}, [1e9]
+
+    def at(name, l, h):
+        step[0] = 100 * l + OPT["steps"].index((name, h))
     O = OPT
     Q = {"v": g.vector, "s": g.scalar, "p": g.tensor, "g": g, "y": g.sync}
     V, S, P = g.vector, g.scalar, g.tensor
-    calls, names = [], {}
+    calls = []
     wr, rd = {}, {}
+    cnt = {}
 
     def add(q, r, w, busy, lag, emit, soft=()):
         deps = set()
-        for k in r:
-            if k in wr:
+        turns = [k for k in w if k[0] == "~"]
+        soft = list(soft) + [(k, 0.0) for k in turns if k in wr]
+        w = [k for k in w if k not in turns]
+        for k in list(r) + list(w):
+            if k in wr and k in w and calls[wr[k]]["q"] == q and (k in BANKS or k in O["free"]):
+                soft.append((k, 0.0))
+            elif k in wr:
                 deps.add(wr[k])
         for k in w:
-            if k in wr:
-                deps.add(wr[k])
             deps.update(rd.get(k, []))
         me = len(calls)
-        nm = q + (w or r)[-1]
+        nm = tag[0] + q + (w or r)[-1]
         names[nm] = names.get(nm, -1) + 1
-        calls.append({"name": "%s.%d" % (nm, names[nm]), "q": q, "deps": deps, "busy": busy, "lag": lag, "emit": emit,
-                      "soft": [(wr[k], d) for k, d in soft]})
+        calls.append({"name": "%s.%d" % (nm, names[nm]), "step": step[0], "q": q, "deps": deps, "busy": busy, "lag": lag, "emit": emit, "soft": [(wr[k], d) for k, d in soft]})
         for k in r:
             rd.setdefault(k, []).append(me)
-        for k in w:
+        for k in w + turns:
             wr[k] = me
             rd[k] = []
-
-    cnt = {}
 
     def op(q, r, w, els, fn):
         def emit():
@@ -111,7 +220,7 @@ def rank_program(g, core, T, topo):
             fn().then_inc(T.sem[s], 1)
             cnt[s] = cnt.get(s, 0) + 1
             return (s, cnt[s])
-        add(q, r, w, els * O["pe"] if q == "p" else 55 + 0.83 * max(64, els), 0, emit)
+        add(q, r, w, els * O["pe"] if q == "p" else {"v": 55, "s": 65, "g": 150}[q] + 0.83 * max(64, els), O["hop"], emit)
 
     def dmas(q, s, r, w, pairs, lag):
         def emit():
@@ -121,202 +230,419 @@ def rank_program(g, core, T, topo):
             return (s, cnt[s])
         add(q, r, w, 60 * len(pairs), lag, emit)
 
+    def mm(r, w, cycles, triples):
+        def run():
+            for grp in triples:
+                for i, (o, a, b) in enumerate(grp):
+                    m = P.matmul(o, a, b, i == 0, i == len(grp) - 1)
+            return m
+        op("p", r, w, cycles, run)
+
+    def mm_part(r, w, cycles, grp, start, stop):
+        def run():
+            for i, (o, a, b) in enumerate(grp):
+                m = P.matmul(o, a, b, start and i == 0, i >= len(grp) - int(stop))
+            return m
+        op("p", r, w, cycles, run)
+
     sig, gam = O["sig"], O["gam"]
 
-    dmas("y", "dsa", [], ["SI0"], [(T.SI0[64 * f:64 * f + 64, :], T.slot[:, 0:H]) for f in range(2)], 2300)
-    dmas("s", "dsb", [], ["SI1"], [(T.SI1[64 * f:64 * f + 64, :], T.slot[:, H:2 * H]) for f in range(2)], 2300)
-    dmas("y", "dxa", [], ["X0"], [(T.X[:, 0:H], T.x[:, 0:H])], 4500)
-    dmas("y", "dxb", [], ["X1"], [(T.X[:, H:2 * H], T.x[:, H:2 * H])], 6000)
+    for h in range(2):
+        si, src = T["SI%d" % h], T.slot[:, H * h:H * h + H]
+        dmas("ys"[h], "ds" + "ab"[h], [], ["SI%d" % h],
+             [(si[:, 0:128], src)] if O["pos"][h] == "t" else [(si[64 * f:64 * f + 64, :], src) for f in range(2)], 2300)
+    dmas("y", "dxa", [], ["X0"], [(T.X0[:], T.x[:, 0:H])], 4500)
+    dmas("y", "dxb", [], ["X1"], [(T.X1[:], T.x[:, H:2 * H])], 6000)
     dmas("y", "dw", [], ["wc"], [(T.wc[:, 0:1], T.w[:])], 2500)
-    dmas("y", "dsj", [], ["SJ"], [(T.SJ[:, 16 * j:16 * j + 16], T.slot[j, H:2 * H]) for j in range(8)], 4000)
 
     fl = {"allow_small_or_imprecise_dtypes": True}
-    op("g", [], ["p0"], 100, lambda: g.iota(T.p0[:, 0:1], [[0, 1]], 0, 1))
-    op("g", [], ["JJ"], 350, lambda: g.iota(T.JJ[:], [[8, 8], [0, 16]], 0, 0, **fl))
-    op("g", [], ["DD"], 350, lambda: g.iota(T.DD[:], [[0, 8], [1, 16]], 0, 0, **fl))
-    op("g", [], ["IC"], 380, lambda: g.iota(T.IC[:], [[1, 144]], 0, 0, **fl))
-    op("g", [], ["M8"], 110, lambda: g.iota(T.M8[:], [[1, 8]], 0, 0, **fl))
-    op("g", [], ["I64"], 480, lambda: g.iota(T.I64[:], [[0, 3], [1, 64]], 0, 0, **fl))
-    op("g", [], ["HC"], 160, lambda: g.iota(T.HC[:], [[0, 2], [1, 16]], int(CEN), 0, **fl))
-    op("v", [], ["CO1"], 128, lambda: V.memset(T.CO[64:128, :], -1.0))
-    op("g", [], ["mB"], 100 + 2 * PF, lambda: g.iota(T.mB[:], [[0, PF]], int(NEUT), 0, **fl))
-    op("g", [], ["mF"], 100 + 2 * PF, lambda: g.iota(T.mF[:], [[0, PF]], -1, 0, **fl))
-    op("g", [], ["mZ"], 100 + 2 * WC // 3, lambda: g.iota(T.mZ[:], [[0, WC // 3]], 0, 0, **fl))
-    fills, fk = [], ["fill", "DW0", "DW1", "DF0", "DF1"]
-    caps = [h for h in range(2) if O["capA" if h == 0 else "capB"] == "x"]
-    if caps:
-        op("g", [], ["mC"], 100 + 2 * PF, lambda: g.iota(T.mC[:], [[0, PF]], 512, 0, **fl))
-    for j in range(3):
-        c = slice(PF * j, PF * j + PF)
-        fills += [(T.NEG[:, c], T.mB[:]), (T.DW0[:, c], T.mB[:]), (T.DF0[:, c], T.mF[:]), (T.DW1[:, c], T.mB[:]), (T.DF1[:, c], T.mF[:])]
-        fills += [(T["CP%d%d" % (l, h)][:, c], T.mC[:]) for l in range(2) for h in caps]
-    fk += ["CP%d%d%d" % (l, h, q) for l in range(2) for h in caps for q in range(2)]
-    dmas("y", "dfill", ["mB", "mF", "mC"], fk, fills, 6000)
+
+    def iota(k, o, els, pattern, base, cm=0):
+        op("g", [], [k], 2 * els, lambda: g.iota(o, pattern, base, cm, **fl))
+    op("g", [], ["p0"], 1, lambda: g.iota(T.p0[:, 0:1], [[0, 1]], 0, 1))
+    iota("IC", T.IC[:], 144, [[1, 144]], 0)
+    iota("KEY", T.KEY[:], 128, [[64, 4], [1, 16], [32, 2]], 0)
+    iota("JG", T.JG[:], 128, [[16, 8], [0, 16]], 15)
+    iota("ZR", T.ZR[:], NZ, [[0, NZ]], 0)
+    iota("mB", T.mB[:], 256, [[0, 256]], -1)
+    iota("mF", T.mF[:], 384, [[0, 384]], -1)
+    iota("mC", T.mC[:], PF, [[0, PF]], 1)
+    op("g", ["mC"], ["HD"], 512, lambda: g.affine_select(T.HD[:], T.mC[:, 0:256], [[0, 16], [1, 16]], A.is_equal, 0.0, 0, 0))
+    for q in range(0, NST, 256):
+        op("g", ["mC"], ["ST"], 512, lambda q=q: g.affine_select(T.ST[:, q:q + 256], T.mC[:, 0:256], [[0, 256]], A.is_gt, SC, 0, 0))
+    dmas("y", "dneg", ["ZR", "SI0"], ["U2"], [(T.U2[:, 2 * j:2 * j + 2, :], T.ZR[:]) for j in range(4)], O["dl"] * 2500)
+    iota("JJ", T.JJ[:], 128, [[8, 8], [0, 16]], 0)
+    iota("DD", T.DD[:], 128, [[0, 8], [1, 16]], 0)
+    iota("M8", T.M8[:], 8, [[1, 8]], 0)
+    iota("I64", T.I64[:], 192, [[0, 3], [1, 64]], 0)
+    iota("JH", T.JH[:], 128, [[0, 2], [8, 8], [0, 8]], 7)
+    iota("HR", T.HR[:], 32, [[0, 2], [1, 16]], int(CEN))
+    iota("mZ", T.mZ[:], WC // 3, [[0, WC // 3]], 0)
+    iota("mN", T.mN[:], 512, [[0, 512]], -2048)
+    dmas("y", "dneg", ["mN", "X0"], ["NEG"], [(T.NEG[:, 512 * j:512 * j + 512], T.mN[:]) for j in range(4)], 3500)
+
+    def fill(l, h, after):
+        k, m = "WN%d%d" % (l, h), "mF" if O["put"][l][h] == "s" else "mB"
+        if l == 0:
+            if h:
+                dmas("y", "f" + k, ["mF"] + after, [k], [(T[k][:, 384 * j:384 * j + 384], T.mF[:]) for j in range(6)], O["dl"] * 4000)
+            for q in range(2 - 2 * h):
+                iota(k, T[k][:, HW * q:HW * q + HW], HW, [[0, HW]], -1)
+        if O["cap"][l][h] == "x":
+            k = "CP%d%d" % (l, h)
+            dmas("y", "f" + k, ["mC"] + after, [k + "0", k + "1", "~cap"], [(T[k][:, PF * j:PF * j + PF], T.mC[:]) for j in range(3)], O["dl"] * 3500)
+    fill(0, 0, ["X1"]); fill(0, 1, ["X1"])
+
+    masks = [127, 15] + [16, 1, 30, 96] * ("t" in O["pos"]) + [7, 56] * ("r" in O["pos"])
 
     def low_bits(j, m):
         op("v", ["p0"], ["pI%d" % j], 1, lambda: V.tensor_scalar(T.pI[:, j:j + 1], T.p0[:, 0:1], m, None, A.bitwise_and))
-    for j, m in enumerate((56, 7, 15, 127)):
+    for j, m in enumerate(masks):
         low_bits(j, m)
-    op("v", ["pI0", "pI1", "pI2", "pI3"], ["pF"], 1, lambda: V.tensor_copy(T.pF[:, 0:4], T.pI[:, 0:4]))
-    p56, p7, pd, pp = (T.pF[:, j:j + 1] for j in range(4))
-    dsq, b1, b16, c2, d16, zc, zh = (T.pF[:, j:j + 1] for j in range(4, 11))
+    nm = len(masks)
+    op("v", ["pI%d" % j for j in range(nm)], ["pF"], 1, lambda: V.tensor_copy(T.pF[:, 0:nm], T.pI[:, 0:nm]))
+    pp, p15, p16, p1, p30, p96, p7, p56 = (T.pF[:, masks.index(m):masks.index(m) + 1] if m in masks else None for m in (127, 15, 16, 1, 30, 96, 7, 56))
+    col = {}
+
+    def column(k, r, a, s1, s2, o0, o1):
+        c = col[k] = T.pF[:, 8 + len(col):9 + len(col)]
+        op("v", ["pF"] + r, [k], 1, lambda: V.tensor_scalar(c, a, s1, s2, o0, o1))
+    column("odd", [], p16, 0.0625, 0.0, A.mult, A.add)
+    column("even", [], p16, -0.0625, 1.0, A.mult, A.add)
+    column("zc", [], pp, p15, 15.0, A.subtract, A.add)
+    column("c1", [], pp, p16, 16.0, A.subtract, A.add)
+    column("n1", [], p1, -1.0, 1.0, A.mult, A.add)
+    column("d0", [], p30, 0.5, p96, A.mult, A.add)
+    column("dest", ["d0"], p1, 16.0, col["d0"], A.mult, A.add)
+    column("klo", [], p30, 0.5, 0.0, A.mult, A.add)
+    column("k1", [], p1, 16.0, p96, A.mult, A.add)
+    column("k0", ["k1"], col["k1"], 2.0, 0.0, A.mult, A.add)
+    column("t0", [], p15, 15.0, 2304.0, A.is_equal, A.mult)
+    column("t1", [], pp, 127.0, -1151.0, A.is_equal, A.mult)
+
+    def match(k, o, src, sk, c, ck, mul, mk):
+        op("v", [sk, ck] + mk, [k], 144, lambda: V.tensor_scalar(o, src, c, mul, A.is_equal, A.mult))
+    match("ID", T.ID[:], T.IC[:, 0:128], "IC", pp, "pF", 1.0, [])
+    op("s", ["ID"], ["NID"], 128, lambda: S.activation(T.NID[:], T.ID[:], F.Identity, scale=-1.0))
+    op("s", ["ID"], ["N16"], 128, lambda: S.activation(T.N16[:], T.ID[:], F.Identity, scale=-16.0))
+    iota("I2", T.I2[:], 256, [[0, 256]], 1)
+    op("g", [], ["I2"], 512, lambda: g.affine_select(T.I2[:], T.I2[:], [[32, 4], [0, 2], [1, 32]], A.is_equal, 0.0, 0, -1))
+    for b in range(4):
+        for d in range(4 * b, 4 * b + 4):
+            op("s", ["I2"], ["CT%d" % d], 128, lambda d=d: S.activation(T.CS[:, 128 * d:128 * d + 128], T.I2[:, :, d + 1:d + 33], F.Identity))
+        o = T.CS[:, 512 * b:512 * b + 512]
+        op("g", ["CT%d" % d for d in range(4 * b, 4 * b + 4)], ["CS%d" % b], 1024,
+           lambda o=o: g.affine_select(o, o, [[0, 4], [1, 128]], A.not_equal, -1.0, 0, -1))
+    for q in range(2):
+        r, pm = T["R%d" % q], T["PM%d" % q]
+        iota("R%da" % q, r[:, 0:16], 16, [[0, 16]], 0)
+        op("g", ["mC", "R%da" % q], ["R%d" % q], 256, lambda r=r, q=q: g.affine_select(
+            r[:, 16:144], T.mC[:, 0:128], [[-32, 4], [-1000, 2], [-1, 16]], A.is_equal, 0.0, -16 * q, 1))
+        iota("PM%da" % q, pm[:, 128:144], 16, [[0, 16]], 0)
+        op("g", ["mC", "PM%da" % q], ["PM%d" % q], 256, lambda pm=pm, q=q: g.affine_select(
+            pm[:, 0:128], T.mC[:, 0:128], [[-32, 4], [1000, 2], [-2, 16]], A.is_equal, 0.0, -1001 * q, 1))
+    op("v", ["KEY", "klo", "k0"], ["TA"], 128, lambda: V.tensor_scalar(T.TA[:], T.KEY[:], col["k0"], col["klo"], A.subtract, A.is_gt))
+    op("v", ["KEY", "k0"], ["TR"], 128, lambda: V.tensor_scalar(T.TR[:], T.KEY[:], col["k0"], 15.0, A.subtract, A.is_le))
+    op("v", ["TA", "TR"], ["TQ"], 256, lambda: V.tensor_tensor(T.TQ[:], T.TR[:], T.TA[:], A.mult))
+    op("g", [], ["HD"], 1, lambda: g.iota(T.HD[:, 0:1], [[0, 1]], -1024, 0, **fl))
+    column("kc", [], p30, 512.5, 1.0 - CEN, A.mult, A.add)
+    op("v", [], ["HC0"], 1, lambda: V.memset(T.HC[:, 0:16], -1.0))
+    op("v", [], ["HC1"], 1, lambda: V.memset(T.HC[:, 16:31], -2.0))
+    op("v", ["t0", "t1"], ["HC2"], 1, lambda: V.tensor_scalar(T.HC[:, 31:32], col["t0"], col["t1"], -2.0, A.add, A.add))
+    op("s", ["wc"], ["ws0"], 1, lambda: S.activation(T.ws[:, 0:1], T.wc[:, 0:1], F.Identity, scale=1.0 / SC))
+    op("s", ["wc"], ["ws1"], 1, lambda: S.activation(T.ws[:, 1:2], T.wc[:, 0:1], F.Identity, scale=-1.0 / SC))
+    match("ZW", T.ZW[:], T.IC[:], "IC", col["zc"], "zc", T.ws[:, 0:1], ["ws0"])
+    match("GW", T.GW[:], T.JG[:], "JG", col["zc"], "zc", T.ws[:, 1:2], ["ws1"])
+    for u in ("U2",):
+        op("s", ["ID"], [u], 128, lambda u=u: S.activation(T[u][:, :, 0:256:17], T.ID[:], F.Identity))
+    op("v", [], ["CO1"], 128, lambda: V.memset(T.CO[64:128, :], -1.0))
     op("v", ["DD"], ["CO0"], 128, lambda: V.tensor_scalar(T.CO[0:64, :], T.DD[0:64, :], 2.0, None, A.mult))
     op("v", ["JJ", "pF"], ["EB"], 128, lambda: V.tensor_scalar(T.EB[:], T.JJ[:], p56, None, A.is_equal))
     op("v", ["M8", "pF"], ["M8"], 8, lambda: V.tensor_scalar(T.M8[:], T.M8[:], p7, None, A.is_equal))
     op("v", ["EB", "CO0", "CO1"], ["EB"], 256, lambda: V.tensor_tensor(T.EB[:], T.EB[:], T.CO[:], A.mult))
-    op("v", ["pF"], ["dsq"], 1, lambda: V.tensor_scalar(dsq, pd, pd, None, A.mult))
-    op("v", ["dsq"], ["b1"], 1, lambda: V.tensor_scalar(b1, dsq, -1.0, 1.0, A.mult, A.add))
-    op("v", ["pF"], ["zc"], 1, lambda: V.tensor_scalar(zc, pp, pd, 15.0, A.subtract, A.add))
-    op("v", ["IC", "pF"], ["TA"], 128, lambda: V.tensor_scalar(T.TA[:], T.IC[:, 0:128], pp, None, A.is_gt))
-    op("v", ["IC", "zc"], ["TR"], 128, lambda: V.tensor_scalar(T.TR[:], T.IC[:, 0:128], zc, None, A.is_le))
-    op("v", ["TA", "TR"], ["TR"], 256, lambda: V.tensor_tensor(T.TR[:], T.TR[:], T.TA[:], A.mult))
-    op("v", ["dsq"], ["b16"], 1, lambda: V.tensor_scalar(b16, dsq, -16.0, 16.0, A.mult, A.add))
-    op("v", ["pF"], ["c2"], 1, lambda: V.tensor_scalar(c2, pd, 16.0, -CEN, A.mult, A.add))
-    op("v", ["pF"], ["d16"], 1, lambda: V.tensor_scalar(d16, pd, 16.0, None, A.mult))
-    op("v", ["zc"], ["zh"], 1, lambda: V.tensor_scalar(zh, zc, 0.5, -0.5, A.mult, A.add))
-    op("v", ["IC", "zc"], ["Z"], 144, lambda: V.tensor_scalar(T.Z[:], T.IC[:], zc, None, A.is_equal))
-    op("v", ["IC", "zc", "d16"], ["ZD"], 144, lambda: V.tensor_scalar(T.ZD[:], T.IC[:], zc, d16, A.is_equal, A.mult))
-    op("v", ["wc"], ["ws"], 1, lambda: V.tensor_scalar(T.ws[:, 0:1], T.wc[:, 0:1], 1.0 / SC, None, A.mult))
-    op("v", ["I64", "zh", "ws"], ["ZH0"], 192, lambda: V.tensor_scalar(T.ZH0[:], T.I64[:], zh, T.ws[:, 0:1], A.is_equal, A.mult))
-    op("v", ["I64", "zh", "wc"], ["ZH1"], 192, lambda: V.tensor_scalar(T.ZH1[:], T.I64[:], zh, T.wc[:, 0:1], A.is_equal, A.mult))
-    op("v", ["IC", "pF"], ["ID"], 128, lambda: V.tensor_scalar(T.ID[:], T.IC[:, 0:128], pp, None, A.is_equal))
-    op("v", ["IC", "zc", "wc"], ["ZW"], 144, lambda: V.tensor_scalar(T.ZW[:], T.IC[:], zc, T.wc[:, 0:1], A.is_equal, A.mult))
-
-    def slot_list(l):
-        if l == 0:
-            op("v", ["SJ"], ["SB"], 128, lambda: V.tensor_copy(T.SB[:], T.SJ[:]))
-            op("p", ["SB", "ID"], ["Q11"], 128, lambda: P.matmul(T.Q11[:, 0:128], T.SB[:], T.ID[:], True, True))
-            op("v", [], ["Q11", "SL"], 128, lambda: V.tensor_copy(T.SL[:], T.Q11[:, 0:128]))
-            return
-
-        def run():
-            for r in range(16):
-                m = P.matmul(T.Q11[:, 0:128], T.ZW[:, 15 - r:143 - r], T.Y0[:, H + r:2 * H:16], r == 0, r == 15)
-            return m
-        op("p", ["ZW"] + ["Y0%d" % j for j in range(4, 8)], ["Q11"], 2048, run)
-        op("v", [], ["Q11", "SJ"], 128, lambda: V.tensor_copy(T.SJ[:], T.Q11[:, 0:128]))
-        op("v", ["SJ"], ["SJ"], 128, lambda: V.tensor_scalar(T.SJ[:], T.SJ[:], 255, None, A.bitwise_and))
-        op("v", ["SJ"], ["SL"], 128, lambda: V.tensor_copy(T.SL[:], T.SJ[:]))
-
-    def spread(i):
-        o = T.EE[:, 128 * i:128 * i + 128]
-        if i % 2:
-            op("s", ["EB", "M8"], ["EE%d" % i], 128, lambda: S.activation(o, T.EB[:], F.Identity, scale=T.M8[:, i:i + 1]))
-        else:
-            op("v", ["EB", "M8"], ["EE%d" % i], 128, lambda: V.tensor_scalar(o, T.EB[:], T.M8[:, i:i + 1], None, A.mult))
     for i in range(8):
-        spread(i)
-
-    def digit(h, d):
-        di, db = T["DI%d" % h][:, 256 * d:256 * d + 256], T["DB%d" % h]
-        k = "%d%d" % (h, d)
-        if d == 0:
-            op("v", ["SI%d" % h], ["DI" + k], 256, lambda: V.tensor_scalar(di, T["SI%d" % h][:], 4, 15, A.arith_shift_right, A.bitwise_and))
+        o, m = T.EE[:, 128 * i:128 * i + 128], T.M8[:, i:i + 1]
+        if i % 2:
+            op("s", ["EB", "M8"], ["EE%d" % i], 128, lambda o=o, m=m: S.activation(o, T.EB[:], F.Identity, scale=m))
         else:
-            op("v", ["SI%d" % h], ["DI" + k], 256, lambda: V.tensor_scalar(di, T["SI%d" % h][:], 15, None, A.bitwise_and))
-        op("v", ["DI" + k], ["DB" + k], 256, lambda: V.tensor_copy(db[:, 256 * d:256 * d + 256], di))
-        u = db[64:128, 256 * d:256 * d + 256]
-        op("s", ["DB" + k], ["DB" + k], 256, lambda: S.activation(u, u, F.Square))
+            op("v", ["EB", "M8"], ["EE%d" % i], 128, lambda o=o, m=m: V.tensor_scalar(o, T.EB[:], m, None, A.mult))
+    column("dsq", [], p15, p15, -1.0, A.mult, A.mult)
+    column("b1", ["dsq"], col["dsq"], 1.0, 1.0, A.mult, A.add)
+    column("b16", ["dsq"], col["dsq"], 16.0, 16.0, A.mult, A.add)
+    column("c2", [], p15, 16.0, -CEN, A.mult, A.add)
+    column("d16", [], p15, 16.0, 0.0, A.mult, A.add)
+    column("zh", ["zc"], col["zc"], 0.5, -0.5, A.mult, A.add)
+    op("v", ["IC", "pF"], ["TC"], 128, lambda: V.tensor_scalar(T.TC[:], T.IC[:, 0:128], pp, None, A.is_gt))
+    op("v", ["IC", "zc"], ["TS"], 128, lambda: V.tensor_scalar(T.TS[:], T.IC[:, 0:128], col["zc"], None, A.is_le))
+    op("v", ["TC", "TS"], ["TS"], 256, lambda: V.tensor_tensor(T.TS[:], T.TS[:], T.TC[:], A.mult))
+    match("Z", T.Z[:], T.IC[:], "IC", col["zc"], "zc", 1.0, [])
+    match("ZD", T.ZD[:], T.IC[:], "IC", col["zc"], "zc", col["d16"], ["d16"])
+    match("ZH", T.ZH[:], T.I64[:], "I64", col["zh"], "zh", T.ws[:, 0:1], ["ws0"])
+    match("GH", T.GH[:], T.JH[:], "JH", col["zh"], "zh", T.ws[:, 1:2], ["ws1"])
 
-    def indicate(h, d, q):
-        px = T["PX%d" % q]
+    def front(l, h):
+        M, mk = T["M%d" % h], "M%d" % h
+        si, di, db, lk = (T["%s%d" % (k, h)] for k in ("SI", "DI", "DB", "LK"))
 
-        def run():
-            for j in range(4):
-                i = 4 * q + j
-                m = P.matmul(px[:, 256 * j:256 * j + 256], T.EE[:, 128 * i:128 * i + 128],
-                             T["DB%d" % h][:, 256 * d:256 * d + 256], True, True)
-            return m
-        op("p", ["DB%d%d" % (h, d)] + ["EE%d" % (4 * q + j) for j in range(4)], ["PX%d" % q], 1024, run)
-        o = T[("IH%d", "IL%d")[d] % h][:, 1024 * q:1024 * q + 1024]
-        c = 2 * d + q
-        op("s", [("b1", "b16")[d]], ["PX%d" % q, "I%d%d%d" % (d, h, q), "TO%d%d" % (h, c)], 1050,
-           lambda: S.activation(o, px[:], F.Relu, bias=(b1, b16)[d], scale=(1.0, 16.0)[d], accum_out=T["TO%d" % h][:, c:c + 1]))
+        def K(s):
+            return "%s%d" % (s, h)
 
-    def base(h, d):
-        op("p", ["TR", "TO%d%d" % (h, 2 * d), "TO%d%d" % (h, 2 * d + 1)], ["Q%d1" % h], 256,
-           lambda: P.matmul(T["Q%d1" % h][:, 0:2], T.TR[:], T["TO%d" % h][:, 2 * d:2 * d + 2], True, True))
-        op("v", [], ["Q%d1" % h, "BS%d%d" % (h, 2 * d)], 2,
-           lambda: V.tensor_reduce(T["BS%d" % h][:, 2 * d:2 * d + 1], T["Q%d1" % h][:, 0:2], AX.X, A.add))
-
-    def gather_mm(h, q, src, keys, z, zk, start, stop):
-        def run():
-            for r in range(16):
-                m = P.matmul(T["Q%d%d" % (h, q)][:, 0:64], z[:, 15 - r:143 - r], src[:, 1024 * q + r:1024 * q + 1024:16],
-                             start and r == 0, stop and r == 15)
-            return m
-        op("p", keys + [zk], ["Q%d%d" % (h, q)], 1024, run)
-
-    def to_list(h, q, name, mul, plus):
-        op("v", [], ["Q%d%d" % (h, q), "%s%d%d" % (name, h, q)], 64,
-           lambda: V.tensor_scalar(T["%s%d" % (name, h)][:, 64 * q:64 * q + 64], T["Q%d%d" % (h, q)][:, 0:64], mul, plus, A.mult, A.add))
-
-    def pass1(h):
-        bs, ih, cu, pr = T["BS%d" % h], T["IH%d" % h], T["CU%d" % h], T["PR%d" % h]
-        base(h, 0)
-        op("v", ["BS%d0" % h, "I0%d0" % h, "I0%d1" % h], ["CU%d" % h], 1024,
-           lambda: V.tensor_tensor_scan(cu[:], ih[:], ih[:], bs[:, 0:1], A.add, A.max))
-
-        def piece(q):
-            c = slice(1024 * q, 1024 * q + 1024)
-            op("v", ["CU%d" % h, "I0%d%d" % (h, q)], ["PR%d%d" % (h, q)], 512,
-               lambda: V.tensor_tensor_scan(pr[:, c], cu[:, c], ih[:, c], 0.0, A.max, A.mult))
-            gather_mm(h, q, pr, ["PR%d%d" % (h, q)], T.Z, "Z", True, True)
-            to_list(h, q, "L1", 1.0, 0.25)
-        piece(0); piece(1)
-
-    def span(name, h, a, b):
-        return ["%s%d%d" % (name, h, q) for q in range(a // 1024, (b + 1023) // 1024)]
-
-    def scatter1(e, h, a, b):
-        keys = span("I1", h, a, b) + span("L1", h, a, b)
-        sw = "SV0" if e == "v" else "SW%d" % h
-        o = T[sw][:, 0:H + 1].indirect(T["L1%d" % h][:, a // 16:b // 16])
-        i = T["IL%d" % h][:, a:b]
-        if e == "v":
-            op("v", keys, [sw], sig * (b - a), lambda: V.tensor_scalar(o, i, 0.0625, 0.0, A.mult, A.add))
+        at("front", l, h)
+        if l == 1:
+            for a in (0, 2):
+                grp = [(M[:, 0:4, :], T.GW[:], T.ST[:, 0:128])] if a == 0 else []
+                grp += [(M[:, a:a + 2, :], T.ZW[:, 15 - j:143 - j], T.Y0[:, 4 * h + a:4 * h + a + 2, 32 * j:32 * j + 32]) for j in range(16)]
+                mm_part(["ZW", "GW", "ST", "Y0%d%d" % (h, a), "Y0%d%d" % (h, a + 1)], [mk], 1024 + 128 * (a == 0), grp, a == 0, a == 2)
+            op("v", [], [mk, K("DI")], 128, lambda: V.tensor_copy(di[:], M[:, 0:4, :]))
+            op("v", [K("DI")], [K("SI")], 128, lambda: V.tensor_scalar(si[:, 0:128], di[:], 255, None, A.bitwise_and))
+            op("v", [K("DI")], [K("SJ")], 128, lambda: V.tensor_scalar(si[:, 128:256], di[:], 4, 15, A.arith_shift_right, A.bitwise_and))
         else:
-            op("s", keys, [sw], sig * (b - a), lambda: S.activation(o, i, F.Tanh))
+            op("v", [K("SI")], [K("SJ")], 128, lambda: V.tensor_scalar(si[:, 128:256], si[:, 0:128], 4, None, A.arith_shift_right))
+        op("v", [K("SI"), K("SJ")], [K("DS"), K("DH")], 256, lambda: V.tensor_copy(db[:], si[:]))
+        op("v", [K("DS"), "odd"], [K("LK")], 64, lambda: V.tensor_scalar(lk[:], db[:, 0:4, :], 2.0, col["odd"], A.mult, A.add))
+        mm([K("DS"), K("DH"), "ID", "N16"], [mk], 512,
+           [[(M[:, 8:12, :], db[:, 0:4, :], T.ID[:]), (M[:, 8:12, :], db[:, 4:8, :], T.N16[:])],
+            [(M[:, 12:16, :], db[:, 4:8, :], T.ID[:])], [(M[:, 4:8, :], db[:, 0:4, :], T.ID[:])]])
+        op("s", [], [mk, K("TL")], 384, lambda: S.activation(T.TL[:, h, :], M[:, 4:16, :], F.Identity))
+        a, b = (0, 2) if O["joint"][l] else (h, h + 1)
+        for d in range(16 * (b == h + 1)):
+            op("v", ["TL%d" % x for x in range(a, b)], ["OH%d_%d" % (d, x) for x in range(a, b)] + ["~oh"], 128 * (b - a),
+               lambda d=d: V.tensor_scalar(T.OH[:, 8 * a:8 * b, d, :], T.TL[:, a:b, 128:384], float(d), None, A.is_equal))
 
-    def pass2(h):
-        bs, cw, to = T["BS%d" % h], T["CW%d" % h], T["TO%d" % h]
-        base(h, 1)
-        op("v", ["BS%d2" % h, "c2"], ["CW%d" % h], 1, lambda: V.tensor_scalar(cw[:, 0:1], bs[:, 2:3], 0.0625, c2, A.mult, A.add))
-        op("v", ["BS%d0" % h, "TO%d0" % h, "TO%d1" % h], ["BS%d1" % h], 1,
-           lambda: V.tensor_scalar(bs[:, 1:2], bs[:, 0:1], to[:, 0:1], to[:, 1:2], A.add, A.add))
-        op("v", ["BS%d0" % h, "BS%d1" % h], ["BL%d" % h], 1, lambda: V.tensor_copy(T["BL%d" % h][:], bs[:, 0:2]))
+    def places(l, h):
+        M, D, QA, QB = (T["%s%d" % (k, h)] for k in ("M", "D", "QA", "QB"))
+        mk, dk, ak, bk = ("%s%d" % (k, h) for k in ("M", "D", "QA", "QB"))
+        db, lk, ph, tt, ea, eq, xe, xt = (T["%s%d" % (k, h)] for k in ("DB", "LK", "PH", "TT", "EA", "EQ", "XE", "XT"))
+
+        def K(s):
+            return "%s%d" % (s, h)
+
+        def oh(rows, x, digits, j):
+            return T.OH[0:rows, 8 * h + x, digits, j:32:16]
+        ohk, every = [K("OH%d_" % d) for d in range(16)], slice(0, 16)
+
+        at("near", l, h)
+        for b, (bank, key) in enumerate(((D, dk), (QA, ak), (D, dk), (QA, ak))):
+            mm([K("TL"), "CS%d" % b], [key], 512,
+               [[(bank[:, 4 * i:4 * i + 4, :], T.CS[:, 512 * b + 128 * i:512 * b + 128 * i + 128], T.TL[:, h, 0:128])] for i in range(4)])
+            rows = slice(16 * b, 16 * b + 16)
+            how = O["near"][l][h]
+            if how == "v":
+                op("v", [], [key, K("EQ%d_" % b)], 512, lambda bank=bank, rows=rows: V.tensor_scalar(eq[:, rows, :], bank[:], 0.0, None, A.is_equal))
+            else:
+                op("s", [], [key, K("EA%d_" % b)], 512, lambda bank=bank, rows=rows: S.activation(ea[:, rows, :], bank[:], F.Abs))
+                if how == "sv":
+                    op("v", [K("EA%d_" % b)], [K("EQ%d_" % b)], 256, lambda rows=rows: V.tensor_scalar(eq[:, rows, :], ea[:, rows, :], 0.0, None, A.is_equal))
+                elif b % 2:
+                    rows = slice(16 * b - 16, 16 * b + 16)
+                    op("s", [K("EA%d_" % (b - 1)), K("EA%d_" % b)], [K("EQ%d_" % (b - 1)), K("EQ%d_" % b)], 1024,
+                       lambda rows=rows: S.activation(eq[:, rows, :], ea[:, rows, :], F.Relu, bias=1.0, scale=-1.0))
+
+        at("sums", l, h)
+        grps = [[(QB[32 * a:32 * a + 32, j + 1:256:16, :], oh(128, a, every, j), oh(128, 4 + a, every, j))] for j in range(15) for a in range(4)]
+        grps += [[(QB[32 * a:32 * a + 32, 16:256:16, :], oh(128, a, every, 15), oh(128, 4 + a, slice(0, 15), 15))] for a in range(4)]
+        grps += [[(QB[32 * a:32 * a + 32, 0, :], oh(128, a, every, 15), oh(128, 4 + a, 15, 15))] for a in range(4)]
+        mm(ohk, [bk], 2176, grps)
+        for c in range(2):
+            op("v", ["HD"], [bk, K("PH%d_" % c)], 256,
+               lambda c=c: V.tensor_tensor_scan(ph[:, c, :], T.HD[:], QB[:, :, c], 0.0, A.add, A.add))
+        mm([K("PH0_"), K("PH1_"), "TQ", "NID"], [bk], 128, [[(QB[:, 0, :], T.TQ[:], ph[:, :, 255]), (QB[:, 0, :], T.NID[:], ph[:, :, 0])]])
+        pq, phk = T[K("PQ")], [K("PQ0_"), K("PQ1_")]
+        for c in range(2):
+            op("v", [K("PH%d_" % c), "kc"], [bk, phk[c]], 256 if WIDE else 128, lambda c=c: V.tensor_scalar(
+                pq[:, :, 16 * c:16 * c + 16], ph[:, c, :], QB[:, 0, c:c + 1], col["kc"], A.add, A.add))
+        hq = T[K("HQ")]
+        if l == 0:
+            op("v", ["ZR"], [K("HQ")], 32, lambda: V.tensor_copy(hq[:], T.ZR[:, 0:48]))
+        op("v", phk, [K("HQ")], 32, lambda: V.tensor_copy(hq[:, 0:16, :], pq[:, :, 0:32:16]))
+
+        def heads():
+            at("heads", l, h)
+            grp = [(QB[:, 0:16, :], T.ID[:], T.HC[:])]
+            for c in range(2):
+                pm = T["PM%d" % c]
+                grp += [(QB[:, 0:8, :], pm[:, 0:128], hq[:, 0:16, c]), (QB[:, 8:16, :], pm[:, 0:128], hq[:, 1:17, c]),
+                        (QB[:, 15, 1:2], pm[:, 1:129], hq[:, 0, c:c + 1])]
+            mm([K("HQ"), "PM0", "PM1", "HC0", "HC1", "HC2", "ID"], [bk], 450, [grp])
+            op("v", [], [bk, K("HE")], 32, lambda: V.tensor_scalar(T[K("HE")][:], QB[:, 0:16, :], CEN + 0.25, None, A.add))
+
+        at("count", l, h)
+        for b in range(4 * l):
+            mm_part([K("EQ%d_" % b), "WS%d" % b], [mk], 512,
+                    [(M[:, 0:4, :], eq[:, 16 * b + 4 * i:16 * b + 4 * i + 4, :], T.WS[:, 512 * b + 128 * i:512 * b + 128 * i + 128]) for i in range(4)],
+                    b == 0, b == 3)
+        for b in range(4 - 4 * l):
+            grp = [(M[:, 0:4, :], T.ID[:], T.ZR[:, 0:128])] if b == 0 else []
+            for i in range(4):
+                d, e = 4 * b + i + 1, eq[:, 16 * b + 4 * i:16 * b + 4 * i + 4, :]
+                grp.append((M[:, 0:4, d:32], e, T.ID[:, :, 0:32 - d]))
+                if d < 16:
+                    grp.append((M[:, 0:4, 32 - d:32], e, T.ID[:, :, 32 - d:32]))
+            mm_part([K("EQ%d_" % b), "ZR", "ID"], [mk], 650, grp, b == 0, b == 3)
+        op("s", [], [mk, K("NR")], 128, lambda: S.activation(T[K("NR")][:], M[:, 0:4, :], F.Identity))
+
+        who = O["look"][l][h]
+        for i in range(4):
+            at("early" if i < O["pieces"][h][0][1] else "late", l, h)
+            bank, key = ((D, dk), (QA, ak))[i % 2]
+            counts = [(bank[32 * a:32 * a + 32, :, j:32:16], oh(32 * i, a, every, j), oh(32 * i, 4 + a, every, j))
+                      for j in range(16 if i else 0) for a in range(4)]
+            c = slice(512 * i, 512 * i + 512)
+            if WIDE and i == 0:
+                op("v", phk, [K("TT0_")], 512, lambda c=c: V.transpose(tt[:, c], pq[:]))
+            elif str(i) in O["addv"][l][h]:
+                mm(ohk, [key], 2048, [[x] for x in counts])
+                ts = T[K("TU")]
+                op("v", phk, [key, K("TU")], 512, lambda bank=bank: V.tensor_tensor(ts[:], bank[:], pq[:], A.add))
+                bank, key = ts, K("TU")
+            elif i == 0 or i > O["zero"]:
+                mm_part(ohk + phk + ["ID"], [key], 2560 if i else 512, [(bank[:], T.ID[:], pq[:])] + counts, True, 4 if i else 1)
+            else:
+                mm_part(ohk + ["ZR", "ID"], [key], 2560, [(bank[:], T.ID[:], T.ZR[:])] + counts, True, False)
+                mm_part(phk + ["ID"], [key], 512, [(bank[:], T.ID[:], pq[:])], False, True)
+            if i or not WIDE:
+                op("v", [], [key, K("TT%d_" % i)], 512, lambda bank=bank, c=c: V.transpose(tt[:, c], bank[:]))
+            win = tt[:, c].indirect(lk[:, 32 * i:32 * i + 32])
+            if who[i] == "s":
+                op("s", [K("TT%d_" % i), K("LK")], [K("G%d_" % i)], gam * 512, lambda c=c, win=win: S.activation(T[K("G4")][:, c], win, F.Identity))
+            else:
+                op("v", [K("TT%d_" % i), K("LK")], [K("G%d_" % i)], gam * 512, lambda c=c, win=win: V.tensor_copy(T[K("G2")][:, c], win))
+            for a, b in O["pieces"][h]:
+                if b != i + 1:
+                    continue
+                gk, uk = (K("G4"), "U4") if who[a] == "s" else (K("G2"), "U2")
+                grp = [(M[:, a:b, :], T.ID[:], T[K("NR")][:, 32 * a:32 * b])]
+                grp += [(M[:, a:b, :], T[uk][:, :, j:256:16], T[gk][:, 512 * a + j:512 * b:16]) for j in range(16)]
+                mm([K("G%d_" % x) for x in range(a, b)] + [uk, K("NR")], [mk], 64 + 1024 * (4 if who[a] == "s" else 1), [grp])
+                c = slice(32 * a, 32 * b)
+                op("v", [], [mk, K("XE%d_" % a)], 64, lambda a=a, b=b, c=c: V.tensor_copy(xe[:, c], M[:, a:b, :]))
+                op("v", [K("XE%d_" % a)], [K("XT%d_" % a)], 64, lambda a=a, b=b, c=c: V.transpose(xt[:, a:b, :], xe[:, c]))
+                to_list(h, xt, [K("XT%d_" % a)], a, b, "LP", CEN + 0.25, False)
+                if (a == 0, b == 4)[O["late"][h]]:
+                    heads()
+        at("lists", l, h)
+        if l == 1:
+            to_list(h, xt, [K("XT%d_" % a) for a, b in O["pieces"][h]], 0, 4, "LN", CEN + 0.25, True)
+        if O["carry"][l][h] == "k" and (rank or h):
+            op("v", [K("DS")], [K("SX")], 64, lambda: V.transpose(T[K("SX")][:], db[:, 0:4, :]))
+            to_list(h, T[K("SX")], [K("SX")], 0, 4, "SL", 0.25, l == 1)
+
+    def radix(l, h):
+        M, QB, mk, bk = T["M%d" % h], T["QB%d" % h], "M%d" % h, "QB%d" % h
+        si, di, db, ih, il, to, bs, cu, pr, cw = (T["%s%d" % (k, h)] for k in ("SI", "DI", "DB", "IH", "IL", "TO", "BS", "CU", "PR", "CW"))
+        qs = ((M[:, 0:2, :], mk), (QB[:, 0:32, :], bk))
+
+        def K(s):
+            return "%s%d" % (s, h)
+
+        at("front", l, h)
+        if l == 1:
+            for k in range(4):
+                grp = [(M[:, 0:8, :], T.GH[:], T.ST[:, 0:256])] if k == 0 else []
+                grp += [(M[:, 0:8, :], T.ZH[:, 7 - i:135 - i], T.Y0[:, H * h + 256 * i:H * h + 256 * i + 256]) for i in (2 * k, 2 * k + 1)]
+                mm_part(["ZH", "GH", "ST", "Y0%d%d" % (h, k)], [mk], 512, grp, k == 0, k == 3)
+            op("v", [], [mk, K("SI")], 256, lambda: V.tensor_copy(si[:], M[:, 0:8, :]))
+
+        def indicate(d):
+            c = slice(256 * d, 256 * d + 256)
+            if d == 0:
+                op("v", [K("SI")], [K("DI0")], 256, lambda: V.tensor_scalar(di[:, c], si[:], 4, 15, A.arith_shift_right, A.bitwise_and))
+            else:
+                op("v", [K("SI")], [K("DI1")], 256, lambda: V.tensor_scalar(di[:, c], si[:], 15, None, A.bitwise_and))
+            op("v", [K("DI%d" % d)], [K("DB%d" % d)], 256, lambda: V.tensor_copy(db[:, c], di[:, c]))
+            op("s", [K("DB%d" % d)], [K("DB%d" % d)], 256, lambda: S.activation(db[64:128, c], db[64:128, c], F.Square))
+            for q in range(2):
+                px, pk = T[K("PX")] if "t" in O["pos"] else T["PX%d" % q], K("PX") if "t" in O["pos"] else "PX%d" % q
+                mm([K("DB%d" % d)] + ["EE%d" % (4 * q + j) for j in range(4)], [pk], 1024,
+                   [[(px[:, 256 * j:256 * j + 256], T.EE[:, 512 * q + 128 * j:512 * q + 128 * j + 128], db[:, c])] for j in range(4)])
+                op("s", [("b1", "b16")[d]], [pk, K("I%d%d" % (d, q)), K("TO%d" % (2 * d + q))], 1050, lambda q=q, px=px: S.activation(
+                    (ih, il)[d][:, 1024 * q:1024 * q + 1024], px[:], F.Relu, bias=col[("b1", "b16")[d]], scale=(1.0, 16.0)[d],
+                    accum_out=to[:, 2 * d + q:2 * d + q + 1]))
+
+        def base(d):
+            mm(["TS", K("TO%d" % (2 * d)), K("TO%d" % (2 * d + 1))], [bk], 256, [[(QB[:, 40, :], T.TS[:], to[:, 2 * d:2 * d + 2])]])
+            op("v", [], [bk, K("BS%d" % (2 * d))], 2, lambda: V.tensor_reduce(bs[:, 2 * d:2 * d + 1], QB[:, 40, :], AX.X, A.add))
+
+        def gather_mm(q, src, keys, z, start, stop):
+            mm_part(keys + [z], [qs[q][1]], 1024, [(qs[q][0], T[z][:, 15 - r:143 - r], src[:, 1024 * q + r:1024 * q + 1024:16]) for r in range(16)],
+                    start, stop)
+
+        def listed(q, name, keys, mul, plus):
+            op("v", [], [qs[q][1]] + keys, 64, lambda: V.tensor_scalar(T[K(name)][:, 64 * q:64 * q + 64], qs[q][0], mul, plus, A.mult, A.add))
+
+        indicate(0)
+        at("near", l, h)
+        indicate(1)
+        at("sums", l, h)
+        base(0)
+        op("v", [K("BS0"), K("I00"), K("I01")], [K("CU")], 1024, lambda: V.tensor_tensor_scan(cu[:], ih[:], ih[:], bs[:, 0:1], A.add, A.max))
         for q in range(2):
-            gather_mm(h, q, T["IH%d" % h], ["I0%d%d" % (h, q)], T.ZD, "ZD", True, False)
-        if h == 0:
-            op("v", ["SW0", "SV0"], ["CW0"], H,
-               lambda: V.tensor_tensor_scan(cw[:, 1:H + 1], T.SV0[:, 1:H + 1], T.SW0[:, 1:H + 1], cw[:, 0:1], A.add, A.add))
-        else:
-            op("v", ["SW1", "fill"], ["CW1"], H,
-               lambda: V.tensor_tensor_scan(cw[:, 1:H + 1], T.NEG[:, 0:H], T.SW1[:, 1:H + 1], cw[:, 0:1], A.max, A.add))
-
-        def piece(q):
             c = slice(1024 * q, 1024 * q + 1024)
-            op("v", ["CW%d" % h, "L1%d%d" % (h, q), "I1%d%d" % (h, q)], ["PR%d%d" % (h, q)], gam * 1024,
-               lambda: V.tensor_tensor(T["PR%d" % h][:, c], cw[:, 0:H + 1].indirect(T["L1%d" % h][:, 64 * q:64 * q + 64]),
-                                       T["IL%d" % h][:, c], A.mult))
-            gather_mm(h, q, T["PR%d" % h], ["PR%d%d" % (h, q)], T.Z, "Z", False, True)
-            to_list(h, q, "L2", 0.0625, CEN + 0.25)
-        piece(0); piece(1)
-        op("v", ["CW%d" % h, "BL%d" % h, "HC"], ["HF%d" % h], 50,
-           lambda: V.tensor_tensor(T["HF%d" % h][:], cw[:, 0:H + 1].indirect(T["BL%d" % h][:]), T.HC[:], A.add))
-        op("v", ["HF%d" % h], ["HE%d" % h], 32, lambda: V.tensor_scalar(T["HE%d" % h][:], T["HF%d" % h][:], 0.25, None, A.add))
+            op("v", [K("CU"), K("I0%d" % q)], [K("PR%d" % q)], 512, lambda c=c: V.tensor_tensor_scan(pr[:, c], cu[:, c], ih[:, c], 0.0, A.max, A.mult))
+            gather_mm(q, pr, [K("PR%d" % q)], "Z", True, True)
+            listed(q, "L1", [K("L1%d" % q)], 1.0, 0.25)
+        at("count", l, h)
+        cuts = O["cuts"][l][h]
+        both = any(e == "v" for e, a, b in cuts)
+        if both:
+            z = WC // 3
+            dmas("y", "dz%d%d" % (l, h), ["mZ"], [K("SW"), K("SV")], [(T[K(k)][:, z * j:z * j + z], T.mZ[:]) for k in ("SW", "SV") for j in range(3)], 5000)
+        for e, a, b in cuts:
+            keys = [K("%s%d" % (k, q)) for k in ("I1", "L1") for q in range(a // 1024, (b + 1023) // 1024)]
+            o = T[K("SV" if e == "v" else "SW")][:, 0:H + 1].indirect(T[K("L1")][:, a // 16:b // 16])
+            if e == "v":
+                op("v", keys, [K("SV")], sig * (b - a), lambda o=o, a=a, b=b: V.tensor_scalar(o, il[:, a:b], 0.0625, 0.0, A.mult, A.add))
+            else:
+                op("s", keys, [K("SW")], sig * (b - a), lambda o=o, a=a, b=b: S.activation(o, il[:, a:b], F.Tanh))
+        at("early", l, h)
+        base(1)
+        op("v", [K("BS2"), "c2"], [K("CW")], 1, lambda: V.tensor_scalar(cw[:, 0:1], bs[:, 2:3], 0.0625, col["c2"], A.mult, A.add))
+        op("v", [K("BS0"), K("TO0"), K("TO1")], [K("BS1")], 1, lambda: V.tensor_scalar(bs[:, 1:2], bs[:, 0:1], to[:, 0:1], to[:, 1:2], A.add, A.add))
+        op("v", [K("BS0"), K("BS1")], [K("BL")], 1, lambda: V.tensor_copy(T[K("BL")][:], bs[:, 0:2]))
+        for q in range(2):
+            gather_mm(q, ih, [K("I0%d" % q)], "ZD", True, False)
+        if both:
+            op("v", [K("SW"), K("SV")], [K("CW")], H,
+               lambda: V.tensor_tensor_scan(cw[:, 1:H + 1], T[K("SV")][:, 1:H + 1], T[K("SW")][:, 1:H + 1], cw[:, 0:1], A.add, A.add))
+        else:
+            op("v", [K("SW"), "NEG"], [K("CW")], H,
+               lambda: V.tensor_tensor_scan(cw[:, 1:H + 1], T.NEG[:, 0:H], T[K("SW")][:, 1:H + 1], cw[:, 0:1], A.max, A.add))
+        for q in range(2):
+            c = slice(1024 * q, 1024 * q + 1024)
+            op("v", [K("CW"), K("L1%d" % q), K("I1%d" % q)], [K("PR%d" % q)], gam * 1024, lambda c=c, q=q: V.tensor_tensor(
+                pr[:, c], cw[:, 0:H + 1].indirect(T[K("L1")][:, 64 * q:64 * q + 64]), il[:, c], A.mult))
+            gather_mm(q, pr, [K("PR%d" % q)], "Z", False, True)
+            listed(q, "LP", ["LP%d_%d" % (k, h) for k in (2 * q, 2 * q + 1)], 0.0625, CEN + 0.25)
+        at("heads", l, h)
+        op("v", [K("CW"), K("BL"), "HR"], [K("HF")], 50, lambda: V.tensor_tensor(T[K("HF")][:], cw[:, 0:H + 1].indirect(T[K("BL")][:]), T.HR[:], A.add))
+        op("v", [K("HF")], [K("HE")], 32, lambda: V.tensor_scalar(T[K("HE")][:], T[K("HF")][:], 0.25, None, A.add))
+        at("lists", l, h)
+        if O["carry"][l][h] == "k" and (rank or h):
+            sj, sl, o = T[K("SK")], ["SL%d_%d" % (k, h) for k in range(4)], QB[:, 64:128, :]
+            if l == 0:
+                dmas("y", "dsj%d" % h, [], [K("SK")], [(sj[:, 16 * j:16 * j + 16], T.slot[j, H * h:H * h + H]) for j in range(8)], 4000)
+                op("v", [K("SK")], [K("SX")], 128, lambda: V.tensor_copy(T[K("SX")][:], sj[:]))
+                mm([K("SX"), "ID"], [bk], 128, [[(o, T[K("SX")][:], T.ID[:])]])
+                op("v", [], [bk] + sl, 128, lambda: V.tensor_copy(T[K("SL")][:], o))
+            else:
+                mm(["ZW", "GW", "ST"] + ["Y0%d%d" % (h, k) for k in range(4)], [bk], 2176,
+                   [[(o, T.GW[:], T.ST[:, 0:128])] + [(o, T.ZW[:, 15 - r:143 - r], T.Y0[:, H * h + r:H * h + H:16]) for r in range(16)]])
+                op("v", [], [bk, K("SK")], 128, lambda: V.tensor_copy(sj[:], o))
+                op("v", [K("SK")], [K("SK")], 128, lambda: V.tensor_scalar(sj[:], sj[:], 255, None, A.bitwise_and))
+                op("v", [K("SK")], sl, 128, lambda: V.tensor_copy(T[K("SL")][:], sj[:]))
 
-    def next_slots(h):
-        def part(j):
-            def run():
-                for i in (2 * j, 2 * j + 1):
-                    m = P.matmul(T["Q%d0" % h][:, 0:256], T["ZH%d" % h][:, 7 - i:135 - i],
-                                 T.Y0[:, H * h + 256 * i:H * h + 256 * i + 256], i == 0, i == 7)
-                return m
-            op("p", ["ZH%d" % h, "Y0%d" % (4 * h + j)], ["Q%d0" % h], 512, run)
-        for j in range(4):
-            part(j)
-        op("v", [], ["Q%d0" % h, "SI%d" % h], 256, lambda: V.tensor_copy(T["SI%d" % h][:], T["Q%d0" % h][:, 0:256]))
+    def to_list(h, xt, keys, a0, b0, name, plus, natural):
+        D, dk = T["QB%d" % h], "QB%d" % h
+        outs = [(slice(64 + x, 128, 4), x) for x in range(4)] if natural else [(slice(64 + 16 * a0, 64 + 16 * b0), slice(a0, b0))]
+        mm(keys + ["R0", "R1"], [dk], 256 * len(outs),
+           [[(D[:, m, q], T["R%d" % q][:, 16 - 16 * y:144 - 16 * y], xt[:, x, 16 * y:16 * y + 16]) for y in range(2)] for m, x in outs for q in range(2)])
+        op("v", [], [dk] + ["%s%d_%d" % (name, k, h) for k in range(a0, b0)], 32 * (b0 - a0),
+           lambda: V.tensor_scalar(T["%s%d" % (name, h)][:, 32 * a0:32 * b0], D[:, 64 + 16 * a0:64 + 16 * b0, :], plus, None, A.add))
+
+    def part(l, h, k, m):
+        if l == 0 and O["pos"] == "tt":
+            return T.Y0[:, 4 * h + k, :] if m == 1 else T.Y0[:, 4 * h + k:4 * h + k + m, :]
+        return T["Y%d" % l][:, H * h + 512 * k:H * h + 512 * (k + m)]
 
     def receivers(l, r):
         return [1] if (l, r) == (1, 0) else list(range(r + 1, n))
@@ -328,171 +654,261 @@ def rank_program(g, core, T, topo):
         return m
 
     def layer(l):
-        src = (T.X, T.Y0)[l]
-        bkeys = ["X1"] if l == 0 else ["Y0%d" % j for j in range(4, 8)]
         dst = T["Y%d" % l]
-        df, dw = T["DF%d" % l], T["DW%d" % l]
-        win, wink = (T.DA, dw), ("DA", "DW%d" % l)
         tb, ld = T["TB%d" % l], T["LD%d" % l]
-        cp = (T["CP%d0" % l], T["CP%d1" % l])
-        cpk = [["CP%d%d%d" % (l, h, q) for q in range(2)] for h in range(2)]
+        wink = ["WN0%d" % h for h in range(2)]
+        win = [T[k] for k in wink]
+        cap = [T["CP%d%d" % (l, h)] for h in range(2)]
+        capk = [["CP%d%d%d" % (l, h, q) for q in range(2)] for h in range(2)]
 
-        if l == 1:
-            next_slots(0); next_slots(1)
-            dmas("g", "dxf", ["Y0%d" % j for j in range(4)], ["XF"], [(T.XF[:], T.Y0[:, 0:H])], 6000)
-        elif O["xf"] == "s":
-            op("s", ["X0"], ["XF"], H, lambda: S.activation(T.XF[:], T.X[:, 0:H], F.Identity, scale=SC))
-        else:
-            op("v", ["X0"], ["XF"], H, lambda: V.tensor_scalar(T.XF[:], T.X[:, 0:H], SC, None, A.mult))
-        for h, d in ((0, 0), (1, 0), (0, 1), (1, 1)):
-            digit(h, d)
-            indicate(h, d, 0); indicate(h, d, 1)
-        pass1(0); pass1(1)
-        z = WC // 3
-        dmas("y", "dz%d" % l, ["mZ"], ["SW0", "SV0"], [(T[k][:, z * j:z * j + z], T.mZ[:]) for k in ("SW0", "SV0") for j in range(3)], 5000)
-        slot_list(l)
-        for who, h, cuts in ((O["x1e"], 0, O["x1a"][l]), ("ssss", 1, O["x1b"])):
-            for e, a, b in zip(who, cuts, cuts[1:]):
-                scatter1(e, h, a, b)
-        pass2(0); pass2(1)
-
-        def place_a(q):
-            op("s", ["XF", "L20%d" % q], ["DF%d" % l], sig * 1024,
-               lambda: S.activation(df[:].indirect(T.L20[:, 64 * q:64 * q + 64]), T.XF[:, 1024 * q:1024 * q + 1024], F.Tanh))
-
-        def place_b(a, b):
-            op("v", bkeys + span("L2", 1, a, b), ["DW%d" % l], sig * (b - a),
-               lambda: V.tensor_copy(dw[:].indirect(T.L21[:, a // 16:b // 16]), src[:, H + a:H + b]))
-        place_a(0); place_a(1)
-        for a, b in zip(O["x2b"], O["x2b"][1:]):
-            place_b(a, b)
-        HW = W // 2
-
-        def rounded(q):
-            c = slice(HW * q, HW * q + HW)
-            op("s", ["DF%d" % l], ["TM%d" % q], HW, lambda: S.activation(T.TM[:, c], df[:, c], F.Identity, bias=MAG, scale=1.0 / SC))
-            op("s", ["TM%d" % q], ["DA%d" % q] + (["DA"] if q == 0 else []), HW, lambda: S.activation(T.DA[:, c], T.TM[:, c], F.Identity, bias=-MAG))
-        rounded(0); rounded(1)
-        part = [["DA0", "DA1"], [wink[1], wink[1]]]
-
-        def cap(h, e):
-            if e == "x":
-                op("v", ["HE%d" % h, "fill"], cpk[h], sig * 256,
-                   lambda: V.tensor_copy(cp[h][:].indirect(T["HE%d" % h][:, 0:16]), T.NEG[:, 0:256]))
-                return
-
-            def piece(q):
-                c = slice(HW * q, HW * q + HW)
-                if e == "v":
-                    op("v", [part[h][q]], [cpk[h][q]], HW / 2, lambda: V.tensor_scalar(cp[h][:, c], win[h][:, c], 1024.0, 261632.0, A.mult, A.add))
+        def put(h):
+            xf, xk = T["XF%d" % h], "XF%d" % h
+            at("put", l, h)
+            e, x, tables = O["put"][l][h], T["X%d" % h], O["pos"][h] == "t"
+            if e == "s" and l == 1:
+                for k in (0, 2):
+                    dmas("g", "dxf%d%d" % (h, k), ["Y0%d%d" % (h, k), "Y0%d%d" % (h, k + 1)], [xk + str(k), xk + str(k + 1), "~xf"],
+                         [(xf[:, 512 * k:512 * k + 1024], part(0, h, k, 2))], O["dl"] * 4000)
+            elif e == "s":
+                for a, b in ((0, 1), (1, 2), (2, 3), (3, 4)) if tables else ((0, 2), (2, 4)):
+                    op("s", ["X%d" % h], [xk + str(k) for k in range(a, b)], 512 * (b - a), lambda a=a, b=b: S.activation(
+                        xf[:, 512 * a:512 * b], x[:, :, 32 * a:32 * b] if tables else x[:, 512 * a:512 * b], F.Identity, scale=SC))
+            (places if tables else radix)(l, h)
+            if l == 0:
+                fill(1, h, ["HE%d" % h])
+            at("put", l, h)
+            for k, m in [(a, b - a) for a, b in O["pieces"][h]]:
+                o, lk = win[h][:].indirect(T["LP%d" % h][:, 32 * k:32 * k + 32 * m]), ["LP%d_%d" % (j, h) for j in range(k, k + m)]
+                c = slice(512 * k, 512 * (k + m))
+                if e == "s":
+                    op("s", [xk + str(j) for j in range(k, k + m)] + lk, [wink[h], "~put"], sig * 512 * m, lambda o=o, c=c: S.activation(o, xf[:, c], F.Tanh))
+                elif l == 0:
+                    op("v", ["X%d" % h, "ST"] + lk, [wink[h]], sig * 512 * m, lambda o=o, c=c: V.tensor_tensor(o, x[:, c], T.ST[:, 0:512 * m], A.mult))
                 else:
-                    op("s", [part[h][q]], [cpk[h][q]], HW, lambda: S.activation(cp[h][:, c], win[h][:, c], F.Identity, bias=261632.0, scale=1024.0))
-            piece(0); piece(1)
-        cap(0, O["capA"]); cap(1, O["capB"])
+                    op("v", ["Y0%d%d" % (h, j) for j in range(k, k + m)] + lk, [wink[h]], sig * 512 * m,
+                       lambda o=o, k=k: V.tensor_copy(o, T.Y0[:, H * h + 512 * k:H * h + 512 * (k + m)]))
+            at("cap", l, h)
+            if O["cap"][l][h] == "x":
+                op("v", ["HE%d" % h, "mB"], capk[h], sig * 256, lambda: V.tensor_copy(cap[h][:].indirect(T["HE%d" % h][:, 0:16]), T.mB[:, 0:256]))
+            else:
+                for q in range(2):
+                    c = slice(HW * q, HW * q + HW)
+                    op("s", [wink[h]], [capk[h][q]], HW, lambda c=c: S.activation(cap[h][:, c], win[h][:, c], F.Identity, bias=63.5, scale=64.0))
+        for h in range(2):
+            if O["pos"][h] == "t":
+                front(l, h)
+        put(0); put(1)
+        at("lists", l, 1)
+        for b, k in enumerate(("D0", "QA0") * 2 if l == 0 else ()):
+            grps = []
+            for i in range(4):
+                d, o = 4 * b + i + 1, slice(4 * i, 4 * i + 4)
+                grps.append([(T[k][:, o, :], T.ID[:], T.ZR[:, 0:128]), (T[k][:, o, d:32], T.ID[:], T.ID[:, :, 0:32 - d])]
+                            + [(T[k][:, o, 32 - d:32], T.ID[:], T.ID[:, :, 32 - d:32])] * (d < 16))
+            mm(["ID", "ZR"], [k], 1200, grps)
+            op("s", [], [k, "WS%d" % b], 512, lambda b=b, k=k: S.activation(T.WS[:, 512 * b:512 * b + 512], T[k][:], F.Identity))
 
-        def running(h, split):
-            ys = T["YS%d" % h]
-            if not split:
-                op("v", cpk[h] + part[h] + [wink[h]], ["YS%d" % h, "YS%db" % h], HW,
-                   lambda: V.tensor_tensor_scan(ys[:], cp[h][:], win[h][:], NEUT, A.min, A.max))
+        def first(h):
+            ys, narrow = T["YS%d" % h], O["narrow"][l][h] == "s"
+            src = T["YR%d" % h] if narrow else win[h]
+            if not narrow:
+                op("v", capk[h] + [wink[h]], ["YS%d" % h, "YS%db" % h], W, lambda: V.tensor_tensor_scan(ys[:], src[:], cap[h][:], -1.0, A.max, A.min))
                 return
-            op("v", [cpk[h][0], part[h][0], wink[h]], ["YS%d" % h], HW / 2,
-               lambda: V.tensor_tensor_scan(ys[:, 0:HW], cp[h][:, 0:HW], win[h][:, 0:HW], NEUT, A.min, A.max))
-            op("v", [cpk[h][1], part[h][1], wink[h], "YS%d" % h], ["YS%db" % h], HW / 2,
-               lambda: V.tensor_tensor_scan(ys[:, HW:W], cp[h][:, HW:W], win[h][:, HW:W], ys[:, HW - 1:HW], A.min, A.max))
+            for q in range(2):
+                c = slice(HW * q, HW * q + HW)
+                if narrow:
+                    op("s", [wink[h]], ["YR%d" % h + "b" * q], HW, lambda c=c: S.activation(src[:, c], win[h][:, c], F.Identity))
+                op("v", [capk[h][q], "YR%d" % h + "b" * q if narrow else wink[h]] + ["YS%d" % h] * q, ["YS%d" % h + "b" * q], HW / 2 if narrow else HW,
+                   lambda c=c, q=q: V.tensor_tensor_scan(ys[:, c], src[:, c], cap[h][:, c], ys[:, HW - 1:HW] if q else -1.0, A.max, A.min))
 
         def table(h):
-            op("v", ["YS%d" % h, "YS%db" % h, "HE%d" % h], ["TB%d%d" % (l, h)], gam * 256,
-               lambda: V.tensor_copy(tb[:, 256 * h:256 * h + 256], T["YS%d" % h][:].indirect(T["HE%d" % h][:, 16:32])))
+            i, o = T["YS%d" % h][:].indirect(T["HE%d" % h][:, 16:32]), tb[:, 256 * h:256 * h + 256]
+            e = O["tab"][h]
+            op(e, ["YS%d" % h, "YS%db" % h, "HE%d" % h], ["TB%d%d" % (l, h)], gam * 256,
+               (lambda: V.tensor_copy(o, i)) if e == "v" else (lambda: S.activation(o, i, F.Identity)))
 
-        def store(a, b, w):
-            if l == 1:
-                dmas("y", "dout", w, [], [(T.y[:, a:b], dst[:, a:b])], 2000 + (b - a))
+        def again(h, cy, cyk):
+            ys = T["YS%d" % h]
+            op("v", [cyk, "HE%d" % h], ["YS%d" % h, "YS%db" % h], sig * 256, lambda: V.tensor_copy(ys[:].indirect(T["HE%d" % h][:, 0:16]), cy))
+            op("v", capk[h] + ["YS%d" % h, "YS%db" % h], ["YR%d" % h, "YR%db" % h], HW,
+               lambda: V.tensor_tensor_scan(T["YR%d" % h][:], cap[h][:], ys[:], -1.0, A.min, A.max))
 
-        def unsort_a(e, a, b):
-            i = T.YS0[:].indirect(T.L20[:, a // 16:b // 16])
-            r = ["YS0", "YS0b"] + span("L2", 0, a, b)
-            w = ["Y%d%d" % (l, j) for j in range(a // 512, b // 512)]
-            k = SC if l == 0 else 1.0
-            if e == "v":
-                op("v", r, w, gam * (b - a), lambda: V.tensor_scalar(dst[:, a:b], i, k, None, A.mult))
+        mul, plus = ((1.0, SC), (1.0 / SC, -1.0))[l]
+
+        def store(h):
+            for b in range(4 * l):
+                a = H * h + 512 * b
+                dmas("y", "dout", ["Y1%d%d" % (h, b)], [], [(T.y[:, a:a + 512], dst[:, a:a + 512])], 2500)
+
+        def back(h, src, keys, local=False):
+            who, name = O["back"][l][h], "LN" if l == 1 and O["pos"][h] == "t" else "LP"
+            for k in range(4):
+                i = src[:].indirect(T["%s%d" % (name, h)][:, 32 * k:32 * k + 32])
+                o = T["YL%d" % h][:, 512 * k:512 * k + 512] if local else part(l, h, k, 1)
+                r, w = keys + ["%s%d_%d" % (name, k, h)], ["Y%s%d%d" % ("L" if local else l, h, k)]
+                if who[k % len(who)] == "v":
+                    op("v", r, w, gam * 512, lambda i=i, o=o: V.tensor_scalar(o, i, mul, plus, A.mult, A.add))
+                else:
+                    op("s", r, w, gam * 512, lambda i=i, o=o: S.activation(o, i, F.Identity, bias=plus, scale=mul))
+
+        def by_slot(h, cy, cyk):
+            ck = T["CK%d" % h]
+            op("v", [cyk], ["CK%d" % h], 128, lambda: V.tensor_scalar(ck[:], cy, mul, plus, A.mult, A.add))
+            for k in range(4):
+                i, o = ck[:].indirect(T["SL%d" % h][:, 32 * k:32 * k + 32]), part(l, h, k, 1)
+                op("v", ["CK%d" % h, "SL%d_%d" % (k, h), "YL%d%d" % (h, k)], ["Y%d%d%d" % (l, h, k)], gam * 512,
+                   lambda i=i, o=o, k=k: V.tensor_tensor(o, i, T["YL%d" % h][:, 512 * k:512 * k + 512], A.max))
+
+        def finish(h, cy, cyk):
+            ys = ["YS%d" % h, "YS%db" % h]
+            if cy is None:
+                back(h, T["YS%d" % h], ys)
+            elif O["carry"][l][h] == "k":
+                back(h, T["YS%d" % h], ys, True)
+                by_slot(h, cy, cyk)
             else:
-                op("s", r, w, gam * (b - a), lambda: S.activation(dst[:, a:b], i, F.Identity, scale=k))
-            store(a, b, w)
-
-        def local_b(e, a, b):
-            i = T.YS1[:].indirect(T.L21[:, a // 16:b // 16])
-            r, w = ["YS1", "YS1b"] + span("L2", 1, a, b), ["YL%d" % j for j in range(a // 512, b // 512)]
-            if e == "v":
-                op("v", r, w, gam * (b - a), lambda: V.tensor_copy(T.YL[:, a:b], i))
-            else:
-                op("s", r, w, gam * (b - a), lambda: S.activation(T.YL[:, a:b], i, F.Identity))
+                again(h, cy, cyk)
+                back(h, T["YR%d" % h], ["YR%d" % h, "YR%db" % h])
+            store(h)
 
         def merge(out, outk, a, ak, b, bk):
-            op("v", [ak, bk], [outk], 512, lambda: V.tensor_tensor(out, a, b, A.max))
+            if not O["mp"]:
+                op("v", [ak, bk], [outk], 512, lambda: V.tensor_tensor(out, a, b, A.max))
+                return
+            k = ("M0", "M1", "D1", "QA1")[len(used) % 4]
+            used.append(k)
+            mm([bk, "ID"], [k], 256, [[(T[k][:, 8:16, :], T.ID[:], b)]])
+            op("v", [ak], [k, outk], 256, lambda: V.tensor_tensor(out, T[k][:, 8:16, :], a, A.max))
+        used = []
 
-        running(0, True); table(0)
-        running(1, True)
+        at("first", l, 0)
+        first(0); table(0)
+        at("first", l, 1)
+        first(1)
         if rank < n - 1:
             table(1)
-        for j, e in enumerate(O["lb"]):
-            local_b(e, H // len(O["lb"]) * j, H // len(O["lb"]) * (j + 1))
         senders = [r for r in range(rank) if rank in receivers(l, r)]
-        if senders:
-            def landed():
-                cnt["arr%d" % l] = sum(bin(engine_mask(l, r)).count("1") for r in senders)
-                return ("arr%d" % l, cnt["arr%d" % l])
-            soft = [("TB%d0" % l, O["E"]), ("TB%d1" % l, O["E"])] if rank < n - 1 else [("TB%d0" % l, O["E"] + 400), ("YS1b", O["E"] + 400)]
-            add("x", [], ["LD%d" % l], 0, 0, landed, soft)
-        if rank < n - 1:
-            peers = [T.cores[t] for t in receivers(l, rank)]
+
+        def exchange(name, land, halves, wait):
+            keys = ["TB%d%d" % (l, h) for h in halves]
             passed = (l, rank) == (1, 1)
 
-            def send():
-                ids = [DstId(rid=topo.addr(c)[0], pnc=topo.addr(c)[1]) for c in peers]
-                srcs = [tb[:, 0:256], tb[:, 256:512]] + ([ld[:, 0, :]] if passed else [])
-                g.remote_dma_fused([RemoteDMATransfer(dst_ids=ids, dma_engine_mask=engine_mask(l, rank), remote_sem=T.sem["arr%d" % l],
-                                                      srcs=srcs, dsts=[ld[:, rank, :] for c in peers], alu_op=2)],
-                                   local_sem=T.sem["sent%d" % l])
-                cnt["sent%d" % l] = bin(engine_mask(l, rank)).count("1")
-                return ("sent%d" % l, cnt["sent%d" % l])
-            add("g", (["LD%d" % l] if passed else []) + ["TB%d0" % l, "TB%d1" % l], [], 300, 2000, send)
+            def landed():
+                cnt["arr" + name] = sum(bin(engine_mask(l, r)).count("1") for r in senders)
+                return ("arr" + name, cnt["arr" + name])
+            if senders and (passed or rank == n - 1):
+                add("x", [], ["LD" + name], 0, 0, landed, [(k if rank < n - 1 or k[-1] == "0" else "YS1b", wait) for k in keys])
+            if rank < n - 1:
+                peers = [T.cores[t] for t in receivers(l, rank)]
+
+                def send():
+                    ids = [DstId(rid=topo.addr(c)[0], pnc=topo.addr(c)[1]) for c in peers]
+                    srcs = [tb[:, 256 * h:256 * h + 256] for h in halves] + ([land[:, 0, :]] if passed else [])
+                    g.remote_dma_fused([RemoteDMATransfer(dst_ids=ids, dma_engine_mask=engine_mask(l, rank), remote_sem=T.sem["arr" + name], srcs=srcs,
+                                                          dsts=[land[:, rank, :] for c in peers], alu_op=2 if len(srcs) > 1 else 0)],
+                                       local_sem=T.sem["sent" + name])
+                    cnt["sent" + name] = bin(engine_mask(l, rank)).count("1")
+                    return ("sent" + name, cnt["sent" + name])
+                add("g", (["LD" + name] if passed else []) + keys, ["~send"], 1800 if name == "A" else 300, 2000, send)
+                if senders and not passed:
+                    add("x", [], ["LD" + name], 0, 0, landed, [("~send", O["E"] - 550)])
+
+        early = l == 0 and O["early"]
+        if early:
+            exchange("A", T.LA, [0], O["E"] + 1500)
+        exchange(str(l), ld, [1] if early else [0, 1], O["E"])
+        at("carry", l + 1, 0)
         if senders:
-            ca, cak = ld[:, senders[0], :], "LD%d" % l
-            for r in senders[1:]:
-                merge(T.CA0[:], "CA0", ca, cak, ld[:, r, :], "LD%d" % l)
-                ca, cak = T.CA0[:], "CA0"
-            op("v", [cak, "HE0"], ["DA", "DA0", "DA1"], sig * 256, lambda: V.tensor_copy(T.DA[:].indirect(T.HE0[:, 0:16]), ca))
-            running(0, False)
-            merge(T.CA1[:], "CA1", ca, cak, tb[:, 0:256], "TB%d0" % l)
-            cb, cbk = T.CA1[:], "CA1"
+            parts = [(T.LA[:, r, :], "LDA") for r in senders if early] + [(ld[:, r, :], "LD%d" % l) for r in senders]
+            ca, cak = parts[0]
+            for b, bk in parts[1:]:
+                merge(T.CY0[:], "CY0", ca, cak, b, bk)
+                ca, cak = T.CY0[:], "CY0"
+            finish(0, ca, cak)
+            at("carry", l + 1, 1)
+            merge(T.CY1[:], "CY1", ca, cak, tb[:, 0:256], "TB%d0" % l)
+            finish(1, T.CY1[:], "CY1")
         else:
-            cb, cbk = tb[:, 0:256], "TB%d0" % l
+            finish(0, None, None)
+            at("carry", l + 1, 1)
+            finish(1, tb[:, 0:256], "TB%d0" % l)
 
-        def carry_b(a, b):
-            w = ["Y%d%d" % (l, j) for j in range((H + a) // 512, (H + b) // 512)]
-            op("v", [cbk, "SL"] + ["YL%d" % j for j in range(a // 512, b // 512)], w, gam * (b - a),
-               lambda: V.tensor_tensor(dst[:, H + a:H + b], cb.indirect(T.SL[:, a // 16:b // 16]), T.YL[:, a:b], A.max))
-            store(H + a, H + b, w)
-        who = O["ua"] if l == 0 else O["ua1"]
-        for j, e in enumerate(who):
-            unsort_a(e, H // len(who) * j, H // len(who) * (j + 1))
-        cuts = O["kb"] if l == 0 else O["kb1"]
-        for a, b in zip(cuts, cuts[1:]):
-            carry_b(a, b)
+    for l in range(2):
+        tag[0] = str(l)
+        layer(l)
+    live = [c["step"] < 1e9 for c in calls]
+    for i in range(len(calls) - 1, -1, -1):
+        for d in list(calls[i]["deps"]) + [d for d, x in calls[i]["soft"]] if live[i] else ():
+            live[d] = True
+    new = {i: k for k, i in enumerate(i for i in range(len(calls)) if live[i])}
+    calls = [dict(c, deps=set(new[d] for d in c["deps"]), soft=[(new[d], x) for d, x in c["soft"]]) for c, x in zip(calls, live) if x]
+    return calls, cnt, Q
 
-    layer(0); layer(1)
 
-    N = len(calls)
-    if O.get("hook"):
-        O["hook"](calls)
+def plan(calls):
+    O, N = OPT, len(calls)
+    before = [[(d, calls[d]["lag"]) for d in c["deps"]] + list(c["soft"]) for c in calls]
     users = [[] for _ in range(N)]
-    left = [0] * N
+    for i in range(N):
+        for d, x in before[i]:
+            users[d].append((i, x))
+    busy, tail = [c["busy"] for c in calls], [c["lag"] for c in calls]
+
+    def lay(turn, after, head):
+        start, taken = [0.0] * N, {}
+        for i in turn:
+            t = max([start[d] + busy[d] + x for d, x in after[i]] + [head[i]])
+            gaps = taken.setdefault(calls[i]["q"], [])
+            k = 0
+            while k < len(gaps) and gaps[k][1] <= t:
+                k += 1
+            while k < len(gaps) and gaps[k][0] < t + busy[i]:
+                t = max(t, gaps[k][1]); k += 1
+            gaps.insert(k, (t, t + busy[i]))
+            start[i] = t
+        return start
+
+    step = [c["step"] for c in calls]
+    for i in range(N - 1, -1, -1):
+        step[i] = min([step[i]] + [step[u] for u, x in users[i]])
+    turn, best = sorted(range(N), key=lambda i: (step[i], i)), None
+    for _ in range(O["rounds"]):
+        start = lay(turn, before, [0.0] * N)
+        end = max(start[i] + busy[i] + tail[i] for i in range(N))
+        if best is None or end < best[0]:
+            best = (end, start, turn)
+        rank_in = {i: k for k, i in enumerate(turn)}
+        late = lay(sorted(range(N), key=lambda i: (-start[i] - busy[i], -rank_in[i])), users, tail)
+        turn = sorted(range(N), key=lambda i: (-late[i] - busy[i], rank_in[i]))
+    rank_in = {i: k for k, i in enumerate(best[2])}
+    order = sorted(range(N), key=lambda i: (best[1][i], rank_in[i]))
+    late = [c["name"] == "0xLD0.0" for c in calls]
+    for i in range(N):
+        late[i] = late[i] or any(late[d] for d, x in before[i])
+    queue, first = [c["q"] for c in calls], [i for i in order if not late[i]]
+    sent = [0.0 if c["name"] == "0gTB01.0" else -O["E"] for c in calls]
+    first = polish(first, 0, queue, before, [[(u, x) for u, x in b if not late[u]] for b in users], busy, sent, O["moves"])
+    order = polish(first + [i for i in order if late[i]], len(first), queue, before, users, busy, tail, O["moves"])
+    return {calls[i]["name"]: k for k, i in enumerate(order)}
+
+
+PLANS = {}
+
+
+def rank_program(g, core, T, topo):
+    rank = T.rank_of(core)
+    if rank is None:
+        return
+    like = len(T.cores) - 2
+    if like not in PLANS:
+        PLANS[like] = plan(collect(g, T, topo, like)[0])
+    place = PLANS[like]
+    calls, cnt, Q = collect(g, T, topo, rank)
+    N = len(calls)
+    users, left, prio = [[] for _ in range(N)], [0] * N, [0.0] * N
     for i, c in enumerate(calls):
         for d in list(c["deps"]) + [d for d, x in c["soft"]]:
             users[d].append(i); left[i] += 1
-    place = {nm: j for j, nm in enumerate(O["order"].split())}
-    prio = [0.0] * N
     for i in range(N - 1, -1, -1):
         prio[i] = place.get(calls[i]["name"], min([prio[u] for u in users[i]] + [1e9]) - 0.5)
     ready, order = [i for i in range(N) if left[i] == 0], []

import math
from concourse.bass import DstId, RemoteDMATransfer
from concourse.mybir import AluOpType as A, AxisListType as AX, ActivationFunctionType as F

H = 2048
W = H + 256
HW = W // 2
PF = W // 3
CEN = 1152.0
WC = H + 16
SC = 2.0 ** -12

OPT = {"sig": 2.6, "gam": 1.3, "pe": 0.46, "E": 2800.0, "hop": 220.0,
       "near": [["ss", "ss"], ["ss", "ss"]],
       "look": [["vvvv", "vvvv"], ["vvvv", "vvvv"]],
       "back": [["s", "s"], ["s", "s"]],
       "pos": "tt", "put": ["ss", "ss"], "cap": ["xx", "xx"], "tab": "vv", "size": [2, 1], "carry": ["ka", "ak"], "moves": 210000, "heat": 200.0,
       "early": True, "zero": 0, "joint": [False, False], "mp": False, "late": [1, 0], "addv": [["123", "123"], ["123", "123"]], "slow": 2.2, "mix": 0.6, "seed": 9, "narrow": ["vv", "vv"], "free": [], "dl": 2.0,
       "cuts": [[[("s", 0, 1024), ("v", 1024, 2048)], [("s", 0, 1024), ("s", 1024, 2048)]]] * 2,
       "pieces": [[(0, 2), (2, 4)], [(0, 2), (2, 3), (3, 4)]], "rounds": 1,
       "steps": [("carry", 0), ("front", 0), ("sums", 0), ("near", 0), ("count", 0), ("early", 0), ("carry", 1), ("front", 1),
                 ("near", 1), ("late", 0), ("sums", 1), ("count", 1), ("early", 1), ("late", 1), ("put", 0), ("put", 1),
                 ("heads", 1), ("cap", 1), ("first", 1), ("heads", 0), ("cap", 0), ("first", 0), ("lists", 0), ("lists", 1)],
       "far": [50000.0, 12000.0]}

SCRATCH = {}
WIDE = all(x == "123" for y in OPT["addv"] for x in y)
NZ = 512
NST = 1024 if "v" in OPT["put"][0] else 256
SCRATCH = {
    "Y0": ("sbuf", [128, 8, 512] if OPT["pos"] == "tt" else [128, 2 * H], "bfloat16"), "Y1": ("sbuf", [128, 2 * H], "bfloat16"),
    "wc": ("sbuf", [128, 4], "float32"), "ws": ("sbuf", [128, 4], "float32"),
    "pI": ("sbuf", [128, 8], "int32"), "pF": ("sbuf", [128, 32], "float32"), "p0": ("sbuf", [128, 4], "int32"),
    "IC": ("sbuf", [128, 144], "float32"), "KEY": ("sbuf", [128, 128], "float32"), "JG": ("sbuf", [128, 128], "float32"),
    "I2": ("sbuf", [128, 4, 64], "bfloat16"), "CS": ("sbuf", [128, H], "bfloat16"), "WS": ("sbuf", [128, H], "bfloat16"),
    "ID": ("sbuf", [128, 4, 32], "bfloat16"), "NID": ("sbuf", [128, 128], "bfloat16"), "N16": ("sbuf", [128, 128], "bfloat16"),
    "ZR": ("sbuf", [128, NZ], "bfloat16"), "TA": ("sbuf", [128, 128], "float32"), "TQ": ("sbuf", [128, 128], "bfloat16"), "TR": ("sbuf", [128, 128], "float32"),
    "HD": ("sbuf", [128, 256], "float32"), "HC": ("sbuf", [128, 32], "float16"),
    "ZW": ("sbuf", [128, 144], "bfloat16"), "GW": ("sbuf", [128, 128], "bfloat16"),
    "U2": ("sbuf", [128, 8, 256], "bfloat16"),
    "mB": ("sbuf", [128, 256], "bfloat16"), "mF": ("sbuf", [128, 384], "float32"), "mC": ("sbuf", [128, PF], "bfloat16"),
    "ST": ("sbuf", [128, NST], "bfloat16"), "LA": ("sbuf", [128, 3, 256], "bfloat16"),
    "JJ": ("sbuf", [128, 128], "float32"), "DD": ("sbuf", [128, 128], "float32"), "JH": ("sbuf", [128, 128], "float32"),
    "I64": ("sbuf", [128, 192], "float32"), "HR": ("sbuf", [128, 32], "float32"), "M8": ("sbuf", [128, 8], "float32"),
    "CO": ("sbuf", [128, 128], "float32"), "EB": ("sbuf", [128, 128], "float32"), "EE": ("sbuf", [128, 1024], "bfloat16"),
    "Z": ("sbuf", [128, 144], "float16"), "ZD": ("sbuf", [128, 144], "bfloat16"), "ZH": ("sbuf", [128, 192], "bfloat16"),
    "GH": ("sbuf", [128, 128], "bfloat16"), "TC": ("sbuf", [128, 128], "float32"), "TS": ("sbuf", [128, 128], "float32"),
    "mZ": ("sbuf", [128, WC // 3], "float32"), "mN": ("sbuf", [128, 512], "bfloat16"), "NEG": ("sbuf", [128, H], "bfloat16"),
}
for _h in range(2):
    SCRATCH.update({
        "R%d" % _h: ("sbuf", [128, 144], "bfloat16"), "PM%d" % _h: ("sbuf", [128, 144], "bfloat16"),
        "SI%d" % _h: ("sbuf", [128, 256], "int32"),
        "LP%d" % _h: ("sbuf", [128, 128], "uint16"), "HE%d" % _h: ("sbuf", [128, 32], "uint16"),
        "YS%d" % _h: ("sbuf", [128, W], "bfloat16"), "YR%d" % _h: ("sbuf", [128, W], "bfloat16"), "CY%d" % _h: ("sbuf", [128, 256], "bfloat16"),
        "SX%d" % _h: ("sbuf", [128, 4, 32], "bfloat16"), "SL%d" % _h: ("sbuf", [128, 128], "uint16"),
        "YL%d" % _h: ("sbuf", [128, H], "bfloat16"), "CK%d" % _h: ("sbuf", [128, 256], "bfloat16"),
        "XF%d" % _h: ("sbuf", [128, H], "float32"),
        "TB%d" % _h: ("sbuf", [128, 512], "bfloat16"), "LD%d" % _h: ("sbuf", [128, 3, 256], "bfloat16"),
        "M%d" % _h: ("psum", [128, 16, 32], "float32"), "QB%d" % _h: ("psum", [128, 256, 2], "float32"),
    })
    if OPT["pos"][_h] == "t":
        SCRATCH.update({
            "X%d" % _h: ("sbuf", [128, 16, 128], "bfloat16"),
            "DI%d" % _h: ("sbuf", [128, 128], "int32"), "DB%d" % _h: ("sbuf", [128, 8, 32], "bfloat16"),
            "LK%d" % _h: ("sbuf", [128, 128], "uint16"),
            "TL": ("sbuf", [128, 2, 384], "bfloat16"), "OH": ("sbuf", [128, 16, 16, 32], "bfloat16"),
            "PH%d" % _h: ("sbuf", [128, 2, 256], "float16"), "TT%d" % _h: ("sbuf", [128, H], "float32"),
            "G2%d" % _h: ("sbuf", [128, H], "float16"),
            "EA%d" % _h: ("sbuf", [128, 64, 32], "bfloat16"), "EQ%d" % _h: ("sbuf", [128, 64, 32], "bfloat16"),
            "XE%d" % _h: ("sbuf", [128, 128], "float16"), "XT%d" % _h: ("sbuf", [128, 4, 32], "float16"),
            "TU%d" % _h: ("sbuf", [128, 512], "float32"), "PQ%d" % _h: ("sbuf", [128, 16, 32], "float32" if WIDE else "float16"),
            "HQ%d" % _h: ("sbuf", [128, 24, 2], "float16"), "NR%d" % _h: ("sbuf", [128, 128], "bfloat16"), "LN%d" % _h: ("sbuf", [128, 128], "uint16"),
            "D%d" % _h: ("psum", [128, 16, 32], "float32"), "QA%d" % _h: ("psum", [128, 16, 32], "float32"),
        })
    else:
        SCRATCH.update({
            "X%d" % _h: ("sbuf", [128, H], "bfloat16"), "DI%d" % _h: ("sbuf", [128, 512], "int32"), "DB%d" % _h: ("sbuf", [128, 512], "bfloat16"),
            "IH%d" % _h: ("sbuf", [128, H], "bfloat16"), "IL%d" % _h: ("sbuf", [128, H], "float32"),
            "TO%d" % _h: ("sbuf", [128, 4], "float32"), "BS%d" % _h: ("sbuf", [128, 4], "float32"), "BL%d" % _h: ("sbuf", [128, 2], "uint16"),
            "CU%d" % _h: ("sbuf", [128, H], "float16"), "PR%d" % _h: ("sbuf", [128, H], "float16"), "L1%d" % _h: ("sbuf", [128, 128], "uint16"),
            "SW%d" % _h: ("sbuf", [128, WC], "float32"), "SV%d" % _h: ("sbuf", [128, WC], "float32"), "CW%d" % _h: ("sbuf", [128, WC], "float32"),
            "HF%d" % _h: ("sbuf", [128, 32], "float32"), "SK%d" % _h: ("sbuf", [128, 128], "int32"),
            "PX%d" % _h: ("psum", [128, 1024], "float32"),
        })
    for _l in range(2):
        SCRATCH["WN0%d" % _h] = ("sbuf", [128, W], "float32" if OPT["put"][0][_h] == "s" else "bfloat16")
        SCRATCH["CP%d%d" % (_l, _h)] = ("sbuf", [128, W], "bfloat16")
SEMAPHORES = ["sv", "ss", "sp", "sg", "dsa", "dsb", "dw", "dxa", "dxb", "dxf00", "dxf02", "dxf10", "dxf12", "dout", "arr0", "arr1", "sent0", "sent1",
              "arrA", "sentA", "dneg", "dsj0", "dsj1", "dz00", "dz01", "dz10", "dz11"]
SEMAPHORES += ["f%s%d%d" % (_k, _l, _h) for _k in ("WN", "CP") for _l in range(2) for _h in range(2)]
BANKS = [_k for _k in SCRATCH if SCRATCH[_k][0] == "psum"]


def polish(order, fixed, queue, before, users, busy, tail, moves):
    N, L = len(busy), len(order)
    preds, succs = [set(d for d, x in b) for b in before], [set(u for u, x in b) for b in users]
    seed = [OPT["seed"]]

    def draw():
        seed[0] = (seed[0] * 1103515245 + 12345) % 2147483648
        return seed[0] / 2147483648.0

    names = sorted(set(queue))
    queue = [-1 if q == "x" else names.index(q) for q in queue]
    cases = []
    for slow in (1.0, OPT["slow"]):
        b, rest = [x * slow if names[q] == "p" and q >= 0 else x for x, q in zip(busy, queue)], [0.0] * N
        for i in range(N - 1, -1, -1):
            rest[i] = max([tail[i]] + [x + b[u] + rest[u] for u, x in users[i]])
        cases.append((b, rest))
    ends = [i for i in order if not users[i] or tail[i] >= 0.0 > min(tail)]
    mix = OPT["mix"]

    def both(order, lo, old, limit):
        a = length(order, lo, old[0][2], old[0][3], (limit - mix * 0.98 * old[1][0]) / (1 - mix), *cases[0])
        b = a and (length(order, lo, old[1][2], old[1][3], (limit - (1 - mix) * a[0]) / mix, *cases[1]) if mix else a)
        return b and (a, b)

    def length(order, lo, fin, cause, limit, busy, rest):
        fin, cause, last = fin[:], cause[:], [-1] * (len(names) + 1)
        for i in order[:lo]:
            last[queue[i]] = i
        for i in order[lo:]:
            t, c, q = 0.0, -1, queue[i]
            for d, x in before[i]:
                if fin[d] + x > t:
                    t, c = fin[d] + x, d
            if q >= 0:
                j = last[q]
                if j >= 0 and fin[j] > t:
                    t, c = fin[j], -2 - j
                last[q] = i
            t += busy[i]
            if t + rest[i] > limit:
                return None
            fin[i], cause[i] = t, c
        e = max(ends, key=lambda i: fin[i] + tail[i])
        end, pairs = fin[e] + tail[e], []
        while e >= 0:
            c = cause[e]
            if c <= -2:
                c = -2 - c
                pairs.append((c, e))
            e = c
        return end, pairs, fin, cause

    held = both(order, 0, [(0.0, [], [0.0] * N, [-1] * N)] * 2, 1e18)
    now = (1 - mix) * held[0][0] + mix * held[1][0]
    best, pos = (now, order), {v: j for j, v in enumerate(order)}
    for k in range(moves):
        pairs = held[k % 2][1]
        if pairs and draw() < 0.7:
            a, b = pairs[int(draw() * len(pairs))]
            far = (0, 0, 0, 3, 10, 30)[int(draw() * 6)]
            v, to = (b, pos[a] - far) if draw() < 0.5 else (a, pos[b] + far)
        else:
            v = order[fixed + int(draw() * (L - fixed))]
            to = pos[v] + int((draw() + draw() - 1.0) * 60)
        to, p = max(fixed, min(L - 1, to)), pos[v]
        if p < fixed:
            continue
        lo, hi = min(to, p), max(to, p) + 1
        part, need = order[lo:hi], {v}
        for u in (reversed(part) if to < p else part):
            if u in need:
                need |= (preds if to < p else succs)[u]
        go, stay = [u for u in part if u in need], [u for u in part if u not in need]
        part = go + stay if to < p else stay + go
        new = order[:lo] + part + order[hi:]
        got = both(new, lo, held, now - math.log(draw() + 1e-9) * (OPT["heat"] * (1.0 - k / moves) ** 2 + 2.0))
        if got:
            order, held = new, got
            now = (1 - mix) * held[0][0] + mix * held[1][0]
            for j, u in enumerate(part):
                pos[u] = lo + j
            if now < best[0]:
                best = (now, order)
    return best[1]


def collect(g, T, topo, rank):
    n = len(T.cores)
    tag, names, step = [""], {}, [1e9]

    def at(name, l, h):
        step[0] = 100 * l + OPT["steps"].index((name, h))
    O = OPT
    Q = {"v": g.vector, "s": g.scalar, "p": g.tensor, "g": g, "y": g.sync}
    V, S, P = g.vector, g.scalar, g.tensor
    calls = []
    wr, rd = {}, {}
    cnt = {}

    def add(q, r, w, busy, lag, emit, soft=()):
        deps = set()
        turns = [k for k in w if k[0] == "~"]
        soft = list(soft) + [(k, 0.0) for k in turns if k in wr]
        w = [k for k in w if k not in turns]
        for k in list(r) + list(w):
            if k in wr and k in w and calls[wr[k]]["q"] == q and (k in BANKS or k in O["free"]):
                soft.append((k, 0.0))
            elif k in wr:
                deps.add(wr[k])
        for k in w:
            deps.update(rd.get(k, []))
        me = len(calls)
        nm = tag[0] + q + (w or r)[-1]
        names[nm] = names.get(nm, -1) + 1
        calls.append({"name": "%s.%d" % (nm, names[nm]), "step": step[0], "q": q, "deps": deps, "busy": busy, "lag": lag, "emit": emit, "soft": [(wr[k], d) for k, d in soft]})
        for k in r:
            rd.setdefault(k, []).append(me)
        for k in w + turns:
            wr[k] = me
            rd[k] = []

    def op(q, r, w, els, fn):
        def emit():
            s = "s" + q
            fn().then_inc(T.sem[s], 1)
            cnt[s] = cnt.get(s, 0) + 1
            return (s, cnt[s])
        add(q, r, w, els * O["pe"] if q == "p" else {"v": 55, "s": 65, "g": 150}[q] + 0.83 * max(64, els), O["hop"], emit)

    def dmas(q, s, r, w, pairs, lag):
        def emit():
            for o, i in pairs:
                Q[q].dma_start(o, i).then_inc(T.sem[s], 16)
                cnt[s] = cnt.get(s, 0) + 16
            return (s, cnt[s])
        add(q, r, w, 60 * len(pairs), lag, emit)

    def mm(r, w, cycles, triples):
        def run():
            for grp in triples:
                for i, (o, a, b) in enumerate(grp):
                    m = P.matmul(o, a, b, i == 0, i == len(grp) - 1)
            return m
        op("p", r, w, cycles, run)

    def mm_part(r, w, cycles, grp, start, stop):
        def run():
            for i, (o, a, b) in enumerate(grp):
                m = P.matmul(o, a, b, start and i == 0, i >= len(grp) - int(stop))
            return m
        op("p", r, w, cycles, run)

    sig, gam = O["sig"], O["gam"]

    for h in range(2):
        si, src = T["SI%d" % h], T.slot[:, H * h:H * h + H]
        dmas("ys"[h], "ds" + "ab"[h], [], ["SI%d" % h],
             [(si[:, 0:128], src)] if O["pos"][h] == "t" else [(si[64 * f:64 * f + 64, :], src) for f in range(2)], 2300)
    dmas("y", "dxa", [], ["X0"], [(T.X0[:], T.x[:, 0:H])], 4500)
    dmas("y", "dxb", [], ["X1"], [(T.X1[:], T.x[:, H:2 * H])], 6000)
    dmas("y", "dw", [], ["wc"], [(T.wc[:, 0:1], T.w[:])], 2500)

    fl = {"allow_small_or_imprecise_dtypes": True}

    def iota(k, o, els, pattern, base, cm=0):
        op("g", [], [k], 2 * els, lambda: g.iota(o, pattern, base, cm, **fl))
    op("g", [], ["p0"], 1, lambda: g.iota(T.p0[:, 0:1], [[0, 1]], 0, 1))
    iota("IC", T.IC[:], 144, [[1, 144]], 0)
    iota("KEY", T.KEY[:], 128, [[64, 4], [1, 16], [32, 2]], 0)
    iota("JG", T.JG[:], 128, [[16, 8], [0, 16]], 15)
    iota("ZR", T.ZR[:], NZ, [[0, NZ]], 0)
    iota("mB", T.mB[:], 256, [[0, 256]], -1)
    iota("mF", T.mF[:], 384, [[0, 384]], -1)
    iota("mC", T.mC[:], PF, [[0, PF]], 1)
    op("g", ["mC"], ["HD"], 512, lambda: g.affine_select(T.HD[:], T.mC[:, 0:256], [[0, 16], [1, 16]], A.is_equal, 0.0, 0, 0))
    for q in range(0, NST, 256):
        op("g", ["mC"], ["ST"], 512, lambda q=q: g.affine_select(T.ST[:, q:q + 256], T.mC[:, 0:256], [[0, 256]], A.is_gt, SC, 0, 0))
    dmas("y", "dneg", ["ZR", "SI0"], ["U2"], [(T.U2[:, 2 * j:2 * j + 2, :], T.ZR[:]) for j in range(4)], O["dl"] * 2500)
    iota("JJ", T.JJ[:], 128, [[8, 8], [0, 16]], 0)
    iota("DD", T.DD[:], 128, [[0, 8], [1, 16]], 0)
    iota("M8", T.M8[:], 8, [[1, 8]], 0)
    iota("I64", T.I64[:], 192, [[0, 3], [1, 64]], 0)
    iota("JH", T.JH[:], 128, [[0, 2], [8, 8], [0, 8]], 7)
    iota("HR", T.HR[:], 32, [[0, 2], [1, 16]], int(CEN))
    iota("mZ", T.mZ[:], WC // 3, [[0, WC // 3]], 0)
    iota("mN", T.mN[:], 512, [[0, 512]], -2048)
    dmas("y", "dneg", ["mN", "X0"], ["NEG"], [(T.NEG[:, 512 * j:512 * j + 512], T.mN[:]) for j in range(4)], 3500)

    def fill(l, h, after):
        k, m = "WN%d%d" % (l, h), "mF" if O["put"][l][h] == "s" else "mB"
        if l == 0:
            if h:
                dmas("y", "f" + k, ["mF"] + after, [k], [(T[k][:, 384 * j:384 * j + 384], T.mF[:]) for j in range(6)], O["dl"] * 4000)
            for q in range(2 - 2 * h):
                iota(k, T[k][:, HW * q:HW * q + HW], HW, [[0, HW]], -1)
        if O["cap"][l][h] == "x":
            k = "CP%d%d" % (l, h)
            dmas("y", "f" + k, ["mC"] + after, [k + "0", k + "1", "~cap"], [(T[k][:, PF * j:PF * j + PF], T.mC[:]) for j in range(3)], O["dl"] * 3500)
    fill(0, 0, ["X1"]); fill(0, 1, ["X1"])

    masks = [127, 15] + [16, 1, 30, 96] * ("t" in O["pos"]) + [7, 56] * ("r" in O["pos"])

    def low_bits(j, m):
        op("v", ["p0"], ["pI%d" % j], 1, lambda: V.tensor_scalar(T.pI[:, j:j + 1], T.p0[:, 0:1], m, None, A.bitwise_and))
    for j, m in enumerate(masks):
        low_bits(j, m)
    nm = len(masks)
    op("v", ["pI%d" % j for j in range(nm)], ["pF"], 1, lambda: V.tensor_copy(T.pF[:, 0:nm], T.pI[:, 0:nm]))
    pp, p15, p16, p1, p30, p96, p7, p56 = (T.pF[:, masks.index(m):masks.index(m) + 1] if m in masks else None for m in (127, 15, 16, 1, 30, 96, 7, 56))
    col = {}

    def column(k, r, a, s1, s2, o0, o1):
        c = col[k] = T.pF[:, 8 + len(col):9 + len(col)]
        op("v", ["pF"] + r, [k], 1, lambda: V.tensor_scalar(c, a, s1, s2, o0, o1))
    column("odd", [], p16, 0.0625, 0.0, A.mult, A.add)
    column("even", [], p16, -0.0625, 1.0, A.mult, A.add)
    column("zc", [], pp, p15, 15.0, A.subtract, A.add)
    column("c1", [], pp, p16, 16.0, A.subtract, A.add)
    column("n1", [], p1, -1.0, 1.0, A.mult, A.add)
    column("d0", [], p30, 0.5, p96, A.mult, A.add)
    column("dest", ["d0"], p1, 16.0, col["d0"], A.mult, A.add)
    column("klo", [], p30, 0.5, 0.0, A.mult, A.add)
    column("k1", [], p1, 16.0, p96, A.mult, A.add)
    column("k0", ["k1"], col["k1"], 2.0, 0.0, A.mult, A.add)
    column("t0", [], p15, 15.0, 2304.0, A.is_equal, A.mult)
    column("t1", [], pp, 127.0, -1151.0, A.is_equal, A.mult)

    def match(k, o, src, sk, c, ck, mul, mk):
        op("v", [sk, ck] + mk, [k], 144, lambda: V.tensor_scalar(o, src, c, mul, A.is_equal, A.mult))
    match("ID", T.ID[:], T.IC[:, 0:128], "IC", pp, "pF", 1.0, [])
    op("s", ["ID"], ["NID"], 128, lambda: S.activation(T.NID[:], T.ID[:], F.Identity, scale=-1.0))
    op("s", ["ID"], ["N16"], 128, lambda: S.activation(T.N16[:], T.ID[:], F.Identity, scale=-16.0))
    iota("I2", T.I2[:], 256, [[0, 256]], 1)
    op("g", [], ["I2"], 512, lambda: g.affine_select(T.I2[:], T.I2[:], [[32, 4], [0, 2], [1, 32]], A.is_equal, 0.0, 0, -1))
    for b in range(4):
        for d in range(4 * b, 4 * b + 4):
            op("s", ["I2"], ["CT%d" % d], 128, lambda d=d: S.activation(T.CS[:, 128 * d:128 * d + 128], T.I2[:, :, d + 1:d + 33], F.Identity))
        o = T.CS[:, 512 * b:512 * b + 512]
        op("g", ["CT%d" % d for d in range(4 * b, 4 * b + 4)], ["CS%d" % b], 1024,
           lambda o=o: g.affine_select(o, o, [[0, 4], [1, 128]], A.not_equal, -1.0, 0, -1))
    for q in range(2):
        r, pm = T["R%d" % q], T["PM%d" % q]
        iota("R%da" % q, r[:, 0:16], 16, [[0, 16]], 0)
        op("g", ["mC", "R%da" % q], ["R%d" % q], 256, lambda r=r, q=q: g.affine_select(
            r[:, 16:144], T.mC[:, 0:128], [[-32, 4], [-1000, 2], [-1, 16]], A.is_equal, 0.0, -16 * q, 1))
        iota("PM%da" % q, pm[:, 128:144], 16, [[0, 16]], 0)
        op("g", ["mC", "PM%da" % q], ["PM%d" % q], 256, lambda pm=pm, q=q: g.affine_select(
            pm[:, 0:128], T.mC[:, 0:128], [[-32, 4], [1000, 2], [-2, 16]], A.is_equal, 0.0, -1001 * q, 1))
    op("v", ["KEY", "klo", "k0"], ["TA"], 128, lambda: V.tensor_scalar(T.TA[:], T.KEY[:], col["k0"], col["klo"], A.subtract, A.is_gt))
    op("v", ["KEY", "k0"], ["TR"], 128, lambda: V.tensor_scalar(T.TR[:], T.KEY[:], col["k0"], 15.0, A.subtract, A.is_le))
    op("v", ["TA", "TR"], ["TQ"], 256, lambda: V.tensor_tensor(T.TQ[:], T.TR[:], T.TA[:], A.mult))
    op("g", [], ["HD"], 1, lambda: g.iota(T.HD[:, 0:1], [[0, 1]], -1024, 0, **fl))
    column("kc", [], p30, 512.5, 1.0 - CEN, A.mult, A.add)
    op("v", [], ["HC0"], 1, lambda: V.memset(T.HC[:, 0:16], -1.0))
    op("v", [], ["HC1"], 1, lambda: V.memset(T.HC[:, 16:31], -2.0))
    op("v", ["t0", "t1"], ["HC2"], 1, lambda: V.tensor_scalar(T.HC[:, 31:32], col["t0"], col["t1"], -2.0, A.add, A.add))
    op("s", ["wc"], ["ws0"], 1, lambda: S.activation(T.ws[:, 0:1], T.wc[:, 0:1], F.Identity, scale=1.0 / SC))
    op("s", ["wc"], ["ws1"], 1, lambda: S.activation(T.ws[:, 1:2], T.wc[:, 0:1], F.Identity, scale=-1.0 / SC))
    match("ZW", T.ZW[:], T.IC[:], "IC", col["zc"], "zc", T.ws[:, 0:1], ["ws0"])
    match("GW", T.GW[:], T.JG[:], "JG", col["zc"], "zc", T.ws[:, 1:2], ["ws1"])
    for u in ("U2",):
        op("s", ["ID"], [u], 128, lambda u=u: S.activation(T[u][:, :, 0:256:17], T.ID[:], F.Identity))
    op("v", [], ["CO1"], 128, lambda: V.memset(T.CO[64:128, :], -1.0))
    op("v", ["DD"], ["CO0"], 128, lambda: V.tensor_scalar(T.CO[0:64, :], T.DD[0:64, :], 2.0, None, A.mult))
    op("v", ["JJ", "pF"], ["EB"], 128, lambda: V.tensor_scalar(T.EB[:], T.JJ[:], p56, None, A.is_equal))
    op("v", ["M8", "pF"], ["M8"], 8, lambda: V.tensor_scalar(T.M8[:], T.M8[:], p7, None, A.is_equal))
    op("v", ["EB", "CO0", "CO1"], ["EB"], 256, lambda: V.tensor_tensor(T.EB[:], T.EB[:], T.CO[:], A.mult))
    for i in range(8):
        o, m = T.EE[:, 128 * i:128 * i + 128], T.M8[:, i:i + 1]
        if i % 2:
            op("s", ["EB", "M8"], ["EE%d" % i], 128, lambda o=o, m=m: S.activation(o, T.EB[:], F.Identity, scale=m))
        else:
            op("v", ["EB", "M8"], ["EE%d" % i], 128, lambda o=o, m=m: V.tensor_scalar(o, T.EB[:], m, None, A.mult))
    column("dsq", [], p15, p15, -1.0, A.mult, A.mult)
    column("b1", ["dsq"], col["dsq"], 1.0, 1.0, A.mult, A.add)
    column("b16", ["dsq"], col["dsq"], 16.0, 16.0, A.mult, A.add)
    column("c2", [], p15, 16.0, -CEN, A.mult, A.add)
    column("d16", [], p15, 16.0, 0.0, A.mult, A.add)
    column("zh", ["zc"], col["zc"], 0.5, -0.5, A.mult, A.add)
    op("v", ["IC", "pF"], ["TC"], 128, lambda: V.tensor_scalar(T.TC[:], T.IC[:, 0:128], pp, None, A.is_gt))
    op("v", ["IC", "zc"], ["TS"], 128, lambda: V.tensor_scalar(T.TS[:], T.IC[:, 0:128], col["zc"], None, A.is_le))
    op("v", ["TC", "TS"], ["TS"], 256, lambda: V.tensor_tensor(T.TS[:], T.TS[:], T.TC[:], A.mult))
    match("Z", T.Z[:], T.IC[:], "IC", col["zc"], "zc", 1.0, [])
    match("ZD", T.ZD[:], T.IC[:], "IC", col["zc"], "zc", col["d16"], ["d16"])
    match("ZH", T.ZH[:], T.I64[:], "I64", col["zh"], "zh", T.ws[:, 0:1], ["ws0"])
    match("GH", T.GH[:], T.JH[:], "JH", col["zh"], "zh", T.ws[:, 1:2], ["ws1"])

    def front(l, h):
        M, mk = T["M%d" % h], "M%d" % h
        si, di, db, lk = (T["%s%d" % (k, h)] for k in ("SI", "DI", "DB", "LK"))

        def K(s):
            return "%s%d" % (s, h)

        at("front", l, h)
        if l == 1:
            for a in (0, 2):
                grp = [(M[:, 0:4, :], T.GW[:], T.ST[:, 0:128])] if a == 0 else []
                grp += [(M[:, a:a + 2, :], T.ZW[:, 15 - j:143 - j], T.Y0[:, 4 * h + a:4 * h + a + 2, 32 * j:32 * j + 32]) for j in range(16)]
                mm_part(["ZW", "GW", "ST", "Y0%d%d" % (h, a), "Y0%d%d" % (h, a + 1)], [mk], 1024 + 128 * (a == 0), grp, a == 0, a == 2)
            op("v", [], [mk, K("DI")], 128, lambda: V.tensor_copy(di[:], M[:, 0:4, :]))
            op("v", [K("DI")], [K("SI")], 128, lambda: V.tensor_scalar(si[:, 0:128], di[:], 255, None, A.bitwise_and))
            op("v", [K("DI")], [K("SJ")], 128, lambda: V.tensor_scalar(si[:, 128:256], di[:], 4, 15, A.arith_shift_right, A.bitwise_and))
        else:
            op("v", [K("SI")], [K("SJ")], 128, lambda: V.tensor_scalar(si[:, 128:256], si[:, 0:128], 4, None, A.arith_shift_right))
        op("v", [K("SI"), K("SJ")], [K("DS"), K("DH")], 256, lambda: V.tensor_copy(db[:], si[:]))
        op("v", [K("DS"), "odd"], [K("LK")], 64, lambda: V.tensor_scalar(lk[:], db[:, 0:4, :], 2.0, col["odd"], A.mult, A.add))
        mm([K("DS"), K("DH"), "ID", "N16"], [mk], 512,
           [[(M[:, 8:12, :], db[:, 0:4, :], T.ID[:]), (M[:, 8:12, :], db[:, 4:8, :], T.N16[:])],
            [(M[:, 12:16, :], db[:, 4:8, :], T.ID[:])], [(M[:, 4:8, :], db[:, 0:4, :], T.ID[:])]])
        op("s", [], [mk, K("TL")], 384, lambda: S.activation(T.TL[:, h, :], M[:, 4:16, :], F.Identity))
        a, b = (0, 2) if O["joint"][l] else (h, h + 1)
        for d in range(16 * (b == h + 1)):
            op("v", ["TL%d" % x for x in range(a, b)], ["OH%d_%d" % (d, x) for x in range(a, b)] + ["~oh"], 128 * (b - a),
               lambda d=d: V.tensor_scalar(T.OH[:, 8 * a:8 * b, d, :], T.TL[:, a:b, 128:384], float(d), None, A.is_equal))

    def places(l, h):
        M, D, QA, QB = (T["%s%d" % (k, h)] for k in ("M", "D", "QA", "QB"))
        mk, dk, ak, bk = ("%s%d" % (k, h) for k in ("M", "D", "QA", "QB"))
        db, lk, ph, tt, ea, eq, xe, xt = (T["%s%d" % (k, h)] for k in ("DB", "LK", "PH", "TT", "EA", "EQ", "XE", "XT"))

        def K(s):
            return "%s%d" % (s, h)

        def oh(rows, x, digits, j):
            return T.OH[0:rows, 8 * h + x, digits, j:32:16]
        ohk, every = [K("OH%d_" % d) for d in range(16)], slice(0, 16)

        at("near", l, h)
        for b, (bank, key) in enumerate(((D, dk), (QA, ak), (D, dk), (QA, ak))):
            mm([K("TL"), "CS%d" % b], [key], 512,
               [[(bank[:, 4 * i:4 * i + 4, :], T.CS[:, 512 * b + 128 * i:512 * b + 128 * i + 128], T.TL[:, h, 0:128])] for i in range(4)])
            rows = slice(16 * b, 16 * b + 16)
            how = O["near"][l][h]
            if how == "v":
                op("v", [], [key, K("EQ%d_" % b)], 512, lambda bank=bank, rows=rows: V.tensor_scalar(eq[:, rows, :], bank[:], 0.0, None, A.is_equal))
            else:
                op("s", [], [key, K("EA%d_" % b)], 512, lambda bank=bank, rows=rows: S.activation(ea[:, rows, :], bank[:], F.Abs))
                if how == "sv":
                    op("v", [K("EA%d_" % b)], [K("EQ%d_" % b)], 256, lambda rows=rows: V.tensor_scalar(eq[:, rows, :], ea[:, rows, :], 0.0, None, A.is_equal))
                elif b % 2:
                    rows = slice(16 * b - 16, 16 * b + 16)
                    op("s", [K("EA%d_" % (b - 1)), K("EA%d_" % b)], [K("EQ%d_" % (b - 1)), K("EQ%d_" % b)], 1024,
                       lambda rows=rows: S.activation(eq[:, rows, :], ea[:, rows, :], F.Relu, bias=1.0, scale=-1.0))

        at("sums", l, h)
        grps = [[(QB[32 * a:32 * a + 32, j + 1:256:16, :], oh(128, a, every, j), oh(128, 4 + a, every, j))] for j in range(15) for a in range(4)]
        grps += [[(QB[32 * a:32 * a + 32, 16:256:16, :], oh(128, a, every, 15), oh(128, 4 + a, slice(0, 15), 15))] for a in range(4)]
        grps += [[(QB[32 * a:32 * a + 32, 0, :], oh(128, a, every, 15), oh(128, 4 + a, 15, 15))] for a in range(4)]
        mm(ohk, [bk], 2176, grps)
        for c in range(2):
            op("v", ["HD"], [bk, K("PH%d_" % c)], 256,
               lambda c=c: V.tensor_tensor_scan(ph[:, c, :], T.HD[:], QB[:, :, c], 0.0, A.add, A.add))
        mm([K("PH0_"), K("PH1_"), "TQ", "NID"], [bk], 128, [[(QB[:, 0, :], T.TQ[:], ph[:, :, 255]), (QB[:, 0, :], T.NID[:], ph[:, :, 0])]])
        pq, phk = T[K("PQ")], [K("PQ0_"), K("PQ1_")]
        for c in range(2):
            op("v", [K("PH%d_" % c), "kc"], [bk, phk[c]], 256 if WIDE else 128, lambda c=c: V.tensor_scalar(
                pq[:, :, 16 * c:16 * c + 16], ph[:, c, :], QB[:, 0, c:c + 1], col["kc"], A.add, A.add))
        hq = T[K("HQ")]
        if l == 0:
            op("v", ["ZR"], [K("HQ")], 32, lambda: V.tensor_copy(hq[:], T.ZR[:, 0:48]))
        op("v", phk, [K("HQ")], 32, lambda: V.tensor_copy(hq[:, 0:16, :], pq[:, :, 0:32:16]))

        def heads():
            at("heads", l, h)
            grp = [(QB[:, 0:16, :], T.ID[:], T.HC[:])]
            for c in range(2):
                pm = T["PM%d" % c]
                grp += [(QB[:, 0:8, :], pm[:, 0:128], hq[:, 0:16, c]), (QB[:, 8:16, :], pm[:, 0:128], hq[:, 1:17, c]),
                        (QB[:, 15, 1:2], pm[:, 1:129], hq[:, 0, c:c + 1])]
            mm([K("HQ"), "PM0", "PM1", "HC0", "HC1", "HC2", "ID"], [bk], 450, [grp])
            op("v", [], [bk, K("HE")], 32, lambda: V.tensor_scalar(T[K("HE")][:], QB[:, 0:16, :], CEN + 0.25, None, A.add))

        at("count", l, h)
        for b in range(4 * l):
            mm_part([K("EQ%d_" % b), "WS%d" % b], [mk], 512,
                    [(M[:, 0:4, :], eq[:, 16 * b + 4 * i:16 * b + 4 * i + 4, :], T.WS[:, 512 * b + 128 * i:512 * b + 128 * i + 128]) for i in range(4)],
                    b == 0, b == 3)
        for b in range(4 - 4 * l):
            grp = [(M[:, 0:4, :], T.ID[:], T.ZR[:, 0:128])] if b == 0 else []
            for i in range(4):
                d, e = 4 * b + i + 1, eq[:, 16 * b + 4 * i:16 * b + 4 * i + 4, :]
                grp.append((M[:, 0:4, d:32], e, T.ID[:, :, 0:32 - d]))
                if d < 16:
                    grp.append((M[:, 0:4, 32 - d:32], e, T.ID[:, :, 32 - d:32]))
            mm_part([K("EQ%d_" % b), "ZR", "ID"], [mk], 650, grp, b == 0, b == 3)
        op("s", [], [mk, K("NR")], 128, lambda: S.activation(T[K("NR")][:], M[:, 0:4, :], F.Identity))

        who = O["look"][l][h]
        for i in range(4):
            at("early" if i < O["pieces"][h][0][1] else "late", l, h)
            bank, key = ((D, dk), (QA, ak))[i % 2]
            counts = [(bank[32 * a:32 * a + 32, :, j:32:16], oh(32 * i, a, every, j), oh(32 * i, 4 + a, every, j))
                      for j in range(16 if i else 0) for a in range(4)]
            c = slice(512 * i, 512 * i + 512)
            if WIDE and i == 0:
                op("v", phk, [K("TT0_")], 512, lambda c=c: V.transpose(tt[:, c], pq[:]))
            elif str(i) in O["addv"][l][h]:
                mm(ohk, [key], 2048, [[x] for x in counts])
                ts = T[K("TU")]
                op("v", phk, [key, K("TU")], 512, lambda bank=bank: V.tensor_tensor(ts[:], bank[:], pq[:], A.add))
                bank, key = ts, K("TU")
            elif i == 0 or i > O["zero"]:
                mm_part(ohk + phk + ["ID"], [key], 2560 if i else 512, [(bank[:], T.ID[:], pq[:])] + counts, True, 4 if i else 1)
            else:
                mm_part(ohk + ["ZR", "ID"], [key], 2560, [(bank[:], T.ID[:], T.ZR[:])] + counts, True, False)
                mm_part(phk + ["ID"], [key], 512, [(bank[:], T.ID[:], pq[:])], False, True)
            if i or not WIDE:
                op("v", [], [key, K("TT%d_" % i)], 512, lambda bank=bank, c=c: V.transpose(tt[:, c], bank[:]))
            win = tt[:, c].indirect(lk[:, 32 * i:32 * i + 32])
            if who[i] == "s":
                op("s", [K("TT%d_" % i), K("LK")], [K("G%d_" % i)], gam * 512, lambda c=c, win=win: S.activation(T[K("G4")][:, c], win, F.Identity))
            else:
                op("v", [K("TT%d_" % i), K("LK")], [K("G%d_" % i)], gam * 512, lambda c=c, win=win: V.tensor_copy(T[K("G2")][:, c], win))
            for a, b in O["pieces"][h]:
                if b != i + 1:
                    continue
                gk, uk = (K("G4"), "U4") if who[a] == "s" else (K("G2"), "U2")
                grp = [(M[:, a:b, :], T.ID[:], T[K("NR")][:, 32 * a:32 * b])]
                grp += [(M[:, a:b, :], T[uk][:, :, j:256:16], T[gk][:, 512 * a + j:512 * b:16]) for j in range(16)]
                mm([K("G%d_" % x) for x in range(a, b)] + [uk, K("NR")], [mk], 64 + 1024 * (4 if who[a] == "s" else 1), [grp])
                c = slice(32 * a, 32 * b)
                op("v", [], [mk, K("XE%d_" % a)], 64, lambda a=a, b=b, c=c: V.tensor_copy(xe[:, c], M[:, a:b, :]))
                op("v", [K("XE%d_" % a)], [K("XT%d_" % a)], 64, lambda a=a, b=b, c=c: V.transpose(xt[:, a:b, :], xe[:, c]))
                to_list(h, xt, [K("XT%d_" % a)], a, b, "LP", CEN + 0.25, False)
                if (a == 0, b == 4)[O["late"][h]]:
                    heads()
        at("lists", l, h)
        if l == 1:
            to_list(h, xt, [K("XT%d_" % a) for a, b in O["pieces"][h]], 0, 4, "LN", CEN + 0.25, True)
        if O["carry"][l][h] == "k" and (rank or h):
            op("v", [K("DS")], [K("SX")], 64, lambda: V.transpose(T[K("SX")][:], db[:, 0:4, :]))
            to_list(h, T[K("SX")], [K("SX")], 0, 4, "SL", 0.25, l == 1)

    def radix(l, h):
        M, QB, mk, bk = T["M%d" % h], T["QB%d" % h], "M%d" % h, "QB%d" % h
        si, di, db, ih, il, to, bs, cu, pr, cw = (T["%s%d" % (k, h)] for k in ("SI", "DI", "DB", "IH", "IL", "TO", "BS", "CU", "PR", "CW"))
        qs = ((M[:, 0:2, :], mk), (QB[:, 0:32, :], bk))

        def K(s):
            return "%s%d" % (s, h)

        at("front", l, h)
        if l == 1:
            for k in range(4):
                grp = [(M[:, 0:8, :], T.GH[:], T.ST[:, 0:256])] if k == 0 else []
                grp += [(M[:, 0:8, :], T.ZH[:, 7 - i:135 - i], T.Y0[:, H * h + 256 * i:H * h + 256 * i + 256]) for i in (2 * k, 2 * k + 1)]
                mm_part(["ZH", "GH", "ST", "Y0%d%d" % (h, k)], [mk], 512, grp, k == 0, k == 3)
            op("v", [], [mk, K("SI")], 256, lambda: V.tensor_copy(si[:], M[:, 0:8, :]))

        def indicate(d):
            c = slice(256 * d, 256 * d + 256)
            if d == 0:
                op("v", [K("SI")], [K("DI0")], 256, lambda: V.tensor_scalar(di[:, c], si[:], 4, 15, A.arith_shift_right, A.bitwise_and))
            else:
                op("v", [K("SI")], [K("DI1")], 256, lambda: V.tensor_scalar(di[:, c], si[:], 15, None, A.bitwise_and))
            op("v", [K("DI%d" % d)], [K("DB%d" % d)], 256, lambda: V.tensor_copy(db[:, c], di[:, c]))
            op("s", [K("DB%d" % d)], [K("DB%d" % d)], 256, lambda: S.activation(db[64:128, c], db[64:128, c], F.Square))
            for q in range(2):
                px, pk = T[K("PX")] if "t" in O["pos"] else T["PX%d" % q], K("PX") if "t" in O["pos"] else "PX%d" % q
                mm([K("DB%d" % d)] + ["EE%d" % (4 * q + j) for j in range(4)], [pk], 1024,
                   [[(px[:, 256 * j:256 * j + 256], T.EE[:, 512 * q + 128 * j:512 * q + 128 * j + 128], db[:, c])] for j in range(4)])
                op("s", [("b1", "b16")[d]], [pk, K("I%d%d" % (d, q)), K("TO%d" % (2 * d + q))], 1050, lambda q=q, px=px: S.activation(
                    (ih, il)[d][:, 1024 * q:1024 * q + 1024], px[:], F.Relu, bias=col[("b1", "b16")[d]], scale=(1.0, 16.0)[d],
                    accum_out=to[:, 2 * d + q:2 * d + q + 1]))

        def base(d):
            mm(["TS", K("TO%d" % (2 * d)), K("TO%d" % (2 * d + 1))], [bk], 256, [[(QB[:, 40, :], T.TS[:], to[:, 2 * d:2 * d + 2])]])
            op("v", [], [bk, K("BS%d" % (2 * d))], 2, lambda: V.tensor_reduce(bs[:, 2 * d:2 * d + 1], QB[:, 40, :], AX.X, A.add))

        def gather_mm(q, src, keys, z, start, stop):
            mm_part(keys + [z], [qs[q][1]], 1024, [(qs[q][0], T[z][:, 15 - r:143 - r], src[:, 1024 * q + r:1024 * q + 1024:16]) for r in range(16)],
                    start, stop)

        def listed(q, name, keys, mul, plus):
            op("v", [], [qs[q][1]] + keys, 64, lambda: V.tensor_scalar(T[K(name)][:, 64 * q:64 * q + 64], qs[q][0], mul, plus, A.mult, A.add))

        indicate(0)
        at("near", l, h)
        indicate(1)
        at("sums", l, h)
        base(0)
        op("v", [K("BS0"), K("I00"), K("I01")], [K("CU")], 1024, lambda: V.tensor_tensor_scan(cu[:], ih[:], ih[:], bs[:, 0:1], A.add, A.max))
        for q in range(2):
            c = slice(1024 * q, 1024 * q + 1024)
            op("v", [K("CU"), K("I0%d" % q)], [K("PR%d" % q)], 512, lambda c=c: V.tensor_tensor_scan(pr[:, c], cu[:, c], ih[:, c], 0.0, A.max, A.mult))
            gather_mm(q, pr, [K("PR%d" % q)], "Z", True, True)
            listed(q, "L1", [K("L1%d" % q)], 1.0, 0.25)
        at("count", l, h)
        cuts = O["cuts"][l][h]
        both = any(e == "v" for e, a, b in cuts)
        if both:
            z = WC // 3
            dmas("y", "dz%d%d" % (l, h), ["mZ"], [K("SW"), K("SV")], [(T[K(k)][:, z * j:z * j + z], T.mZ[:]) for k in ("SW", "SV") for j in range(3)], 5000)
        for e, a, b in cuts:
            keys = [K("%s%d" % (k, q)) for k in ("I1", "L1") for q in range(a // 1024, (b + 1023) // 1024)]
            o = T[K("SV" if e == "v" else "SW")][:, 0:H + 1].indirect(T[K("L1")][:, a // 16:b // 16])
            if e == "v":
                op("v", keys, [K("SV")], sig * (b - a), lambda o=o, a=a, b=b: V.tensor_scalar(o, il[:, a:b], 0.0625, 0.0, A.mult, A.add))
            else:
                op("s", keys, [K("SW")], sig * (b - a), lambda o=o, a=a, b=b: S.activation(o, il[:, a:b], F.Tanh))
        at("early", l, h)
        base(1)
        op("v", [K("BS2"), "c2"], [K("CW")], 1, lambda: V.tensor_scalar(cw[:, 0:1], bs[:, 2:3], 0.0625, col["c2"], A.mult, A.add))
        op("v", [K("BS0"), K("TO0"), K("TO1")], [K("BS1")], 1, lambda: V.tensor_scalar(bs[:, 1:2], bs[:, 0:1], to[:, 0:1], to[:, 1:2], A.add, A.add))
        op("v", [K("BS0"), K("BS1")], [K("BL")], 1, lambda: V.tensor_copy(T[K("BL")][:], bs[:, 0:2]))
        for q in range(2):
            gather_mm(q, ih, [K("I0%d" % q)], "ZD", True, False)
        if both:
            op("v", [K("SW"), K("SV")], [K("CW")], H,
               lambda: V.tensor_tensor_scan(cw[:, 1:H + 1], T[K("SV")][:, 1:H + 1], T[K("SW")][:, 1:H + 1], cw[:, 0:1], A.add, A.add))
        else:
            op("v", [K("SW"), "NEG"], [K("CW")], H,
               lambda: V.tensor_tensor_scan(cw[:, 1:H + 1], T.NEG[:, 0:H], T[K("SW")][:, 1:H + 1], cw[:, 0:1], A.max, A.add))
        for q in range(2):
            c = slice(1024 * q, 1024 * q + 1024)
            op("v", [K("CW"), K("L1%d" % q), K("I1%d" % q)], [K("PR%d" % q)], gam * 1024, lambda c=c, q=q: V.tensor_tensor(
                pr[:, c], cw[:, 0:H + 1].indirect(T[K("L1")][:, 64 * q:64 * q + 64]), il[:, c], A.mult))
            gather_mm(q, pr, [K("PR%d" % q)], "Z", False, True)
            listed(q, "LP", ["LP%d_%d" % (k, h) for k in (2 * q, 2 * q + 1)], 0.0625, CEN + 0.25)
        at("heads", l, h)
        op("v", [K("CW"), K("BL"), "HR"], [K("HF")], 50, lambda: V.tensor_tensor(T[K("HF")][:], cw[:, 0:H + 1].indirect(T[K("BL")][:]), T.HR[:], A.add))
        op("v", [K("HF")], [K("HE")], 32, lambda: V.tensor_scalar(T[K("HE")][:], T[K("HF")][:], 0.25, None, A.add))
        at("lists", l, h)
        if O["carry"][l][h] == "k" and (rank or h):
            sj, sl, o = T[K("SK")], ["SL%d_%d" % (k, h) for k in range(4)], QB[:, 64:128, :]
            if l == 0:
                dmas("y", "dsj%d" % h, [], [K("SK")], [(sj[:, 16 * j:16 * j + 16], T.slot[j, H * h:H * h + H]) for j in range(8)], 4000)
                op("v", [K("SK")], [K("SX")], 128, lambda: V.tensor_copy(T[K("SX")][:], sj[:]))
                mm([K("SX"), "ID"], [bk], 128, [[(o, T[K("SX")][:], T.ID[:])]])
                op("v", [], [bk] + sl, 128, lambda: V.tensor_copy(T[K("SL")][:], o))
            else:
                mm(["ZW", "GW", "ST"] + ["Y0%d%d" % (h, k) for k in range(4)], [bk], 2176,
                   [[(o, T.GW[:], T.ST[:, 0:128])] + [(o, T.ZW[:, 15 - r:143 - r], T.Y0[:, H * h + r:H * h + H:16]) for r in range(16)]])
                op("v", [], [bk, K("SK")], 128, lambda: V.tensor_copy(sj[:], o))
                op("v", [K("SK")], [K("SK")], 128, lambda: V.tensor_scalar(sj[:], sj[:], 255, None, A.bitwise_and))
                op("v", [K("SK")], sl, 128, lambda: V.tensor_copy(T[K("SL")][:], sj[:]))

    def to_list(h, xt, keys, a0, b0, name, plus, natural):
        D, dk = T["QB%d" % h], "QB%d" % h
        outs = [(slice(64 + x, 128, 4), x) for x in range(4)] if natural else [(slice(64 + 16 * a0, 64 + 16 * b0), slice(a0, b0))]
        mm(keys + ["R0", "R1"], [dk], 256 * len(outs),
           [[(D[:, m, q], T["R%d" % q][:, 16 - 16 * y:144 - 16 * y], xt[:, x, 16 * y:16 * y + 16]) for y in range(2)] for m, x in outs for q in range(2)])
        op("v", [], [dk] + ["%s%d_%d" % (name, k, h) for k in range(a0, b0)], 32 * (b0 - a0),
           lambda: V.tensor_scalar(T["%s%d" % (name, h)][:, 32 * a0:32 * b0], D[:, 64 + 16 * a0:64 + 16 * b0, :], plus, None, A.add))

    def part(l, h, k, m):
        if l == 0 and O["pos"] == "tt":
            return T.Y0[:, 4 * h + k, :] if m == 1 else T.Y0[:, 4 * h + k:4 * h + k + m, :]
        return T["Y%d" % l][:, H * h + 512 * k:H * h + 512 * (k + m)]

    def receivers(l, r):
        return [1] if (l, r) == (1, 0) else list(range(r + 1, n))

    def engine_mask(l, r):
        m = topo.mask(T.cores[r], T.cores[r + 1])
        for t in receivers(l, r):
            m &= topo.mask(T.cores[r], T.cores[t])
        return m

    def layer(l):
        dst = T["Y%d" % l]
        tb, ld = T["TB%d" % l], T["LD%d" % l]
        wink = ["WN0%d" % h for h in range(2)]
        win = [T[k] for k in wink]
        cap = [T["CP%d%d" % (l, h)] for h in range(2)]
        capk = [["CP%d%d%d" % (l, h, q) for q in range(2)] for h in range(2)]

        def put(h):
            xf, xk = T["XF%d" % h], "XF%d" % h
            at("put", l, h)
            e, x, tables = O["put"][l][h], T["X%d" % h], O["pos"][h] == "t"
            if e == "s" and l == 1:
                for k in (0, 2):
                    dmas("g", "dxf%d%d" % (h, k), ["Y0%d%d" % (h, k), "Y0%d%d" % (h, k + 1)], [xk + str(k), xk + str(k + 1), "~xf"],
                         [(xf[:, 512 * k:512 * k + 1024], part(0, h, k, 2))], O["dl"] * 4000)
            elif e == "s":
                for a, b in ((0, 1), (1, 2), (2, 3), (3, 4)) if tables else ((0, 2), (2, 4)):
                    op("s", ["X%d" % h], [xk + str(k) for k in range(a, b)], 512 * (b - a), lambda a=a, b=b: S.activation(
                        xf[:, 512 * a:512 * b], x[:, :, 32 * a:32 * b] if tables else x[:, 512 * a:512 * b], F.Identity, scale=SC))
            (places if tables else radix)(l, h)
            if l == 0:
                fill(1, h, ["HE%d" % h])
            at("put", l, h)
            for k, m in [(a, b - a) for a, b in O["pieces"][h]]:
                o, lk = win[h][:].indirect(T["LP%d" % h][:, 32 * k:32 * k + 32 * m]), ["LP%d_%d" % (j, h) for j in range(k, k + m)]
                c = slice(512 * k, 512 * (k + m))
                if e == "s":
                    op("s", [xk + str(j) for j in range(k, k + m)] + lk, [wink[h], "~put"], sig * 512 * m, lambda o=o, c=c: S.activation(o, xf[:, c], F.Tanh))
                elif l == 0:
                    op("v", ["X%d" % h, "ST"] + lk, [wink[h]], sig * 512 * m, lambda o=o, c=c: V.tensor_tensor(o, x[:, c], T.ST[:, 0:512 * m], A.mult))
                else:
                    op("v", ["Y0%d%d" % (h, j) for j in range(k, k + m)] + lk, [wink[h]], sig * 512 * m,
                       lambda o=o, k=k: V.tensor_copy(o, T.Y0[:, H * h + 512 * k:H * h + 512 * (k + m)]))
            at("cap", l, h)
            if O["cap"][l][h] == "x":
                op("v", ["HE%d" % h, "mB"], capk[h], sig * 256, lambda: V.tensor_copy(cap[h][:].indirect(T["HE%d" % h][:, 0:16]), T.mB[:, 0:256]))
            else:
                for q in range(2):
                    c = slice(HW * q, HW * q + HW)
                    op("s", [wink[h]], [capk[h][q]], HW, lambda c=c: S.activation(cap[h][:, c], win[h][:, c], F.Identity, bias=63.5, scale=64.0))
        for h in range(2):
            if O["pos"][h] == "t":
                front(l, h)
        put(0); put(1)
        at("lists", l, 1)
        for b, k in enumerate(("D0", "QA0") * 2 if l == 0 else ()):
            grps = []
            for i in range(4):
                d, o = 4 * b + i + 1, slice(4 * i, 4 * i + 4)
                grps.append([(T[k][:, o, :], T.ID[:], T.ZR[:, 0:128]), (T[k][:, o, d:32], T.ID[:], T.ID[:, :, 0:32 - d])]
                            + [(T[k][:, o, 32 - d:32], T.ID[:], T.ID[:, :, 32 - d:32])] * (d < 16))
            mm(["ID", "ZR"], [k], 1200, grps)
            op("s", [], [k, "WS%d" % b], 512, lambda b=b, k=k: S.activation(T.WS[:, 512 * b:512 * b + 512], T[k][:], F.Identity))

        def first(h):
            ys, narrow = T["YS%d" % h], O["narrow"][l][h] == "s"
            src = T["YR%d" % h] if narrow else win[h]
            if not narrow:
                op("v", capk[h] + [wink[h]], ["YS%d" % h, "YS%db" % h], W, lambda: V.tensor_tensor_scan(ys[:], src[:], cap[h][:], -1.0, A.max, A.min))
                return
            for q in range(2):
                c = slice(HW * q, HW * q + HW)
                if narrow:
                    op("s", [wink[h]], ["YR%d" % h + "b" * q], HW, lambda c=c: S.activation(src[:, c], win[h][:, c], F.Identity))
                op("v", [capk[h][q], "YR%d" % h + "b" * q if narrow else wink[h]] + ["YS%d" % h] * q, ["YS%d" % h + "b" * q], HW / 2 if narrow else HW,
                   lambda c=c, q=q: V.tensor_tensor_scan(ys[:, c], src[:, c], cap[h][:, c], ys[:, HW - 1:HW] if q else -1.0, A.max, A.min))

        def table(h):
            i, o = T["YS%d" % h][:].indirect(T["HE%d" % h][:, 16:32]), tb[:, 256 * h:256 * h + 256]
            e = O["tab"][h]
            op(e, ["YS%d" % h, "YS%db" % h, "HE%d" % h], ["TB%d%d" % (l, h)], gam * 256,
               (lambda: V.tensor_copy(o, i)) if e == "v" else (lambda: S.activation(o, i, F.Identity)))

        def again(h, cy, cyk):
            ys = T["YS%d" % h]
            op("v", [cyk, "HE%d" % h], ["YS%d" % h, "YS%db" % h], sig * 256, lambda: V.tensor_copy(ys[:].indirect(T["HE%d" % h][:, 0:16]), cy))
            op("v", capk[h] + ["YS%d" % h, "YS%db" % h], ["YR%d" % h, "YR%db" % h], HW,
               lambda: V.tensor_tensor_scan(T["YR%d" % h][:], cap[h][:], ys[:], -1.0, A.min, A.max))

        mul, plus = ((1.0, SC), (1.0 / SC, -1.0))[l]

        def store(h):
            for b in range(4 * l):
                a = H * h + 512 * b
                dmas("y", "dout", ["Y1%d%d" % (h, b)], [], [(T.y[:, a:a + 512], dst[:, a:a + 512])], 2500)

        def back(h, src, keys, local=False):
            who, name = O["back"][l][h], "LN" if l == 1 and O["pos"][h] == "t" else "LP"
            for k in range(4):
                i = src[:].indirect(T["%s%d" % (name, h)][:, 32 * k:32 * k + 32])
                o = T["YL%d" % h][:, 512 * k:512 * k + 512] if local else part(l, h, k, 1)
                r, w = keys + ["%s%d_%d" % (name, k, h)], ["Y%s%d%d" % ("L" if local else l, h, k)]
                if who[k % len(who)] == "v":
                    op("v", r, w, gam * 512, lambda i=i, o=o: V.tensor_scalar(o, i, mul, plus, A.mult, A.add))
                else:
                    op("s", r, w, gam * 512, lambda i=i, o=o: S.activation(o, i, F.Identity, bias=plus, scale=mul))

        def by_slot(h, cy, cyk):
            ck = T["CK%d" % h]
            op("v", [cyk], ["CK%d" % h], 128, lambda: V.tensor_scalar(ck[:], cy, mul, plus, A.mult, A.add))
            for k in range(4):
                i, o = ck[:].indirect(T["SL%d" % h][:, 32 * k:32 * k + 32]), part(l, h, k, 1)
                op("v", ["CK%d" % h, "SL%d_%d" % (k, h), "YL%d%d" % (h, k)], ["Y%d%d%d" % (l, h, k)], gam * 512,
                   lambda i=i, o=o, k=k: V.tensor_tensor(o, i, T["YL%d" % h][:, 512 * k:512 * k + 512], A.max))

        def finish(h, cy, cyk):
            ys = ["YS%d" % h, "YS%db" % h]
            if cy is None:
                back(h, T["YS%d" % h], ys)
            elif O["carry"][l][h] == "k":
                back(h, T["YS%d" % h], ys, True)
                by_slot(h, cy, cyk)
            else:
                again(h, cy, cyk)
                back(h, T["YR%d" % h], ["YR%d" % h, "YR%db" % h])
            store(h)

        def merge(out, outk, a, ak, b, bk):
            if not O["mp"]:
                op("v", [ak, bk], [outk], 512, lambda: V.tensor_tensor(out, a, b, A.max))
                return
            k = ("M0", "M1", "D1", "QA1")[len(used) % 4]
            used.append(k)
            mm([bk, "ID"], [k], 256, [[(T[k][:, 8:16, :], T.ID[:], b)]])
            op("v", [ak], [k, outk], 256, lambda: V.tensor_tensor(out, T[k][:, 8:16, :], a, A.max))
        used = []

        at("first", l, 0)
        first(0); table(0)
        at("first", l, 1)
        first(1)
        if rank < n - 1:
            table(1)
        senders = [r for r in range(rank) if rank in receivers(l, r)]

        def exchange(name, land, halves, wait):
            keys = ["TB%d%d" % (l, h) for h in halves]
            passed = (l, rank) == (1, 1)

            def landed():
                cnt["arr" + name] = sum(bin(engine_mask(l, r)).count("1") for r in senders)
                return ("arr" + name, cnt["arr" + name])
            if senders and (passed or rank == n - 1):
                add("x", [], ["LD" + name], 0, 0, landed, [(k if rank < n - 1 or k[-1] == "0" else "YS1b", wait) for k in keys])
            if rank < n - 1:
                peers = [T.cores[t] for t in receivers(l, rank)]

                def send():
                    ids = [DstId(rid=topo.addr(c)[0], pnc=topo.addr(c)[1]) for c in peers]
                    srcs = [tb[:, 256 * h:256 * h + 256] for h in halves] + ([land[:, 0, :]] if passed else [])
                    g.remote_dma_fused([RemoteDMATransfer(dst_ids=ids, dma_engine_mask=engine_mask(l, rank), remote_sem=T.sem["arr" + name], srcs=srcs,
                                                          dsts=[land[:, rank, :] for c in peers], alu_op=2 if len(srcs) > 1 else 0)],
                                       local_sem=T.sem["sent" + name])
                    cnt["sent" + name] = bin(engine_mask(l, rank)).count("1")
                    return ("sent" + name, cnt["sent" + name])
                add("g", (["LD" + name] if passed else []) + keys, ["~send"], 1800 if name == "A" else 300, 2000, send)
                if senders and not passed:
                    add("x", [], ["LD" + name], 0, 0, landed, [("~send", O["E"] - 550)])

        early = l == 0 and O["early"]
        if early:
            exchange("A", T.LA, [0], O["E"] + 1500)
        exchange(str(l), ld, [1] if early else [0, 1], O["E"])
        at("carry", l + 1, 0)
        if senders:
            parts = [(T.LA[:, r, :], "LDA") for r in senders if early] + [(ld[:, r, :], "LD%d" % l) for r in senders]
            ca, cak = parts[0]
            for b, bk in parts[1:]:
                merge(T.CY0[:], "CY0", ca, cak, b, bk)
                ca, cak = T.CY0[:], "CY0"
            finish(0, ca, cak)
            at("carry", l + 1, 1)
            merge(T.CY1[:], "CY1", ca, cak, tb[:, 0:256], "TB%d0" % l)
            finish(1, T.CY1[:], "CY1")
        else:
            finish(0, None, None)
            at("carry", l + 1, 1)
            finish(1, tb[:, 0:256], "TB%d0" % l)

    for l in range(2):
        tag[0] = str(l)
        layer(l)
    live = [c["step"] < 1e9 for c in calls]
    for i in range(len(calls) - 1, -1, -1):
        for d in list(calls[i]["deps"]) + [d for d, x in calls[i]["soft"]] if live[i] else ():
            live[d] = True
    new = {i: k for k, i in enumerate(i for i in range(len(calls)) if live[i])}
    calls = [dict(c, deps=set(new[d] for d in c["deps"]), soft=[(new[d], x) for d, x in c["soft"]]) for c, x in zip(calls, live) if x]
    return calls, cnt, Q


def plan(calls):
    O, N = OPT, len(calls)
    before = [[(d, calls[d]["lag"]) for d in c["deps"]] + list(c["soft"]) for c in calls]
    users = [[] for _ in range(N)]
    for i in range(N):
        for d, x in before[i]:
            users[d].append((i, x))
    busy, tail = [c["busy"] for c in calls], [c["lag"] for c in calls]

    def lay(turn, after, head):
        start, taken = [0.0] * N, {}
        for i in turn:
            t = max([start[d] + busy[d] + x for d, x in after[i]] + [head[i]])
            gaps = taken.setdefault(calls[i]["q"], [])
            k = 0
            while k < len(gaps) and gaps[k][1] <= t:
                k += 1
            while k < len(gaps) and gaps[k][0] < t + busy[i]:
                t = max(t, gaps[k][1]); k += 1
            gaps.insert(k, (t, t + busy[i]))
            start[i] = t
        return start

    step = [c["step"] for c in calls]
    for i in range(N - 1, -1, -1):
        step[i] = min([step[i]] + [step[u] for u, x in users[i]])
    turn, best = sorted(range(N), key=lambda i: (step[i], i)), None
    for _ in range(O["rounds"]):
        start = lay(turn, before, [0.0] * N)
        end = max(start[i] + busy[i] + tail[i] for i in range(N))
        if best is None or end < best[0]:
            best = (end, start, turn)
        rank_in = {i: k for k, i in enumerate(turn)}
        late = lay(sorted(range(N), key=lambda i: (-start[i] - busy[i], -rank_in[i])), users, tail)
        turn = sorted(range(N), key=lambda i: (-late[i] - busy[i], rank_in[i]))
    rank_in = {i: k for k, i in enumerate(best[2])}
    order = sorted(range(N), key=lambda i: (best[1][i], rank_in[i]))
    late = [c["name"] == "0xLD0.0" for c in calls]
    for i in range(N):
        late[i] = late[i] or any(late[d] for d, x in before[i])
    queue, first = [c["q"] for c in calls], [i for i in order if not late[i]]
    sent = [0.0 if c["name"] == "0gTB01.0" else -O["E"] for c in calls]
    first = polish(first, 0, queue, before, [[(u, x) for u, x in b if not late[u]] for b in users], busy, sent, O["moves"])
    order = polish(first + [i for i in order if late[i]], len(first), queue, before, users, busy, tail, O["moves"])
    return {calls[i]["name"]: k for k, i in enumerate(order)}


PLANS = {}


def rank_program(g, core, T, topo):
    rank = T.rank_of(core)
    if rank is None:
        return
    like = len(T.cores) - 2
    if like not in PLANS:
        PLANS[like] = plan(collect(g, T, topo, like)[0])
    place = PLANS[like]
    calls, cnt, Q = collect(g, T, topo, rank)
    N = len(calls)
    users, left, prio = [[] for _ in range(N)], [0] * N, [0.0] * N
    for i, c in enumerate(calls):
        for d in list(c["deps"]) + [d for d, x in c["soft"]]:
            users[d].append(i); left[i] += 1
    for i in range(N - 1, -1, -1):
        prio[i] = place.get(calls[i]["name"], min([prio[u] for u in users[i]] + [1e9]) - 0.5)
    ready, order = [i for i in range(N) if left[i] == 0], []
    while ready:
        i = min(ready, key=lambda j: (prio[j], j))
        ready.remove(i); order.append(i)
        for u in users[i]:
            left[u] -= 1
            if left[u] == 0:
                ready.append(u)

    seen, token = {}, {}

    def wait(q, tok):
        s, v = tok
        if seen.get((q, s), 0) < v:
            Q[q].wait_ge(T.sem[s], v)
            seen[(q, s)] = v
    for i in order:
        c = calls[i]
        need = {}
        for d in c["deps"]:
            s, v = token[d]
            need[s] = max(need.get(s, 0), v)
        for s in sorted(need):
            wait(c["q"], (s, need[s]))
        token[i] = c["emit"]()
    for s in sorted(cnt):
        wait("g", (s, cnt[s]))
